import numpy as np
import ml_dtypes


def mxq(x, axis, fmt="e4m3"):
    dtype, down = {"e4m3": (ml_dtypes.float8_e4m3fn, 7), "e5m2": (ml_dtypes.float8_e5m2, 14)}[fmt]
    v = np.moveaxis(np.asarray(x, np.float32).astype(ml_dtypes.bfloat16).astype(np.float64), axis, -1)
    blocks = v.reshape(v.shape[:-1] + (-1, 32))
    amax = np.abs(blocks).max(-1, keepdims=True)
    byte = np.maximum(np.where(amax > 0, np.frexp(amax)[1] - 1 + 127, 0) - down, 1)
    scale = np.exp2(byte - 127.0)
    codes = (blocks / scale).astype(np.float32).astype(dtype).astype(np.float64)
    return np.moveaxis((codes * scale).reshape(v.shape), -1, axis)


WIDE = False


def mx_kscale(k):
    if not WIDE:
        return np.ones(k)
    levels = np.array([10, -10, 5, -5, 0])
    if k % 512:
        return np.exp2(np.random.permutation(np.resize(levels, k // 32))).repeat(32)
    a = np.empty((k // 512, 16))
    for p in range(k // 512):
        a[p, :8] = np.random.permutation(np.resize(levels, 8))
        for g in range(8):
            far = levels[np.abs(levels - a[p, g]) >= 10]
            a[p, g + 8] = far[np.random.randint(len(far))]
    return np.exp2(a.ravel()).repeat(32)


def f64(x):
    return np.asarray(x).astype(np.float64)


def striped(idx):
    return np.tile(idx.reshape(-1, 16).T, (8, 1)).astype(np.uint16)


def unstriped(offs):
    return offs[:16].T.reshape(-1).astype(np.int64)


def striped8(idx):
    return np.concatenate([x.reshape(-1, 16).T for x in idx]).astype(np.uint16)


def runs(offs, k):
    lists = np.stack([offs[16 * r : 16 * r + 16].T.reshape(-1) for r in range(8)]).astype(np.int64)
    return lists[np.arange(k) % 512 // 64]


def pack_weight(w):
    k, n = w.shape
    w = f64(np.asarray(w, np.float32).astype(ml_dtypes.bfloat16)).reshape(k // 32, 32, n)
    amax = np.abs(w).max(1)
    byte = np.clip(np.where(amax > 0, np.frexp(amax)[1] - 1 + 127 - 7, 1), 1, 254)
    scaled = (w * np.exp2(127.0 - byte)[:, None, :]).reshape(k, n).astype(np.float32)
    words = np.ascontiguousarray(scaled.reshape(k // 512, 128, 4, n).transpose(0, 1, 3, 2)).astype(ml_dtypes.float8_e4m3fn).view(np.uint8)
    return words, np.ascontiguousarray(byte.astype(np.uint8).reshape(k // 512, 16, n))


def unpack_weight(words, scales):
    g, p, n, _ = words.shape
    vals = np.ascontiguousarray(words).view(ml_dtypes.float8_e4m3fn).astype(np.float64) * np.repeat(np.exp2(scales.astype(np.float64) - 127.0), 8, axis=1)[..., None]
    return vals.transpose(0, 1, 3, 2).reshape(g * 512, n)


def sigmoid(v):
    return 1.0 / (1.0 + np.exp(-np.maximum(v, -700.0)))


K, T, S, N, H = 512, 2048, 512, 512, 512


def setup_inputs():
    n = np.random.standard_normal
    s = mx_kscale(K)[:, None]
    u = mx_kscale(H)
    packed_xT = pack_weight(n((K, T)) * s)
    return {
        "x_words": packed_xT[0],
        "x_scales": packed_xT[1],
        "w1": (n((K, H)) / np.sqrt(K) / s).astype(np.float32),
        "w2": (n((K, H)) / np.sqrt(K) / s).astype(np.float32),
        "g1": (np.random.uniform(0.5, 1.5, (H, 1)) * u[:, None]).astype(np.float32),
        "g2": (np.random.uniform(0.5, 1.5, (H, 1)) * u[:, None]).astype(np.float32),
        "w3": (n((H, N)) / np.sqrt(2 * H) / u[:, None]).astype(np.float32),
        "w4": (n((H, N)) / np.sqrt(2 * H) / u[:, None]).astype(np.float32),
        "offs": striped(np.random.permutation(T)[:S]),
        "west": striped8(np.stack([np.random.permutation(S) for _ in range(8)])),
        "east": striped8(np.stack([np.random.permutation(S) for _ in range(8)])),
    }


def reference(x_words, x_scales, w1, w2, g1, g2, w3, w4, offs, west, east):
    xq = unpack_weight(x_words, x_scales)[:, unstriped(offs)]
    y = sigmoid(mxq(f64(w1), 0, "e4m3").T @ xq)
    e = sigmoid(mxq(f64(w2), 0, "e4m3").T @ xq)
    re = y * ((e) ** 2)
    z = f64(g1) * (y + 0.25 * (y[np.arange(H)[:, None], runs(west, H)] + y[np.arange(H)[:, None], runs(east, H)] - (2.0 * y)) - re + 0.125 * (-1.0 * y + 1))
    z2 = f64(g2) * (e + 0.125 * (e[np.arange(H)[:, None], runs(west, H)] + e[np.arange(H)[:, None], runs(east, H)] - (2.0 * e)) + re - (0.25 * e))
    return mxq(f64(w3), 0, "e4m3").T @ mxq(z, 0, "e4m3") + mxq(f64(w4), 0, "e4m3").T @ mxq(z2, 0, "e4m3")

@@ -1,0 +1,247 @@
+from contextlib import ExitStack
+
+import concourse.mybir as mybir
+
+K, T, S, N, H = 512, 2048, 512, 512, 512
+FLOPS = 2 * (2 * K * H * S + 2 * H * N * S)
+
+F32 = mybir.dt.float32
+BF16 = mybir.dt.bfloat16
+I32 = mybir.dt.int32
+U32 = mybir.dt.uint32
+U16 = mybir.dt.uint16
+U8 = mybir.dt.uint8
+FP8X4 = mybir.dt.float8_e4m3fn_x4
+ACT = mybir.ActivationFunctionType
+ALU = mybir.AluOpType
+
+P = 128
+PACK = 4
+LIST_COLS = S // 16
+CHUNKS = ((0, 256), (256, 128), (384, 128))
+
+
+def tile_picked_grayscott_none_p_kernel(
+    tc, x_words, x_scales, w1, w2, g1, g2, w3, w4, offs, west, east, out
+):
+    nc = tc.nc
+    with ExitStack() as ctx:
+        lists = ctx.enter_context(tc.tile_pool(name="lists", bufs=1))
+        keep = ctx.enter_context(tc.tile_pool(name="keep", bufs=1))
+        psum = ctx.enter_context(tc.psum_pool(name="psum", bufs=1))
+
+        def sb(name, shape, dtype):
+            return keep.tile(shape, dtype, name=name, align_bytes=64)
+
+        offs_sb = lists.tile([P, LIST_COLS], U16, name="offs_sb")
+        west_sb = lists.tile([P, LIST_COLS], U16, name="west_sb")
+        east_sb = lists.tile([P, LIST_COLS], U16, name="east_sb")
+
+        x_scale_tab = sb("x_scale_tab", [P, T], U8)
+        nc.vector.memset(x_scale_tab[:].bitcast(I32), 0)
+        for quad in range(4):
+            nc.scalar.dma_start(
+                out=x_scale_tab[32 * quad : 32 * quad + 4, :].bitcast(I32),
+                in_=x_scales[0, 4 * quad : 4 * quad + 4, :].bitcast(I32),
+            )
+        nc.sync.dma_start(offs_sb[:], offs)
+        x_word_tab = sb("x_word_tab", [P, T], I32)
+        nc.sync.dma_start(out=x_word_tab[:], in_=x_words[0].rearrange("p n t -> p (n t)").bitcast(I32))
+        nc.sync.dma_start(west_sb[:], west)
+        nc.sync.dma_start(east_sb[:], east)
+
+        def load_weight(name, w):
+            raw = sb(name, [P, PACK, 512], F32)
+            nc.sync.dma_start(out=raw[:], in_=w.rearrange("(p j) c -> p j c", j=PACK))
+            return raw
+
+        w2_raw = load_weight("w2_raw", w2)
+        w1_raw = load_weight("w1_raw", w1)
+        g1_sb = sb("g1_sb", [P, PACK], F32)
+        nc.sync.dma_start(out=g1_sb[:], in_=g1.rearrange("(p t) o -> p (t o)", t=PACK))
+        g2_sb = sb("g2_sb", [P, PACK], F32)
+        nc.sync.dma_start(out=g2_sb[:], in_=g2.rearrange("(p t) o -> p (t o)", t=PACK))
+        w4_raw = load_weight("w4_raw", w4)
+        w3_raw = load_weight("w3_raw", w3)
+
+        warm_in = sb("warm_in", [P, 1], F32)
+        warm_out = sb("warm_out", [P, 1], F32)
+        nc.gpsimd.memset(warm_in[:], 0.0)
+        nc.scalar.activation(warm_out[:], warm_in[:], ACT.Sigmoid)
+
+        e_win = [sb("e_win%d" % t, [P, 2 * S], F32) for t in range(PACK)]
+        for t in range(PACK):
+            nc.gpsimd.memset(e_win[t][:, S:], 0.0)
+
+        def scaled(name, g, factor):
+            res = sb(name, [P, PACK], F32)
+            nc.gpsimd.tensor_scalar(res[:], g[:], factor, 0.0, ALU.mult, ALU.add)
+            return res
+
+        g1_quarter = scaled("g1_quarter", g1_sb, 0.25)
+        g1_eighth = scaled("g1_eighth", g1_sb, 0.125)
+        g2_quarter = scaled("g2_quarter", g2_sb, 0.25)
+        g2_eighth = scaled("g2_eighth", g2_sb, 0.125)
+
+        x_scale = sb("x_scale", [P, S], U8)
+        nc.vector.tensor_copy(x_scale[:], x_scale_tab[:].indirect(offs_sb[:]))
+        x_code = sb("x_code", [P, S], U32)
+        nc.vector.tensor_copy(x_code[:], x_word_tab[:].bitcast(U32).indirect(offs_sb[:]))
+
+        def quantise(name, grouped, width):
+            code = sb(name + "_code", [P, width], U32)
+            scale = sb(name + "_scale", [P, width], U8)
+            nc.vector.quantize_mx(out=code[:].bitcast(FP8X4), scales=scale[:], in_=grouped)
+            return code, scale
+
+        def round_plane_pair(name, raw, u, copy):
+            grouped = sb(name, [P, 2, P, PACK], BF16)
+            copy(
+                grouped[:].rearrange("p t m j -> p m j t"),
+                raw[:].rearrange("p j (m t) -> p m j t", t=PACK)[:, :, :, 2 * u : 2 * u + 2],
+            )
+            return grouped[:].rearrange("p t m j -> p (t m j)")
+
+        def first_product(t, tag, code, scale):
+            bank = psum.tile([P, S], F32, name="pre%d" % tag, tag="pre%d" % tag)
+            cols = slice((t % 2) * P, (t % 2 + 1) * P)
+            nc.tensor.matmul_mx(
+                out=bank[:],
+                lhsT=code[:, cols].bitcast(FP8X4),
+                lhsT_scale=scale[:, cols],
+                rhs=x_code[:].bitcast(FP8X4),
+                rhs_scale=x_scale[:],
+                start=True,
+                stop=True,
+            )
+            return bank
+
+        w2_grp = [round_plane_pair("w2_grp0", w2_raw, 0, nc.vector.tensor_copy), round_plane_pair("w2_grp1", w2_raw, 1, nc.scalar.copy)]
+        w2_q = [quantise("w2_%d" % u, w2_grp[u], 2 * P) for u in range(2)]
+        e4 = [sb("e4_%d" % t, [P, S], F32) for t in range(PACK)]
+        e_west = [sb("e_west%d" % t, [P, S], F32) for t in range(PACK)]
+        e_sum = [sb("e_sum%d" % t, [P, S], F32) for t in range(PACK)]
+        for t in range(PACK):
+            bank = first_product(t, t, *w2_q[t // 2])
+            nc.scalar.activation(e_win[t][:, :S], bank[:], ACT.Sigmoid)
+            nc.scalar.activation(e4[t][:], e_win[t][:, :S], ACT.Copy, scale=4.0)
+
+        w1_grp = [round_plane_pair("w1_grp%d" % u, w1_raw, u, nc.scalar.copy) for u in range(2)]
+
+        def e_west_gather(t):
+            nc.vector.tensor_tensor(e_west[t][:], e_win[t][:].indirect(west_sb[:]), e4[t][:], ALU.add)
+
+        def e_east_gather(t):
+            nc.vector.tensor_tensor(e_sum[t][:], e_win[t][:].indirect(east_sb[:]), e_west[t][:], ALU.add)
+
+        e_west_gather(0)
+        e_west_gather(1)
+        e_east_gather(0)
+        e_west_gather(2)
+        e_east_gather(1)
+        w1_q = [quantise("w1_0", w1_grp[0], 2 * P)]
+        e_west_gather(3)
+        w1_q.append(quantise("w1_1", w1_grp[1], 2 * P))
+        e_east_gather(2)
+        e_east_gather(3)
+
+        y = [sb("y%d" % t, [P, S], F32) for t in range(PACK)]
+        q = [sb("q%d" % t, [P, S], F32) for t in range(PACK)]
+        for t in range(PACK):
+            bank = first_product(t, t, *w1_q[t // 2])
+            nc.scalar.activation(y[t][:], bank[:], ACT.Sigmoid)
+            nc.scalar.activation(q[t][:], e_win[t][:, :S], ACT.Square, scale=2.0)
+
+        def round_rows(name, raw):
+            grouped = sb(name, [P, N, PACK], BF16)
+            nc.scalar.copy(
+                grouped[:].rearrange("p (c i) j -> p c j i", i=4),
+                raw[:].rearrange("p j (c i) -> p c j i", i=4),
+            )
+            return grouped[:].rearrange("p n j -> p (n j)")
+
+        w4_grp = round_rows("w4_grp", w4_raw)
+        w3_grp = round_rows("w3_grp", w3_raw)
+
+        y_local = [sb("y_local%d" % t, [P, S], F32) for t in range(PACK)]
+        made = [sb("made%d" % t, [P, S], F32) for t in range(PACK)]
+        z2_planes = sb("z2_planes", [P, PACK, S], BF16)
+        for t in range(PACK):
+            nc.vector.scalar_tensor_tensor(made[t][:], q[t][:], g2_quarter[:, t : t + 1], y[t][:], ALU.mult, ALU.mult)
+            nc.vector.scalar_tensor_tensor(y_local[t][:], q[t][:], 1.5, y[t][:], ALU.subtract, ALU.mult)
+            nc.vector.scalar_tensor_tensor(z2_planes[:, t, :], e_sum[t][:], g2_eighth[:, t : t + 1], made[t][:], ALU.mult, ALU.add)
+
+        def weave(name, planes, width):
+            grouped = sb(name, [P, width, PACK], BF16)
+            nc.scalar.copy(
+                grouped[:].rearrange("p (c i) t -> p c t i", i=4),
+                planes[:].rearrange("p t (c i) -> p c t i", i=4),
+            )
+            return grouped[:].rearrange("p c t -> p (c t)")
+
+        z2_grp = weave("z2_grp", z2_planes, S)
+
+        out_rows = out.rearrange("(mo p) c -> p mo c", p=P)
+        late = {}
+        z_grp = []
+
+        def diffuse_y(n):
+            c0, width = CHUNKS[n]
+            cells = slice(c0, c0 + width)
+            entries = slice(c0 // 16, (c0 + width) // 16)
+            y_west = [sb("y_west%d_%d" % (n, t), [P, width], F32) for t in range(PACK)]
+            y_sum = [sb("y_sum%d_%d" % (n, t), [P, width], F32) for t in range(PACK)]
+            z_planes = sb("z_planes%d" % n, [P, PACK, width], BF16)
+            for t in range(PACK):
+                nc.vector.tensor_tensor(y_west[t][:], y[t][:].indirect(west_sb[:, entries]), y_local[t][:, cells], ALU.subtract)
+            for t in range(PACK):
+                nc.vector.tensor_tensor(y_sum[t][:], y[t][:].indirect(east_sb[:, entries]), y_west[t][:], ALU.add)
+                nc.scalar.activation(
+                    z_planes[:, t, :], y_sum[t][:], ACT.Identity, bias=g1_eighth[:, t : t + 1], scale=g1_quarter[:, t : t + 1]
+                )
+            z_grp.append(weave("z_grp%d" % n, z_planes, width))
+
+        def second_product(n):
+            c0, width = CHUNKS[n]
+            cells = slice(c0, c0 + width)
+            z_code, z_scale = quantise("z_chunk%d" % n, z_grp[n], width)
+            w3_code, w3_scale = late["w3"]
+            w4_code, w4_scale = late["w4"]
+            z2_code, z2_scale = late["z2"]
+            per_bank = 512 // width
+            result = sb("result%d" % n, [P, PACK, width], F32)
+            for b in range(PACK // per_bank):
+                bank = psum.tile([P, per_bank, width], F32, name="acc%d_%d" % (n, b))
+                for r in range(per_bank):
+                    mo = b * per_bank + r
+                    cols = slice(mo * P, (mo + 1) * P)
+                    nc.tensor.matmul_mx(
+                        out=bank[:, r, :],
+                        lhsT=w4_code[:, cols].bitcast(FP8X4),
+                        lhsT_scale=w4_scale[:, cols],
+                        rhs=z2_code[:, cells].bitcast(FP8X4),
+                        rhs_scale=z2_scale[:, cells],
+                        start=True,
+                        stop=False,
+                    )
+                    nc.tensor.matmul_mx(
+                        out=bank[:, r, :],
+                        lhsT=w3_code[:, cols].bitcast(FP8X4),
+                        lhsT_scale=w3_scale[:, cols],
+                        rhs=z_code[:].bitcast(FP8X4),
+                        rhs_scale=z_scale[:],
+                        start=False,
+                        stop=True,
+                    )
+                nc.scalar.copy(result[:, b * per_bank : (b + 1) * per_bank, :], bank[:])
+            nc.sync.dma_start(out=out_rows[:, :, cells], in_=result[:])
+
+        diffuse_y(0)
+        late["w4"] = quantise("w4", w4_grp, N)
+        late["w3"] = quantise("w3", w3_grp, N)
+        late["z2"] = quantise("z2", z2_grp, S)
+        diffuse_y(1)
+        second_product(0)
+        diffuse_y(2)
+        second_product(1)
+        second_product(2)

@@ -30,8 +30,8 @@ def tile_picked_grayscott_none_p_kernel(
         keep = ctx.enter_context(tc.tile_pool(name="keep", bufs=1))
         psum = ctx.enter_context(tc.psum_pool(name="psum", bufs=1))
 
-        def sb(name, shape, dtype):
-            return keep.tile(shape, dtype, name=name, align_bytes=64)
+        def sb(name, shape, dtype, tag=None):
+            return keep.tile(shape, dtype, name=name, tag=tag or name, align_bytes=64)
 
         offs_sb = lists.tile([P, LIST_COLS], U16, name="offs_sb")
         west_sb = lists.tile([P, LIST_COLS], U16, name="west_sb")
@@ -44,30 +44,30 @@ def tile_picked_grayscott_none_p_kernel(
                 out=x_scale_tab[32 * quad : 32 * quad + 4, :].bitcast(I32),
                 in_=x_scales[0, 4 * quad : 4 * quad + 4, :].bitcast(I32),
             )
-        nc.sync.dma_start(offs_sb[:], offs)
-        x_word_tab = sb("x_word_tab", [P, T], I32)
-        nc.sync.dma_start(out=x_word_tab[:], in_=x_words[0].rearrange("p n t -> p (n t)").bitcast(I32))
-        nc.sync.dma_start(west_sb[:], west)
-        nc.sync.dma_start(east_sb[:], east)
+
+        warm_in = sb("warm_in", [P, 1], F32)
+        warm_out = sb("warm_out", [P, 1], F32)
+        nc.gpsimd.memset(warm_in[:], 0.0)
+        nc.scalar.activation(warm_out[:], warm_in[:], ACT.Sigmoid)
 
         def load_weight(name, w):
             raw = sb(name, [P, PACK, 512], F32)
             nc.sync.dma_start(out=raw[:], in_=w.rearrange("(p j) c -> p j c", j=PACK))
             return raw
 
+        nc.sync.dma_start(offs_sb[:], offs)
         w2_raw = load_weight("w2_raw", w2)
+        nc.sync.dma_start(west_sb[:], west)
+        nc.sync.dma_start(east_sb[:], east)
+        x_word_tab = sb("x_word_tab", [P, T], I32)
+        nc.sync.dma_start(out=x_word_tab[:], in_=x_words[0].rearrange("p n t -> p (n t)").bitcast(I32))
         w1_raw = load_weight("w1_raw", w1)
         g1_sb = sb("g1_sb", [P, PACK], F32)
-        nc.sync.dma_start(out=g1_sb[:], in_=g1.rearrange("(p t) o -> p (t o)", t=PACK))
+        nc.gpsimd.dma_start(out=g1_sb[:], in_=g1.rearrange("(p t) o -> p (t o)", t=PACK))
         g2_sb = sb("g2_sb", [P, PACK], F32)
-        nc.sync.dma_start(out=g2_sb[:], in_=g2.rearrange("(p t) o -> p (t o)", t=PACK))
+        nc.gpsimd.dma_start(out=g2_sb[:], in_=g2.rearrange("(p t) o -> p (t o)", t=PACK))
         w4_raw = load_weight("w4_raw", w4)
         w3_raw = load_weight("w3_raw", w3)
-
-        warm_in = sb("warm_in", [P, 1], F32)
-        warm_out = sb("warm_out", [P, 1], F32)
-        nc.gpsimd.memset(warm_in[:], 0.0)
-        nc.scalar.activation(warm_out[:], warm_in[:], ACT.Sigmoid)
 
         e_win = [sb("e_win%d" % t, [P, 2 * S], F32) for t in range(PACK)]
         for t in range(PACK):
@@ -85,8 +85,6 @@ def tile_picked_grayscott_none_p_kernel(
 
         x_scale = sb("x_scale", [P, S], U8)
         nc.vector.tensor_copy(x_scale[:], x_scale_tab[:].indirect(offs_sb[:]))
-        x_code = sb("x_code", [P, S], U32)
-        nc.vector.tensor_copy(x_code[:], x_word_tab[:].bitcast(U32).indirect(offs_sb[:]))
 
         def quantise(name, grouped, width):
             code = sb(name + "_code", [P, width], U32)
@@ -94,63 +92,76 @@ def tile_picked_grayscott_none_p_kernel(
             nc.vector.quantize_mx(out=code[:].bitcast(FP8X4), scales=scale[:], in_=grouped)
             return code, scale
 
-        def round_plane_pair(name, raw, u, copy):
+        def round_plane_pair(name, raw, u, *copies):
             grouped = sb(name, [P, 2, P, PACK], BF16)
-            copy(
-                grouped[:].rearrange("p t m j -> p m j t"),
-                raw[:].rearrange("p j (m t) -> p m j t", t=PACK)[:, :, :, 2 * u : 2 * u + 2],
-            )
+            share = P // len(copies)
+            for n, copy in enumerate(copies):
+                rows = slice(n * share, (n + 1) * share)
+                copy(
+                    grouped[:].rearrange("p t m j -> p m t j")[:, rows],
+                    raw[:].rearrange("p j (m t) -> p m t j", t=PACK)[:, rows, 2 * u : 2 * u + 2, :],
+                )
             return grouped[:].rearrange("p t m j -> p (t m j)")
 
-        def first_product(t, tag, code, scale):
-            bank = psum.tile([P, S], F32, name="pre%d" % tag, tag="pre%d" % tag)
+        def first_product(t, tag, code, scale, cells=slice(0, S)):
+            bank = psum.tile([P, cells.stop - cells.start], F32, name="pre%d" % tag, tag="pre%d" % tag)
             cols = slice((t % 2) * P, (t % 2 + 1) * P)
             nc.tensor.matmul_mx(
                 out=bank[:],
                 lhsT=code[:, cols].bitcast(FP8X4),
                 lhsT_scale=scale[:, cols],
-                rhs=x_code[:].bitcast(FP8X4),
-                rhs_scale=x_scale[:],
+                rhs=x_code[:, cells].bitcast(FP8X4),
+                rhs_scale=x_scale[:, cells],
                 start=True,
                 stop=True,
             )
             return bank
 
-        w2_grp = [round_plane_pair("w2_grp0", w2_raw, 0, nc.vector.tensor_copy), round_plane_pair("w2_grp1", w2_raw, 1, nc.scalar.copy)]
-        w2_q = [quantise("w2_%d" % u, w2_grp[u], 2 * P) for u in range(2)]
-        e4 = [sb("e4_%d" % t, [P, S], F32) for t in range(PACK)]
-        e_west = [sb("e_west%d" % t, [P, S], F32) for t in range(PACK)]
-        e_sum = [sb("e_sum%d" % t, [P, S], F32) for t in range(PACK)]
-        for t in range(PACK):
-            bank = first_product(t, t, *w2_q[t // 2])
-            nc.scalar.activation(e_win[t][:, :S], bank[:], ACT.Sigmoid)
-            nc.scalar.activation(e4[t][:], e_win[t][:, :S], ACT.Copy, scale=4.0)
+        w2_q = [quantise("w2_%d" % u, round_plane_pair("w2_grp%d" % u, w2_raw, u, nc.scalar.copy), 2 * P) for u in range(2)]
+        x_code = sb("x_code", [P, S], U32)
+        halves = (slice(0, S // 2), slice(S // 2, S))
 
+        def entries(cells):
+            return slice(cells.start // 16, cells.stop // 16)
+
+        for half in halves:
+            nc.vector.tensor_copy(x_code[:, half], x_word_tab[:].bitcast(U32).indirect(offs_sb[:, entries(half)]))
+        e4 = sb("e4", [P, S], F32)
+        for tag, half in zip((4, 0), halves):
+            bank = first_product(0, tag, *w2_q[0], cells=half)
+            nc.scalar.activation(e_win[0][:, half], bank[:], ACT.Sigmoid)
+            nc.scalar.activation(e4[:, half], e_win[0][:, half], ACT.Copy, scale=4.0)
         w1_grp = [round_plane_pair("w1_grp%d" % u, w1_raw, u, nc.scalar.copy) for u in range(2)]
 
-        def e_west_gather(t):
-            nc.vector.tensor_tensor(e_west[t][:], e_win[t][:].indirect(west_sb[:]), e4[t][:], ALU.add)
+        def e_gather(name, t, offsets, addend, tag=None):
+            res = sb(name, [P, S], F32, tag=tag)
+            nc.vector.tensor_tensor(res[:], e_win[t][:].indirect(offsets[:]), addend[:], ALU.add)
+            return res
 
-        def e_east_gather(t):
-            nc.vector.tensor_tensor(e_sum[t][:], e_win[t][:].indirect(east_sb[:]), e_west[t][:], ALU.add)
-
-        e_west_gather(0)
-        e_west_gather(1)
-        e_east_gather(0)
-        e_west_gather(2)
-        e_east_gather(1)
+        e_west0 = sb("e_west0", [P, S], F32)
+        for half in halves:
+            nc.vector.tensor_tensor(e_west0[:, half], e_win[0][:].indirect(west_sb[:, entries(half)]), e4[:, half], ALU.add)
         w1_q = [quantise("w1_0", w1_grp[0], 2 * P)]
-        e_west_gather(3)
+        e_sum = [e_gather("e_sum0", 0, east_sb, e_west0, tag="w1_grp0")]
         w1_q.append(quantise("w1_1", w1_grp[1], 2 * P))
-        e_east_gather(2)
-        e_east_gather(3)
 
         y = [sb("y%d" % t, [P, S], F32) for t in range(PACK)]
         q = [sb("q%d" % t, [P, S], F32) for t in range(PACK)]
+        e_pre = {}
         for t in range(PACK):
-            bank = first_product(t, t, *w1_q[t // 2])
+            if t >= 1:
+                bank = first_product(t, 1 + t, *w2_q[t // 2])
+                e_pre[t] = sb("e_pre%d" % t, [P, S], F32)
+                nc.scalar.activation(e_win[t][:, :S], bank[:], ACT.Sigmoid)
+                nc.scalar.copy(e_pre[t][:], bank[:])
+            bank = first_product(t, t % 2, *w1_q[t // 2])
             nc.scalar.activation(y[t][:], bank[:], ACT.Sigmoid)
             nc.scalar.activation(q[t][:], e_win[t][:, :S], ACT.Square, scale=2.0)
+        e_east = {}
+        for t in (1, 2, 3):
+            e_east[t] = sb("e_east%d" % t, [P, S], F32)
+            for half in halves:
+                nc.scalar.activation(e_east[t][:, half], e_pre[t][:].indirect(east_sb[:, entries(half)]), ACT.Sigmoid)
 
         def round_rows(name, raw):
             grouped = sb(name, [P, N, PACK], BF16)
@@ -166,10 +177,15 @@ def tile_picked_grayscott_none_p_kernel(
         y_local = [sb("y_local%d" % t, [P, S], F32) for t in range(PACK)]
         made = [sb("made%d" % t, [P, S], F32) for t in range(PACK)]
         z2_planes = sb("z2_planes", [P, PACK, S], BF16)
+
+        def finish_z2(t):
+            nc.vector.scalar_tensor_tensor(z2_planes[:, t, :], e_sum[t][:], g2_eighth[:, t : t + 1], made[t][:], ALU.mult, ALU.add)
+
         for t in range(PACK):
             nc.vector.scalar_tensor_tensor(made[t][:], q[t][:], g2_quarter[:, t : t + 1], y[t][:], ALU.mult, ALU.mult)
             nc.vector.scalar_tensor_tensor(y_local[t][:], q[t][:], 1.5, y[t][:], ALU.subtract, ALU.mult)
-            nc.vector.scalar_tensor_tensor(z2_planes[:, t, :], e_sum[t][:], g2_eighth[:, t : t + 1], made[t][:], ALU.mult, ALU.add)
+            if t < 1:
+                finish_z2(t)
 
         def weave(name, planes, width):
             grouped = sb(name, [P, width, PACK], BF16)
@@ -179,69 +195,97 @@ def tile_picked_grayscott_none_p_kernel(
             )
             return grouped[:].rearrange("p c t -> p (c t)")
 
-        z2_grp = weave("z2_grp", z2_planes, S)
 
         out_rows = out.rearrange("(mo p) c -> p mo c", p=P)
         late = {}
         z_grp = []
 
-        def diffuse_y(n):
+        y_west = {}
+        z_q = {}
+
+        def west_y(n, tag=None):
             c0, width = CHUNKS[n]
             cells = slice(c0, c0 + width)
-            entries = slice(c0 // 16, (c0 + width) // 16)
-            y_west = [sb("y_west%d_%d" % (n, t), [P, width], F32) for t in range(PACK)]
-            y_sum = [sb("y_sum%d_%d" % (n, t), [P, width], F32) for t in range(PACK)]
+            y_west[n] = sb("y_west%d" % n, [P, PACK, width], F32, tag=tag)
+            for t in range(PACK):
+                nc.vector.tensor_tensor(
+                    y_west[n][:, t, :], y[t][:].indirect(west_sb[:, entries(cells)]), y_local[t][:, cells], ALU.subtract
+                )
+
+        def east_y(n, tag=None):
+            c0, width = CHUNKS[n]
+            cells = slice(c0, c0 + width)
+            y_sum = sb("y_sum%d" % n, [P, PACK, width], F32, tag=tag)
             z_planes = sb("z_planes%d" % n, [P, PACK, width], BF16)
             for t in range(PACK):
-                nc.vector.tensor_tensor(y_west[t][:], y[t][:].indirect(west_sb[:, entries]), y_local[t][:, cells], ALU.subtract)
-            for t in range(PACK):
-                nc.vector.tensor_tensor(y_sum[t][:], y[t][:].indirect(east_sb[:, entries]), y_west[t][:], ALU.add)
+                nc.vector.tensor_tensor(y_sum[:, t, :], y[t][:].indirect(east_sb[:, entries(cells)]), y_west[n][:, t, :], ALU.add)
                 nc.scalar.activation(
-                    z_planes[:, t, :], y_sum[t][:], ACT.Identity, bias=g1_eighth[:, t : t + 1], scale=g1_quarter[:, t : t + 1]
+                    z_planes[:, t, :], y_sum[:, t, :], ACT.Identity, bias=g1_eighth[:, t : t + 1], scale=g1_quarter[:, t : t + 1]
                 )
             z_grp.append(weave("z_grp%d" % n, z_planes, width))
+
+        def quantise_z(n):
+            z_q[n] = quantise("z_chunk%d" % n, z_grp[n], CHUNKS[n][1])
+
+        def out_pass(acc, mo, w_q, z_q, cells, first):
+            cols = slice(mo * P, (mo + 1) * P)
+            nc.tensor.matmul_mx(
+                out=acc,
+                lhsT=w_q[0][:, cols].bitcast(FP8X4),
+                lhsT_scale=w_q[1][:, cols],
+                rhs=z_q[0][:, cells].bitcast(FP8X4),
+                rhs_scale=z_q[1][:, cells],
+                start=first,
+                stop=not first,
+            )
 
         def second_product(n):
             c0, width = CHUNKS[n]
             cells = slice(c0, c0 + width)
-            z_code, z_scale = quantise("z_chunk%d" % n, z_grp[n], width)
-            w3_code, w3_scale = late["w3"]
-            w4_code, w4_scale = late["w4"]
-            z2_code, z2_scale = late["z2"]
             per_bank = 512 // width
             result = sb("result%d" % n, [P, PACK, width], F32)
             for b in range(PACK // per_bank):
                 bank = psum.tile([P, per_bank, width], F32, name="acc%d_%d" % (n, b))
                 for r in range(per_bank):
-                    mo = b * per_bank + r
-                    cols = slice(mo * P, (mo + 1) * P)
-                    nc.tensor.matmul_mx(
-                        out=bank[:, r, :],
-                        lhsT=w4_code[:, cols].bitcast(FP8X4),
-                        lhsT_scale=w4_scale[:, cols],
-                        rhs=z2_code[:, cells].bitcast(FP8X4),
-                        rhs_scale=z2_scale[:, cells],
-                        start=True,
-                        stop=False,
-                    )
-                    nc.tensor.matmul_mx(
-                        out=bank[:, r, :],
-                        lhsT=w3_code[:, cols].bitcast(FP8X4),
-                        lhsT_scale=w3_scale[:, cols],
-                        rhs=z_code[:].bitcast(FP8X4),
-                        rhs_scale=z_scale[:],
-                        start=False,
-                        stop=True,
-                    )
+                    out_pass(bank[:, r, :], b * per_bank + r, late["w4"], late["z2"], cells, True)
+                    out_pass(bank[:, r, :], b * per_bank + r, late["w3"], z_q[n], slice(0, width), False)
                 nc.scalar.copy(result[:, b * per_bank : (b + 1) * per_bank, :], bank[:])
             nc.sync.dma_start(out=out_rows[:, :, cells], in_=result[:])
 
-        diffuse_y(0)
+        def last_product(n):
+            c0, width = CHUNKS[n]
+            cells = slice(c0, c0 + width)
+            banks = [psum.tile([P, width], F32, name="last%d" % mo, tag="pre%d" % mo) for mo in range(PACK)]
+            for mo in range(PACK):
+                out_pass(banks[mo][:], mo, late["w4"], late["z2"], cells, True)
+            quantise_z(n)
+            result = sb("result%d" % n, [P, PACK, width], F32)
+            for mo in range(PACK):
+                out_pass(banks[mo][:], mo, late["w3"], z_q[n], slice(0, width), False)
+                copy = (nc.scalar.copy, nc.vector.tensor_copy)[mo % 2]
+                copy(result[:, mo, :], banks[mo][:])
+            nc.sync.dma_start(out=out_rows[:, :, cells], in_=result[:])
+
+        west_y(0)
+        east_y(0)
+        e_mix = {}
+        for t in (1, 2, 3):
+            e_mix[t] = sb("e_mix%d" % t, [P, S], F32)
+            nc.vector.scalar_tensor_tensor(e_mix[t][:], e_win[t][:, :S], 4.0, e_east[t][:], ALU.mult, ALU.add)
+        for t in (1, 2, 3):
+            e_sum.append(e_gather("e_sum%d" % t, t, west_sb, e_mix[t]))
+        for t in (1, 2, 3):
+            finish_z2(t)
+        z2_grp = weave("z2_grp", z2_planes, S)
         late["w4"] = quantise("w4", w4_grp, N)
         late["w3"] = quantise("w3", w3_grp, N)
         late["z2"] = quantise("z2", z2_grp, S)
-        diffuse_y(1)
+        quantise_z(0)
+        west_y(1, tag="e_sum3")
+        east_y(1)
         second_product(0)
-        diffuse_y(2)
+        west_y(2, tag="z2_grp")
+        quantise_z(1)
+        east_y(2, tag="z_grp1")
         second_product(1)
-        second_product(2)
+        last_product(2)

@@ -1,6 +1,7 @@
 from contextlib import ExitStack
 
 import concourse.mybir as mybir
+from concourse.masks import make_identity
 
 K, T, S, N, H = 512, 2048, 512, 512, 512
 FLOPS = 2 * (2 * K * H * S + 2 * H * N * S)
@@ -64,14 +65,19 @@ def tile_picked_grayscott_none_p_kernel(
         w1_raw = load_weight("w1_raw", w1)
         g1_sb = sb("g1_sb", [P, PACK], F32)
         nc.gpsimd.dma_start(out=g1_sb[:], in_=g1.rearrange("(p t) o -> p (t o)", t=PACK))
-        g2_sb = sb("g2_sb", [P, PACK], F32)
-        nc.gpsimd.dma_start(out=g2_sb[:], in_=g2.rearrange("(p t) o -> p (t o)", t=PACK))
         w4_raw = load_weight("w4_raw", w4)
         w3_raw = load_weight("w3_raw", w3)
+        g2_row = sb("g2_row", [P, H], F32)
+        nc.sync.dma_start(out=g2_row[:], in_=g2.rearrange("h o -> (h o)").partition_broadcast(P))
 
-        e_win = [sb("e_win%d" % t, [P, 2 * S], F32) for t in range(PACK)]
-        for t in range(PACK):
-            nc.gpsimd.memset(e_win[t][:, S:], 0.0)
+        ident = sb("ident", [P, P], F32)
+        make_identity(nc, ident[:])
+
+        e_window = [sb("e_window%d" % t, [P, 2 * S], F32) for t in range(PACK)]
+        e = [e_window[0][:, :S]] + [sb("e%d" % t, [P, S], F32)[:] for t in range(1, PACK)]
+
+        def bank_tile(name, shape, tag):
+            return psum.tile(shape, F32, name=name, tag="bank%d" % tag)
 
         def scaled(name, g, factor):
             res = sb(name, [P, PACK], F32)
@@ -80,8 +86,8 @@ def tile_picked_grayscott_none_p_kernel(
 
         g1_quarter = scaled("g1_quarter", g1_sb, 0.25)
         g1_eighth = scaled("g1_eighth", g1_sb, 0.125)
-        g2_quarter = scaled("g2_quarter", g2_sb, 0.25)
-        g2_eighth = scaled("g2_eighth", g2_sb, 0.125)
+        for t in range(PACK):
+            nc.gpsimd.memset(e_window[t][:, S:], 0.0)
 
         x_scale = sb("x_scale", [P, S], U8)
         nc.vector.tensor_copy(x_scale[:], x_scale_tab[:].indirect(offs_sb[:]))
@@ -104,7 +110,7 @@ def tile_picked_grayscott_none_p_kernel(
             return grouped[:].rearrange("p t m j -> p (t m j)")
 
         def first_product(t, tag, code, scale, cells=slice(0, S)):
-            bank = psum.tile([P, cells.stop - cells.start], F32, name="pre%d" % tag, tag="pre%d" % tag)
+            bank = bank_tile("pre", [P, cells.stop - cells.start], tag)
             cols = slice((t % 2) * P, (t % 2 + 1) * P)
             nc.tensor.matmul_mx(
                 out=bank[:],
@@ -126,66 +132,91 @@ def tile_picked_grayscott_none_p_kernel(
 
         for half in halves:
             nc.vector.tensor_copy(x_code[:, half], x_word_tab[:].bitcast(U32).indirect(offs_sb[:, entries(half)]))
-        e4 = sb("e4", [P, S], F32)
-        for tag, half in zip((4, 0), halves):
+        e4 = [sb("e4_%d" % t, [P, S], F32) for t in range(PACK)]
+        for tag, half in zip((1, 2), halves):
             bank = first_product(0, tag, *w2_q[0], cells=half)
-            nc.scalar.activation(e_win[0][:, half], bank[:], ACT.Sigmoid)
-            nc.scalar.activation(e4[:, half], e_win[0][:, half], ACT.Copy, scale=4.0)
-        w1_grp = [round_plane_pair("w1_grp%d" % u, w1_raw, u, nc.scalar.copy) for u in range(2)]
-
-        def e_gather(name, t, offsets, addend, tag=None):
-            res = sb(name, [P, S], F32, tag=tag)
-            nc.vector.tensor_tensor(res[:], e_win[t][:].indirect(offsets[:]), addend[:], ALU.add)
-            return res
-
+            nc.scalar.activation(e[0][:, half], bank[:], ACT.Sigmoid)
+            nc.scalar.activation(e4[0][:, half], e[0][:, half], ACT.Copy, scale=4.0)
+        w1_q = [quantise("w1_0", round_plane_pair("w1_grp0", w1_raw, 0, nc.vector.tensor_copy), 2 * P)]
         e_west0 = sb("e_west0", [P, S], F32)
         for half in halves:
-            nc.vector.tensor_tensor(e_west0[:, half], e_win[0][:].indirect(west_sb[:, entries(half)]), e4[:, half], ALU.add)
-        w1_q = [quantise("w1_0", w1_grp[0], 2 * P)]
-        e_sum = [e_gather("e_sum0", 0, east_sb, e_west0, tag="w1_grp0")]
-        w1_q.append(quantise("w1_1", w1_grp[1], 2 * P))
+            nc.vector.tensor_tensor(e_west0[:, half], e_window[0][:].indirect(west_sb[:, entries(half)]), e4[0][:, half], ALU.add)
+        w1_grp1 = round_plane_pair("w1_grp1", w1_raw, 1, nc.vector.tensor_copy)
+        e_sum0 = sb("e_sum0", [P, S], F32, tag="w1_grp0")
+        nc.vector.tensor_tensor(e_sum0[:], e_window[0][:].indirect(east_sb[:]), e_west0[:], ALU.add)
+        w1_q.append(quantise("w1_1", w1_grp1, 2 * P))
 
         y = [sb("y%d" % t, [P, S], F32) for t in range(PACK)]
         q = [sb("q%d" % t, [P, S], F32) for t in range(PACK)]
-        e_pre = {}
+        e_bank = (None, 3, 2, 0)
+        y_bank = (0, 1, 3, 1)
         for t in range(PACK):
             if t >= 1:
-                bank = first_product(t, 1 + t, *w2_q[t // 2])
-                e_pre[t] = sb("e_pre%d" % t, [P, S], F32)
-                nc.scalar.activation(e_win[t][:, :S], bank[:], ACT.Sigmoid)
-                nc.scalar.copy(e_pre[t][:], bank[:])
-            bank = first_product(t, t % 2, *w1_q[t // 2])
+                bank = first_product(t, e_bank[t], *w2_q[t // 2])
+                nc.scalar.activation(e[t], bank[:], ACT.Sigmoid)
+                nc.scalar.copy(e_window[t][:, :S], bank[:])
+            bank = first_product(t, y_bank[t], *w1_q[t // 2])
             nc.scalar.activation(y[t][:], bank[:], ACT.Sigmoid)
-            nc.scalar.activation(q[t][:], e_win[t][:, :S], ACT.Square, scale=2.0)
-        e_east = {}
-        for t in (1, 2, 3):
+            nc.scalar.activation(q[t][:], e[t], ACT.Square, scale=2.0)
+        e_east, e_west = {}, {}
+        for t in range(1, PACK):
             e_east[t] = sb("e_east%d" % t, [P, S], F32)
-            for half in halves:
-                nc.scalar.activation(e_east[t][:, half], e_pre[t][:].indirect(east_sb[:, entries(half)]), ACT.Sigmoid)
+            e_west[t] = sb("e_west%d" % t, [P, S], F32)
+            nc.scalar.activation(e4[t][:], e[t], ACT.Copy, scale=4.0)
+            nc.scalar.activation(e_east[t][:], e_window[t][:].indirect(east_sb[:]), ACT.Sigmoid)
+            nc.scalar.activation(e_west[t][:], e_window[t][:].indirect(west_sb[:]), ACT.Sigmoid)
 
-        def round_rows(name, raw):
+        def round_rows(name, raw, copy):
             grouped = sb(name, [P, N, PACK], BF16)
-            nc.scalar.copy(
+            copy(
                 grouped[:].rearrange("p (c i) j -> p c j i", i=4),
                 raw[:].rearrange("p j (c i) -> p c j i", i=4),
             )
             return grouped[:].rearrange("p n j -> p (n j)")
 
-        w4_grp = round_rows("w4_grp", w4_raw)
-        w3_grp = round_rows("w3_grp", w3_raw)
-
         y_local = [sb("y_local%d" % t, [P, S], F32) for t in range(PACK)]
         made = [sb("made%d" % t, [P, S], F32) for t in range(PACK)]
-        z2_planes = sb("z2_planes", [P, PACK, S], BF16)
-
-        def finish_z2(t):
-            nc.vector.scalar_tensor_tensor(z2_planes[:, t, :], e_sum[t][:], g2_eighth[:, t : t + 1], made[t][:], ALU.mult, ALU.add)
-
         for t in range(PACK):
-            nc.vector.scalar_tensor_tensor(made[t][:], q[t][:], g2_quarter[:, t : t + 1], y[t][:], ALU.mult, ALU.mult)
             nc.vector.scalar_tensor_tensor(y_local[t][:], q[t][:], 1.5, y[t][:], ALU.subtract, ALU.mult)
-            if t < 1:
-                finish_z2(t)
+            nc.vector.scalar_tensor_tensor(made[t][:], q[t][:], 2.0, y[t][:], ALU.mult, ALU.mult)
+
+        z2_sum = [bank_tile("z2_sum%d" % cb, [P, PACK, P], 4 + cb) for cb in range(4)]
+        for t in (1, 0, 2, 3):
+            terms = (e_sum0, made[0]) if t == 0 else (e4[t], e_east[t], made[t], e_west[t])
+            for n, term in enumerate(terms):
+                for cb in range(4):
+                    nc.tensor.matmul(
+                        z2_sum[cb][:, t, :],
+                        lhsT=term[:, cb * P : (cb + 1) * P],
+                        rhs=ident[:],
+                        is_transpose=True,
+                        start=n == 0,
+                        stop=n == len(terms) - 1,
+                    )
+
+        z2_words = sb("z2_words", [P, S, 2], F32)
+
+        def finish_z2():
+            for pair in range(2):
+                back = bank_tile("back%d" % pair, [P, 2, 2, P], 2 + pair)
+                for r in range(2):
+                    cb = 2 * pair + r
+                    z2_t = sb("z2_t%d" % cb, [P, H], BF16)
+                    nc.vector.scalar_tensor_tensor(
+                        z2_t[:].rearrange("c (p t) -> c p t", t=PACK),
+                        z2_sum[cb][:].rearrange("c t p -> c p t"),
+                        0.125,
+                        g2_row[:].rearrange("c (p t) -> c p t", t=PACK),
+                        ALU.mult,
+                        ALU.mult,
+                    )
+                    words = z2_t[:].bitcast(F32)
+                    for u in range(2):
+                        nc.tensor.transpose(back[:, r, u, :], words[:, u : 2 * P : 2], ident[:])
+                nc.scalar.copy(
+                    z2_words[:, pair * 2 * P : (pair + 1) * 2 * P, :].rearrange("p (r c) u -> p r c u", r=2),
+                    back[:].rearrange("p r u c -> p r c u"),
+                )
 
         def weave(name, planes, width):
             grouped = sb(name, [P, width, PACK], BF16)
@@ -212,15 +243,16 @@ def tile_picked_grayscott_none_p_kernel(
                     y_west[n][:, t, :], y[t][:].indirect(west_sb[:, entries(cells)]), y_local[t][:, cells], ALU.subtract
                 )
 
-        def east_y(n, tag=None):
+        def east_y(n, tags=(None, None), planes_tag=None):
             c0, width = CHUNKS[n]
             cells = slice(c0, c0 + width)
-            y_sum = sb("y_sum%d" % n, [P, PACK, width], F32, tag=tag)
-            z_planes = sb("z_planes%d" % n, [P, PACK, width], BF16)
+            sums = [sb("y_sum%d_%d" % (n, u), [P, 2, width], F32, tag=tags[u]) for u in range(2)]
+            z_planes = sb("z_planes%d" % n, [P, PACK, width], BF16, tag=planes_tag)
             for t in range(PACK):
-                nc.vector.tensor_tensor(y_sum[:, t, :], y[t][:].indirect(east_sb[:, entries(cells)]), y_west[n][:, t, :], ALU.add)
+                y_sum = sums[t // 2][:, t % 2, :]
+                nc.vector.tensor_tensor(y_sum, y[t][:].indirect(east_sb[:, entries(cells)]), y_west[n][:, t, :], ALU.add)
                 nc.scalar.activation(
-                    z_planes[:, t, :], y_sum[:, t, :], ACT.Identity, bias=g1_eighth[:, t : t + 1], scale=g1_quarter[:, t : t + 1]
+                    z_planes[:, t, :], y_sum, ACT.Identity, bias=g1_eighth[:, t : t + 1], scale=g1_quarter[:, t : t + 1]
                 )
             z_grp.append(weave("z_grp%d" % n, z_planes, width))
 
@@ -245,7 +277,7 @@ def tile_picked_grayscott_none_p_kernel(
             per_bank = 512 // width
             result = sb("result%d" % n, [P, PACK, width], F32)
             for b in range(PACK // per_bank):
-                bank = psum.tile([P, per_bank, width], F32, name="acc%d_%d" % (n, b))
+                bank = bank_tile("acc%d_%d" % (n, b), [P, per_bank, width], 2 * n + b)
                 for r in range(per_bank):
                     out_pass(bank[:, r, :], b * per_bank + r, late["w4"], late["z2"], cells, True)
                     out_pass(bank[:, r, :], b * per_bank + r, late["w3"], z_q[n], slice(0, width), False)
@@ -255,7 +287,7 @@ def tile_picked_grayscott_none_p_kernel(
         def last_product(n):
             c0, width = CHUNKS[n]
             cells = slice(c0, c0 + width)
-            banks = [psum.tile([P, width], F32, name="last%d" % mo, tag="pre%d" % mo) for mo in range(PACK)]
+            banks = [bank_tile("last%d" % mo, [P, width], 4 + mo) for mo in range(PACK)]
             for mo in range(PACK):
                 out_pass(banks[mo][:], mo, late["w4"], late["z2"], cells, True)
             quantise_z(n)
@@ -264,28 +296,23 @@ def tile_picked_grayscott_none_p_kernel(
                 out_pass(banks[mo][:], mo, late["w3"], z_q[n], slice(0, width), False)
                 copy = (nc.scalar.copy, nc.vector.tensor_copy)[mo % 2]
                 copy(result[:, mo, :], banks[mo][:])
-            nc.sync.dma_start(out=out_rows[:, :, cells], in_=result[:])
+                if mo % 2:
+                    nc.sync.dma_start(out=out_rows[:, mo - 1 : mo + 1, cells], in_=result[:, mo - 1 : mo + 1, :])
 
         west_y(0)
         east_y(0)
-        e_mix = {}
-        for t in (1, 2, 3):
-            e_mix[t] = sb("e_mix%d" % t, [P, S], F32)
-            nc.vector.scalar_tensor_tensor(e_mix[t][:], e_win[t][:, :S], 4.0, e_east[t][:], ALU.mult, ALU.add)
-        for t in (1, 2, 3):
-            e_sum.append(e_gather("e_sum%d" % t, t, west_sb, e_mix[t]))
-        for t in (1, 2, 3):
-            finish_z2(t)
-        z2_grp = weave("z2_grp", z2_planes, S)
+        w4_grp = round_rows("w4_grp", w4_raw, nc.vector.tensor_copy)
+        w3_grp = round_rows("w3_grp", w3_raw, nc.vector.tensor_copy)
         late["w4"] = quantise("w4", w4_grp, N)
         late["w3"] = quantise("w3", w3_grp, N)
-        late["z2"] = quantise("z2", z2_grp, S)
+        west_y(1, tag="y_west0")
+        finish_z2()
+        east_y(1, planes_tag="z2_t3")
         quantise_z(0)
-        west_y(1, tag="e_sum3")
-        east_y(1)
+        late["z2"] = quantise("z2", z2_words[:].rearrange("p c u -> p (c u)").bitcast(BF16), S)
         second_product(0)
-        west_y(2, tag="z2_grp")
+        west_y(2, tag="z2_words")
         quantise_z(1)
-        east_y(2, tag="z_grp1")
+        east_y(2, tags=("z_grp1", None))
         second_product(1)
         last_product(2)

@@ -73,7 +73,7 @@ def tile_picked_grayscott_none_p_kernel(
         ident = sb("ident", [P, P], F32)
         make_identity(nc, ident[:])
 
-        e_window = [sb("e_window%d" % t, [P, 2 * S], F32) for t in range(PACK)]
+        e_window = [sb("e_window%d" % t, [P, 2 * S if t < 2 else S], F32) for t in range(PACK)]
         e = [e_window[0][:, :S]] + [sb("e%d" % t, [P, S], F32)[:] for t in range(1, PACK)]
 
         def bank_tile(name, shape, tag):
@@ -86,14 +86,14 @@ def tile_picked_grayscott_none_p_kernel(
 
         g1_quarter = scaled("g1_quarter", g1_sb, 0.25)
         g1_eighth = scaled("g1_eighth", g1_sb, 0.125)
-        for t in range(PACK):
+        for t in range(2):
             nc.gpsimd.memset(e_window[t][:, S:], 0.0)
 
         x_scale = sb("x_scale", [P, S], U8)
         nc.vector.tensor_copy(x_scale[:], x_scale_tab[:].indirect(offs_sb[:]))
 
-        def quantise(name, grouped, width):
-            code = sb(name + "_code", [P, width], U32)
+        def quantise(name, grouped, width, tag=None):
+            code = sb(name + "_code", [P, width], U32, tag=tag)
             scale = sb(name + "_scale", [P, width], U8)
             nc.vector.quantize_mx(out=code[:].bitcast(FP8X4), scales=scale[:], in_=grouped)
             return code, scale
@@ -123,7 +123,8 @@ def tile_picked_grayscott_none_p_kernel(
             )
             return bank
 
-        w2_q = [quantise("w2_%d" % u, round_plane_pair("w2_grp%d" % u, w2_raw, u, nc.scalar.copy), 2 * P) for u in range(2)]
+        w2_grp = [round_plane_pair("w2_grp0", w2_raw, 0, nc.vector.tensor_copy), round_plane_pair("w2_grp1", w2_raw, 1, nc.scalar.copy)]
+        w2_q = [quantise("w2_%d" % u, w2_grp[u], 2 * P) for u in range(2)]
         x_code = sb("x_code", [P, S], U32)
         halves = (slice(0, S // 2), slice(S // 2, S))
 
@@ -137,10 +138,11 @@ def tile_picked_grayscott_none_p_kernel(
             bank = first_product(0, tag, *w2_q[0], cells=half)
             nc.scalar.activation(e[0][:, half], bank[:], ACT.Sigmoid)
             nc.scalar.activation(e4[0][:, half], e[0][:, half], ACT.Copy, scale=4.0)
-        w1_q = [quantise("w1_0", round_plane_pair("w1_grp0", w1_raw, 0, nc.vector.tensor_copy), 2 * P)]
+        w1_grp0 = round_plane_pair("w1_grp0", w1_raw, 0, nc.vector.tensor_copy)
         e_west0 = sb("e_west0", [P, S], F32)
         for half in halves:
             nc.vector.tensor_tensor(e_west0[:, half], e_window[0][:].indirect(west_sb[:, entries(half)]), e4[0][:, half], ALU.add)
+        w1_q = [quantise("w1_0", w1_grp0, 2 * P, tag="e4_0")]
         w1_grp1 = round_plane_pair("w1_grp1", w1_raw, 1, nc.vector.tensor_copy)
         e_sum0 = sb("e_sum0", [P, S], F32, tag="w1_grp0")
         nc.vector.tensor_tensor(e_sum0[:], e_window[0][:].indirect(east_sb[:]), e_west0[:], ALU.add)
@@ -158,13 +160,13 @@ def tile_picked_grayscott_none_p_kernel(
             bank = first_product(t, y_bank[t], *w1_q[t // 2])
             nc.scalar.activation(y[t][:], bank[:], ACT.Sigmoid)
             nc.scalar.activation(q[t][:], e[t], ACT.Square, scale=2.0)
-        e_east, e_west = {}, {}
-        for t in range(1, PACK):
-            e_east[t] = sb("e_east%d" % t, [P, S], F32)
-            e_west[t] = sb("e_west%d" % t, [P, S], F32)
-            nc.scalar.activation(e4[t][:], e[t], ACT.Copy, scale=4.0)
-            nc.scalar.activation(e_east[t][:], e_window[t][:].indirect(east_sb[:]), ACT.Sigmoid)
-            nc.scalar.activation(e_west[t][:], e_window[t][:].indirect(west_sb[:]), ACT.Sigmoid)
+        e_east = {t: sb("e_east%d" % t, [P, S], F32) for t in range(1, PACK)}
+        e_west = {t: sb("e_west%d" % t, [P, S], F32) for t in range(1, PACK)}
+        steps = [(1, slice(0, S)), (0, slice(0, S))] + [(t, half) for half in halves for t in (2, 3)]
+        for t, cells in steps:
+            if t:
+                nc.scalar.activation(e_east[t][:, cells], e_window[t][:].indirect(east_sb[:, entries(cells)]), ACT.Sigmoid)
+                nc.scalar.activation(e_west[t][:, cells], e_window[t][:].indirect(west_sb[:, entries(cells)]), ACT.Sigmoid)
 
         def round_rows(name, raw, copy):
             grouped = sb(name, [P, N, PACK], BF16)
@@ -179,12 +181,14 @@ def tile_picked_grayscott_none_p_kernel(
         for t in range(PACK):
             nc.vector.scalar_tensor_tensor(y_local[t][:], q[t][:], 1.5, y[t][:], ALU.subtract, ALU.mult)
             nc.vector.scalar_tensor_tensor(made[t][:], q[t][:], 2.0, y[t][:], ALU.mult, ALU.mult)
+            if t:
+                nc.vector.tensor_scalar(e4[t][:], e[t], 4.0, None, ALU.mult)
 
         z2_sum = [bank_tile("z2_sum%d" % cb, [P, PACK, P], 4 + cb) for cb in range(4)]
-        for t in (1, 0, 2, 3):
-            terms = (e_sum0, made[0]) if t == 0 else (e4[t], e_east[t], made[t], e_west[t])
+        for t, cells in steps:
+            terms = (e_sum0, made[0]) if t == 0 else (e_east[t], e4[t], made[t], e_west[t])
             for n, term in enumerate(terms):
-                for cb in range(4):
+                for cb in range(cells.start // P, cells.stop // P):
                     nc.tensor.matmul(
                         z2_sum[cb][:, t, :],
                         lhsT=term[:, cb * P : (cb + 1) * P],
@@ -194,29 +198,25 @@ def tile_picked_grayscott_none_p_kernel(
                         stop=n == len(terms) - 1,
                     )
 
-        z2_words = sb("z2_words", [P, S, 2], F32)
-
-        def finish_z2():
-            for pair in range(2):
-                back = bank_tile("back%d" % pair, [P, 2, 2, P], 2 + pair)
-                for r in range(2):
-                    cb = 2 * pair + r
-                    z2_t = sb("z2_t%d" % cb, [P, H], BF16)
-                    nc.vector.scalar_tensor_tensor(
-                        z2_t[:].rearrange("c (p t) -> c p t", t=PACK),
-                        z2_sum[cb][:].rearrange("c t p -> c p t"),
-                        0.125,
-                        g2_row[:].rearrange("c (p t) -> c p t", t=PACK),
-                        ALU.mult,
-                        ALU.mult,
-                    )
-                    words = z2_t[:].bitcast(F32)
-                    for u in range(2):
-                        nc.tensor.transpose(back[:, r, u, :], words[:, u : 2 * P : 2], ident[:])
-                nc.scalar.copy(
-                    z2_words[:, pair * 2 * P : (pair + 1) * 2 * P, :].rearrange("p (r c) u -> p r c u", r=2),
-                    back[:].rearrange("p r u c -> p r c u"),
+        def finish_z2(pair):
+            z2_words = sb("z2_words%d" % pair, [P, 2 * P, 2], F32)
+            back = bank_tile("back%d" % pair, [P, 2, 2, P], 4 + 2 * pair)
+            for r in range(2):
+                cb = 2 * pair + r
+                z2_t = sb("z2_t%d" % cb, [P, H], BF16)
+                nc.vector.scalar_tensor_tensor(
+                    z2_t[:].rearrange("c (p t) -> c p t", t=PACK),
+                    z2_sum[cb][:].rearrange("c t p -> c p t"),
+                    0.125,
+                    g2_row[:].rearrange("c (p t) -> c p t", t=PACK),
+                    ALU.mult,
+                    ALU.mult,
                 )
+                words = z2_t[:].bitcast(F32)
+                for u in range(2):
+                    nc.tensor.transpose(back[:, r, u, :], words[:, u : 2 * P : 2], ident[:])
+            nc.scalar.copy(z2_words[:].rearrange("p (r c) u -> p r c u", r=2), back[:].rearrange("p r u c -> p r c u"))
+            return z2_words[:].rearrange("p c u -> p (c u)").bitcast(BF16)
 
         def weave(name, planes, width):
             grouped = sb(name, [P, width, PACK], BF16)
@@ -243,13 +243,12 @@ def tile_picked_grayscott_none_p_kernel(
                     y_west[n][:, t, :], y[t][:].indirect(west_sb[:, entries(cells)]), y_local[t][:, cells], ALU.subtract
                 )
 
-        def east_y(n, tags=(None, None), planes_tag=None):
+        def east_y(n, sums):
             c0, width = CHUNKS[n]
             cells = slice(c0, c0 + width)
-            sums = [sb("y_sum%d_%d" % (n, u), [P, 2, width], F32, tag=tags[u]) for u in range(2)]
-            z_planes = sb("z_planes%d" % n, [P, PACK, width], BF16, tag=planes_tag)
+            z_planes = sb("z_planes%d" % n, [P, PACK, width], BF16)
             for t in range(PACK):
-                y_sum = sums[t // 2][:, t % 2, :]
+                y_sum = sums[t]
                 nc.vector.tensor_tensor(y_sum, y[t][:].indirect(east_sb[:, entries(cells)]), y_west[n][:, t, :], ALU.add)
                 nc.scalar.activation(
                     z_planes[:, t, :], y_sum, ACT.Identity, bias=g1_eighth[:, t : t + 1], scale=g1_quarter[:, t : t + 1]
@@ -259,60 +258,95 @@ def tile_picked_grayscott_none_p_kernel(
         def quantise_z(n):
             z_q[n] = quantise("z_chunk%d" % n, z_grp[n], CHUNKS[n][1])
 
-        def out_pass(acc, mo, w_q, z_q, cells, first):
+        def out_pass(acc, mo, n, term, first):
+            c0, width = CHUNKS[n]
+            if term == "z":
+                w_q, act_q, cells = late["w3"], z_q[n], slice(0, width)
+            else:
+                w_q, act_q, cells = late["w4"], late["z2", c0 // 256], slice(c0 % 256, c0 % 256 + width)
             cols = slice(mo * P, (mo + 1) * P)
             nc.tensor.matmul_mx(
                 out=acc,
                 lhsT=w_q[0][:, cols].bitcast(FP8X4),
                 lhsT_scale=w_q[1][:, cols],
-                rhs=z_q[0][:, cells].bitcast(FP8X4),
-                rhs_scale=z_q[1][:, cells],
+                rhs=act_q[0][:, cells].bitcast(FP8X4),
+                rhs_scale=act_q[1][:, cells],
                 start=first,
                 stop=not first,
             )
 
-        def second_product(n):
-            c0, width = CHUNKS[n]
-            cells = slice(c0, c0 + width)
-            per_bank = 512 // width
-            result = sb("result%d" % n, [P, PACK, width], F32)
-            for b in range(PACK // per_bank):
-                bank = bank_tile("acc%d_%d" % (n, b), [P, per_bank, width], 2 * n + b)
-                for r in range(per_bank):
-                    out_pass(bank[:, r, :], b * per_bank + r, late["w4"], late["z2"], cells, True)
-                    out_pass(bank[:, r, :], b * per_bank + r, late["w3"], z_q[n], slice(0, width), False)
-                nc.scalar.copy(result[:, b * per_bank : (b + 1) * per_bank, :], bank[:])
-            nc.sync.dma_start(out=out_rows[:, :, cells], in_=result[:])
+        def open_product(n, term, bank0):
+            banks = [bank_tile("acc%d_%d" % (n, mo), [P, CHUNKS[n][1]], bank0 + mo) for mo in range(PACK)]
+            for mo in range(PACK):
+                out_pass(banks[mo][:], mo, n, term, True)
+            return banks
 
-        def last_product(n):
+        def close_product(n, term, banks, copies):
             c0, width = CHUNKS[n]
-            cells = slice(c0, c0 + width)
-            banks = [bank_tile("last%d" % mo, [P, width], 4 + mo) for mo in range(PACK)]
-            for mo in range(PACK):
-                out_pass(banks[mo][:], mo, late["w4"], late["z2"], cells, True)
-            quantise_z(n)
             result = sb("result%d" % n, [P, PACK, width], F32)
             for mo in range(PACK):
-                out_pass(banks[mo][:], mo, late["w3"], z_q[n], slice(0, width), False)
-                copy = (nc.scalar.copy, nc.vector.tensor_copy)[mo % 2]
-                copy(result[:, mo, :], banks[mo][:])
+                out_pass(banks[mo][:], mo, n, term, False)
+                copies[mo % 2](result[:, mo, :], banks[mo][:])
                 if mo % 2:
-                    nc.sync.dma_start(out=out_rows[:, mo - 1 : mo + 1, cells], in_=result[:, mo - 1 : mo + 1, :])
+                    nc.sync.dma_start(out=out_rows[:, mo - 1 : mo + 1, c0 : c0 + width], in_=result[:, mo - 1 : mo + 1, :])
+
+        def middle_product(n, tag):
+            c0, width = CHUNKS[n]
+            bank = bank_tile("acc%d" % n, [P, PACK, width], 0)
+            for mo in range(PACK):
+                out_pass(bank[:, mo, :], mo, n, "z2", True)
+                out_pass(bank[:, mo, :], mo, n, "z", False)
+            result = sb("result%d" % n, [P, PACK, width], F32, tag=tag)
+            nc.scalar.copy(result[:], bank[:])
+            nc.sync.dma_start(out=out_rows[:, :, c0 : c0 + width], in_=result[:])
+
+        def last_chunk(n, z2_grp):
+            c0, width = CHUNKS[n]
+            cells = slice(c0, c0 + width)
+            west_sum = sb("y_west%d" % n, [P, PACK, width], F32, tag="z2_t2")
+            grouped = sb("z_grp%d" % n, [P, width, PACK], BF16)
+
+            def west_step(t):
+                nc.vector.tensor_tensor(
+                    west_sum[:, t, :], y[t][:].indirect(west_sb[:, entries(cells)]), y_local[t][:, cells], ALU.subtract
+                )
+
+            def east_step(t, tag=None):
+                y_sum = sb("y_sum%d_%d" % (n, t), [P, width], F32, tag=tag)
+                nc.vector.tensor_tensor(y_sum[:], y[t][:].indirect(east_sb[:, entries(cells)]), west_sum[:, t, :], ALU.add)
+                nc.scalar.activation(
+                    grouped[:, :, t], y_sum[:], ACT.Identity, bias=g1_eighth[:, t : t + 1], scale=g1_quarter[:, t : t + 1]
+                )
+
+            west_step(0)
+            west_step(1)
+            quantise_z(n - 1)
+            east_step(0, tag="z_grp%d" % (n - 1))
+            west_step(2)
+            late["z2", 1] = quantise("z2_1", z2_grp, 2 * P)
+            east_step(1, tag="z2_words1")
+            west_step(3)
+            east_step(2)
+            east_step(3)
+            z_grp.append(grouped[:].rearrange("p c t -> p (c t)"))
 
         west_y(0)
-        east_y(0)
+        east_y(0, [sb("y_sum0_%d" % t, [P, 2 * P], F32, tag=tag)[:] for t, tag in enumerate(("q1", "q2", "q3", None))])
         w4_grp = round_rows("w4_grp", w4_raw, nc.vector.tensor_copy)
         w3_grp = round_rows("w3_grp", w3_raw, nc.vector.tensor_copy)
-        late["w4"] = quantise("w4", w4_grp, N)
-        late["w3"] = quantise("w3", w3_grp, N)
+        late["w4"] = quantise("w4", w4_grp, N, tag="q0")
+        late["w3"] = quantise("w3", w3_grp, N, tag="made0")
         west_y(1, tag="y_west0")
-        finish_z2()
-        east_y(1, planes_tag="z2_t3")
+        z2_grp0 = finish_z2(0)
+        y_sum1 = sb("y_sum1", [P, PACK, P], F32, tag="z2_t0")
+        east_y(1, [y_sum1[:, t, :] for t in range(PACK)])
+        z2_grp1 = finish_z2(1)
         quantise_z(0)
-        late["z2"] = quantise("z2", z2_words[:].rearrange("p c u -> p (c u)").bitcast(BF16), S)
-        second_product(0)
-        west_y(2, tag="z2_words")
-        quantise_z(1)
-        east_y(2, tags=("z_grp1", None))
-        second_product(1)
-        last_product(2)
+        first_banks = open_product(0, "z", 0)
+        late["z2", 0] = quantise("z2_0", z2_grp0, 2 * P)
+        close_product(0, "z2", first_banks, (nc.scalar.copy, nc.scalar.copy))
+        last_chunk(2, z2_grp1)
+        last_banks = open_product(2, "z2", 4)
+        middle_product(1, "y_sum2_3")
+        quantise_z(2)
+        close_product(2, "z", last_banks, (nc.scalar.copy, nc.vector.tensor_copy))

@@ -31,8 +31,11 @@ def tile_picked_grayscott_none_p_kernel(
         keep = ctx.enter_context(tc.tile_pool(name="keep", bufs=1))
         psum = ctx.enter_context(tc.psum_pool(name="psum", bufs=1))
 
+        seen = {}
+
         def sb(name, shape, dtype, tag=None):
-            return keep.tile(shape, dtype, name=name, tag=tag or name, align_bytes=64)
+            seen[name] = keep.tile(shape, dtype, name=name, tag=tag or name, align_bytes=64)
+            return seen[name]
 
         offs_sb = lists.tile([P, LIST_COLS], U16, name="offs_sb")
         west_sb = lists.tile([P, LIST_COLS], U16, name="west_sb")
@@ -46,35 +49,32 @@ def tile_picked_grayscott_none_p_kernel(
                 in_=x_scales[0, 4 * quad : 4 * quad + 4, :].bitcast(I32),
             )
 
-        warm_in = sb("warm_in", [P, 1], F32)
-        warm_out = sb("warm_out", [P, 1], F32)
-        nc.gpsimd.memset(warm_in[:], 0.0)
-        nc.scalar.activation(warm_out[:], warm_in[:], ACT.Sigmoid)
-
         def load_weight(name, w):
             raw = sb(name, [P, PACK, 512], F32)
             nc.sync.dma_start(out=raw[:], in_=w.rearrange("(p j) c -> p j c", j=PACK))
             return raw
 
+        def load_gain(name, g):
+            col = sb(name, [P, PACK], F32)
+            nc.sync.dma_start(out=col[:], in_=g.rearrange("(p t) o -> p (t o)", t=PACK))
+            return col
+
         nc.sync.dma_start(offs_sb[:], offs)
-        w2_raw = load_weight("w2_raw", w2)
-        nc.sync.dma_start(west_sb[:], west)
-        nc.sync.dma_start(east_sb[:], east)
+        w1_raw = load_weight("w1_raw", w1)
+        g2_sb = load_gain("g2_sb", g2)
+        g1_sb = load_gain("g1_sb", g1)
         x_word_tab = sb("x_word_tab", [P, T], I32)
         nc.sync.dma_start(out=x_word_tab[:], in_=x_words[0].rearrange("p n t -> p (n t)").bitcast(I32))
-        w1_raw = load_weight("w1_raw", w1)
-        g1_sb = sb("g1_sb", [P, PACK], F32)
-        nc.gpsimd.dma_start(out=g1_sb[:], in_=g1.rearrange("(p t) o -> p (t o)", t=PACK))
+        w2_raw = [sb("w2_raw%d" % h, [P, PACK, H // 2], F32) for h in range(2)]
+        for h in range(2):
+            nc.sync.dma_start(out=w2_raw[h][:], in_=w2.rearrange("(p j) c -> p j c", j=PACK)[:, :, h * H // 2 : (h + 1) * H // 2])
+        nc.sync.dma_start(west_sb[:], west)
+        nc.sync.dma_start(east_sb[:], east)
         w4_raw = load_weight("w4_raw", w4)
         w3_raw = load_weight("w3_raw", w3)
-        g2_row = sb("g2_row", [P, H], F32)
-        nc.sync.dma_start(out=g2_row[:], in_=g2.rearrange("h o -> (h o)").partition_broadcast(P))
 
         ident = sb("ident", [P, P], F32)
         make_identity(nc, ident[:])
-
-        e_window = [sb("e_window%d" % t, [P, 2 * S if t < 2 else S], F32) for t in range(PACK)]
-        e = [e_window[0][:, :S]] + [sb("e%d" % t, [P, S], F32)[:] for t in range(1, PACK)]
 
         def bank_tile(name, shape, tag):
             return psum.tile(shape, F32, name=name, tag="bank%d" % tag)
@@ -84,10 +84,14 @@ def tile_picked_grayscott_none_p_kernel(
             nc.gpsimd.tensor_scalar(res[:], g[:], factor, 0.0, ALU.mult, ALU.add)
             return res
 
+        g2_col = scaled("g2_col", g2_sb, 0.125)
+        spread = bank_tile("spread", [P, PACK, P], 2)
+        for t in range(PACK):
+            nc.tensor.transpose(spread[:, t, :], g2_col[:, t : t + 1].to_broadcast([P, P]), ident[:])
+        g2_eighth = sb("g2_eighth", [P, H], F32)
+        nc.scalar.copy(g2_eighth[:].rearrange("c (p t) -> c p t", t=PACK), spread[:].rearrange("c t p -> c p t"))
         g1_quarter = scaled("g1_quarter", g1_sb, 0.25)
         g1_eighth = scaled("g1_eighth", g1_sb, 0.125)
-        for t in range(2):
-            nc.gpsimd.memset(e_window[t][:, S:], 0.0)
 
         x_scale = sb("x_scale", [P, S], U8)
         nc.vector.tensor_copy(x_scale[:], x_scale_tab[:].indirect(offs_sb[:]))
@@ -98,15 +102,12 @@ def tile_picked_grayscott_none_p_kernel(
             nc.vector.quantize_mx(out=code[:].bitcast(FP8X4), scales=scale[:], in_=grouped)
             return code, scale
 
-        def round_plane_pair(name, raw, u, *copies):
+        def round_plane_pair(name, raw, u, copy):
             grouped = sb(name, [P, 2, P, PACK], BF16)
-            share = P // len(copies)
-            for n, copy in enumerate(copies):
-                rows = slice(n * share, (n + 1) * share)
-                copy(
-                    grouped[:].rearrange("p t m j -> p m t j")[:, rows],
-                    raw[:].rearrange("p j (m t) -> p m t j", t=PACK)[:, rows, 2 * u : 2 * u + 2, :],
-                )
+            copy(
+                grouped[:].rearrange("p t m j -> p m t j"),
+                raw[:].rearrange("p j (m t) -> p m t j", t=PACK)[:, :, 2 * u : 2 * u + 2, :],
+            )
             return grouped[:].rearrange("p t m j -> p (t m j)")
 
         def first_product(t, tag, code, scale, cells=slice(0, S)):
@@ -123,51 +124,6 @@ def tile_picked_grayscott_none_p_kernel(
             )
             return bank
 
-        w2_grp = [round_plane_pair("w2_grp0", w2_raw, 0, nc.vector.tensor_copy), round_plane_pair("w2_grp1", w2_raw, 1, nc.scalar.copy)]
-        w2_q = [quantise("w2_%d" % u, w2_grp[u], 2 * P) for u in range(2)]
-        x_code = sb("x_code", [P, S], U32)
-        halves = (slice(0, S // 2), slice(S // 2, S))
-
-        def entries(cells):
-            return slice(cells.start // 16, cells.stop // 16)
-
-        for half in halves:
-            nc.vector.tensor_copy(x_code[:, half], x_word_tab[:].bitcast(U32).indirect(offs_sb[:, entries(half)]))
-        e4 = [sb("e4_%d" % t, [P, S], F32) for t in range(PACK)]
-        for tag, half in zip((1, 2), halves):
-            bank = first_product(0, tag, *w2_q[0], cells=half)
-            nc.scalar.activation(e[0][:, half], bank[:], ACT.Sigmoid)
-            nc.scalar.activation(e4[0][:, half], e[0][:, half], ACT.Copy, scale=4.0)
-        w1_grp0 = round_plane_pair("w1_grp0", w1_raw, 0, nc.vector.tensor_copy)
-        e_west0 = sb("e_west0", [P, S], F32)
-        for half in halves:
-            nc.vector.tensor_tensor(e_west0[:, half], e_window[0][:].indirect(west_sb[:, entries(half)]), e4[0][:, half], ALU.add)
-        w1_q = [quantise("w1_0", w1_grp0, 2 * P, tag="e4_0")]
-        w1_grp1 = round_plane_pair("w1_grp1", w1_raw, 1, nc.vector.tensor_copy)
-        e_sum0 = sb("e_sum0", [P, S], F32, tag="w1_grp0")
-        nc.vector.tensor_tensor(e_sum0[:], e_window[0][:].indirect(east_sb[:]), e_west0[:], ALU.add)
-        w1_q.append(quantise("w1_1", w1_grp1, 2 * P))
-
-        y = [sb("y%d" % t, [P, S], F32) for t in range(PACK)]
-        q = [sb("q%d" % t, [P, S], F32) for t in range(PACK)]
-        e_bank = (None, 3, 2, 0)
-        y_bank = (0, 1, 3, 1)
-        for t in range(PACK):
-            if t >= 1:
-                bank = first_product(t, e_bank[t], *w2_q[t // 2])
-                nc.scalar.activation(e[t], bank[:], ACT.Sigmoid)
-                nc.scalar.copy(e_window[t][:, :S], bank[:])
-            bank = first_product(t, y_bank[t], *w1_q[t // 2])
-            nc.scalar.activation(y[t][:], bank[:], ACT.Sigmoid)
-            nc.scalar.activation(q[t][:], e[t], ACT.Square, scale=2.0)
-        e_east = {t: sb("e_east%d" % t, [P, S], F32) for t in range(1, PACK)}
-        e_west = {t: sb("e_west%d" % t, [P, S], F32) for t in range(1, PACK)}
-        steps = [(1, slice(0, S)), (0, slice(0, S))] + [(t, half) for half in halves for t in (2, 3)]
-        for t, cells in steps:
-            if t:
-                nc.scalar.activation(e_east[t][:, cells], e_window[t][:].indirect(east_sb[:, entries(cells)]), ACT.Sigmoid)
-                nc.scalar.activation(e_west[t][:, cells], e_window[t][:].indirect(west_sb[:, entries(cells)]), ACT.Sigmoid)
-
         def round_rows(name, raw, copy):
             grouped = sb(name, [P, N, PACK], BF16)
             copy(
@@ -176,27 +132,77 @@ def tile_picked_grayscott_none_p_kernel(
             )
             return grouped[:].rearrange("p n j -> p (n j)")
 
+        def entries(cells):
+            return slice(cells.start // 16, cells.stop // 16)
+
+        halves = (slice(0, S // 2), slice(S // 2, S))
+
+        w1_grp = [round_plane_pair("w1_grp0", w1_raw, 0, nc.vector.tensor_copy), round_plane_pair("w1_grp1", w1_raw, 1, nc.scalar.copy)]
+        w1_q = [quantise("w1_%d" % u, w1_grp[u], 2 * P) for u in range(2)]
+        x_code = sb("x_code", [P, S], U32)
+        for half in halves:
+            nc.vector.tensor_copy(x_code[:, half], x_word_tab[:].bitcast(U32).indirect(offs_sb[:, entries(half)]))
+
+        e_window = [sb("e_window%d" % t, [P, 2 * S], F32) for t in range(PACK)]
+        e_pre = [window[:, :S] for window in e_window]
+        e_tanh = [window[:, S:] for window in e_window]
+        y_window = [sb("y_window%d" % t, [P, S], F32) for t in range(PACK)]
+        y = [window[:] for window in y_window]
+        q_tiles = [sb("q%d" % t, [P, S], F32) for t in range(PACK)]
+        q = [tile[:] for tile in q_tiles]
         y_local = [sb("y_local%d" % t, [P, S], F32) for t in range(PACK)]
         made = [sb("made%d" % t, [P, S], F32) for t in range(PACK)]
+
+        for tag, half in zip((4, 3), halves):
+            bank = first_product(0, tag, *w1_q[0], cells=half)
+            nc.scalar.activation(y[0][:, half], bank[:], ACT.Sigmoid)
+        for t in range(1, PACK):
+            bank = first_product(t, 4 + t, *w1_q[t // 2])
+            nc.scalar.activation(y[t], bank[:], ACT.Sigmoid)
+
+        w2_grp = sb("w2_grp", [P, PACK, P, PACK], BF16)
+        for h in range(2):
+            nc.vector.tensor_copy(
+                w2_grp[:].rearrange("p t m j -> p m t j")[:, h * P // 2 : (h + 1) * P // 2],
+                w2_raw[h][:].rearrange("p j (m t) -> p m t j", t=PACK),
+            )
+        w2_q = [quantise("w2_%d" % u, w2_grp[:, 2 * u : 2 * u + 2].rearrange("p t m j -> p (t m j)"), 2 * P) for u in range(2)]
+        late = {}
+        late_raw = {0: ("w4", w4_raw), 2: ("w3", w3_raw)}
+        e_bank = [first_product(t, t, *w2_q[t // 2]) for t in range(PACK)]
         for t in range(PACK):
-            nc.vector.scalar_tensor_tensor(y_local[t][:], q[t][:], 1.5, y[t][:], ALU.subtract, ALU.mult)
-            nc.vector.scalar_tensor_tensor(made[t][:], q[t][:], 2.0, y[t][:], ALU.mult, ALU.mult)
-            if t:
-                nc.vector.tensor_scalar(e4[t][:], e[t], 4.0, None, ALU.mult)
+            nc.scalar.activation(e_tanh[t], e_bank[t][:], ACT.Tanh, scale=0.5)
+            nc.scalar.activation(q[t], e_tanh[t], ACT.Square, bias=1.0)
+            if t in late_raw:
+                name, raw = late_raw[t]
+                grp = round_rows(name + "_grp", raw, nc.vector.tensor_copy)
+            nc.vector.scalar_tensor_tensor(y_local[t][:], q[t], 1.5, y[t], ALU.subtract, ALU.mult)
+            nc.vector.scalar_tensor_tensor(made[t][:], q[t], 2.0, y[t], ALU.mult, ALU.mult)
+            if t in late_raw:
+                late[name] = quantise(name, grp, N)
 
         z2_sum = [bank_tile("z2_sum%d" % cb, [P, PACK, P], 4 + cb) for cb in range(4)]
-        for t, cells in steps:
-            terms = (e_sum0, made[0]) if t == 0 else (e_east[t], e4[t], made[t], e_west[t])
-            for n, term in enumerate(terms):
-                for cb in range(cells.start // P, cells.stop // P):
-                    nc.tensor.matmul(
-                        z2_sum[cb][:, t, :],
-                        lhsT=term[:, cb * P : (cb + 1) * P],
-                        rhs=ident[:],
-                        is_transpose=True,
-                        start=n == 0,
-                        stop=n == len(terms) - 1,
-                    )
+
+        def sum_z2(cells, planes):
+            for t in planes:
+                if cells.start == 0:
+                    nc.scalar.copy(e_pre[t], e_bank[t][:])
+                width = cells.stop - cells.start
+                e_east = sb("e_east%d_%d" % (t, cells.start), [P, width], F32)
+                e_west = sb("e_west%d_%d" % (t, cells.start), [P, width], F32)
+                nc.scalar.activation(e_east[:], e_window[t][:].indirect(east_sb[:, entries(cells)]), ACT.Sigmoid)
+                nc.scalar.activation(e_west[:], e_window[t][:].indirect(west_sb[:, entries(cells)]), ACT.Sigmoid)
+                terms = (e_tanh[t][:, cells], e_tanh[t][:, cells], made[t][:, cells], e_east, e_west)
+                for n, term in enumerate(terms):
+                    for b, cb in enumerate(range(cells.start // P, cells.stop // P)):
+                        nc.tensor.matmul(
+                            z2_sum[cb][:, t, :],
+                            lhsT=term[:, b * P : (b + 1) * P],
+                            rhs=ident[:],
+                            is_transpose=True,
+                            start=n == 0,
+                            stop=n == len(terms) - 1,
+                        )
 
         def finish_z2(pair):
             z2_words = sb("z2_words%d" % pair, [P, 2 * P, 2], F32)
@@ -207,9 +213,9 @@ def tile_picked_grayscott_none_p_kernel(
                 nc.vector.scalar_tensor_tensor(
                     z2_t[:].rearrange("c (p t) -> c p t", t=PACK),
                     z2_sum[cb][:].rearrange("c t p -> c p t"),
-                    0.125,
-                    g2_row[:].rearrange("c (p t) -> c p t", t=PACK),
-                    ALU.mult,
+                    2.0,
+                    g2_eighth[:].rearrange("c (p t) -> c p t", t=PACK),
+                    ALU.add,
                     ALU.mult,
                 )
                 words = z2_t[:].bitcast(F32)
@@ -218,47 +224,48 @@ def tile_picked_grayscott_none_p_kernel(
             nc.scalar.copy(z2_words[:].rearrange("p (r c) u -> p r c u", r=2), back[:].rearrange("p r u c -> p r c u"))
             return z2_words[:].rearrange("p c u -> p (c u)").bitcast(BF16)
 
-        def weave(name, planes, width):
+        def weave(name, planes, width, copy):
             grouped = sb(name, [P, width, PACK], BF16)
-            nc.scalar.copy(
+            copy(
                 grouped[:].rearrange("p (c i) t -> p c t i", i=4),
                 planes[:].rearrange("p t (c i) -> p c t i", i=4),
             )
             return grouped[:].rearrange("p c t -> p (c t)")
 
-
         out_rows = out.rearrange("(mo p) c -> p mo c", p=P)
-        late = {}
-        z_grp = []
-
+        z_grp = {}
+        z_planes = {}
         y_west = {}
         z_q = {}
 
-        def west_y(n, tag=None):
-            c0, width = CHUNKS[n]
-            cells = slice(c0, c0 + width)
-            y_west[n] = sb("y_west%d" % n, [P, PACK, width], F32, tag=tag)
-            for t in range(PACK):
+        def chunk_cells(n):
+            return slice(CHUNKS[n][0], CHUNKS[n][0] + CHUNKS[n][1])
+
+        def west_step(t):
+            y_west[t] = sb("y_west%d" % t, [P, S], F32)
+            for half in halves:
                 nc.vector.tensor_tensor(
-                    y_west[n][:, t, :], y[t][:].indirect(west_sb[:, entries(cells)]), y_local[t][:, cells], ALU.subtract
+                    y_west[t][:, half], y_window[t][:].indirect(west_sb[:, entries(half)]), y_local[t][:, half], ALU.subtract
                 )
 
-        def east_y(n, sums):
-            c0, width = CHUNKS[n]
-            cells = slice(c0, c0 + width)
-            z_planes = sb("z_planes%d" % n, [P, PACK, width], BF16)
+        def east_step(n, t, dest, tag=None):
+            cells = chunk_cells(n)
+            y_sum = sb("y_sum%d_%d" % (n, t), [P, CHUNKS[n][1]], F32, tag=tag)
+            nc.vector.tensor_tensor(y_sum[:], y_window[t][:].indirect(east_sb[:, entries(cells)]), y_west[t][:, cells], ALU.add)
+            nc.scalar.activation(dest, y_sum[:], ACT.Identity, bias=g1_eighth[:, t : t + 1], scale=g1_quarter[:, t : t + 1])
+
+        def gather_y(n):
+            z_planes[n] = sb("z_planes%d" % n, [P, PACK, CHUNKS[n][1]], BF16)
             for t in range(PACK):
-                y_sum = sums[t]
-                nc.vector.tensor_tensor(y_sum, y[t][:].indirect(east_sb[:, entries(cells)]), y_west[n][:, t, :], ALU.add)
-                nc.scalar.activation(
-                    z_planes[:, t, :], y_sum, ACT.Identity, bias=g1_eighth[:, t : t + 1], scale=g1_quarter[:, t : t + 1]
-                )
-            z_grp.append(weave("z_grp%d" % n, z_planes, width))
+                east_step(n, t, z_planes[n][:, t, :])
+
+        def weave_z(n, copy):
+            z_grp[n] = weave("z_grp%d" % n, z_planes[n], CHUNKS[n][1], copy)
 
         def quantise_z(n):
             z_q[n] = quantise("z_chunk%d" % n, z_grp[n], CHUNKS[n][1])
 
-        def out_pass(acc, mo, n, term, first):
+        def out_pass(acc, mo, n, term, start, stop):
             c0, width = CHUNKS[n]
             if term == "z":
                 w_q, act_q, cells = late["w3"], z_q[n], slice(0, width)
@@ -271,82 +278,86 @@ def tile_picked_grayscott_none_p_kernel(
                 lhsT_scale=w_q[1][:, cols],
                 rhs=act_q[0][:, cells].bitcast(FP8X4),
                 rhs_scale=act_q[1][:, cells],
-                start=first,
-                stop=not first,
+                start=start,
+                stop=stop,
             )
 
         def open_product(n, term, bank0):
             banks = [bank_tile("acc%d_%d" % (n, mo), [P, CHUNKS[n][1]], bank0 + mo) for mo in range(PACK)]
             for mo in range(PACK):
-                out_pass(banks[mo][:], mo, n, term, True)
+                out_pass(banks[mo][:], mo, n, term, True, False)
             return banks
 
         def close_product(n, term, banks, copies):
             c0, width = CHUNKS[n]
             result = sb("result%d" % n, [P, PACK, width], F32)
             for mo in range(PACK):
-                out_pass(banks[mo][:], mo, n, term, False)
+                out_pass(banks[mo][:], mo, n, term, False, True)
                 copies[mo % 2](result[:, mo, :], banks[mo][:])
                 if mo % 2:
                     nc.sync.dma_start(out=out_rows[:, mo - 1 : mo + 1, c0 : c0 + width], in_=result[:, mo - 1 : mo + 1, :])
 
-        def middle_product(n, tag):
-            c0, width = CHUNKS[n]
-            bank = bank_tile("acc%d" % n, [P, PACK, width], 0)
+        def open_middle(n):
+            bank = bank_tile("acc%d" % n, [P, PACK, CHUNKS[n][1]], 5)
             for mo in range(PACK):
-                out_pass(bank[:, mo, :], mo, n, "z2", True)
-                out_pass(bank[:, mo, :], mo, n, "z", False)
-            result = sb("result%d" % n, [P, PACK, width], F32, tag=tag)
+                out_pass(bank[:, mo, :], mo, n, "z2", mo == 0, False)
+            return bank
+
+        def close_middle(n, bank):
+            c0, width = CHUNKS[n]
+            for mo in range(PACK):
+                out_pass(bank[:, mo, :], mo, n, "z", False, mo == PACK - 1)
+            result = sb("result%d" % n, [P, PACK, width], F32)
             nc.scalar.copy(result[:], bank[:])
             nc.sync.dma_start(out=out_rows[:, :, c0 : c0 + width], in_=result[:])
 
-        def last_chunk(n, z2_grp):
+        def open_last(n):
+            banks = [bank_tile("acc%d_%d" % (n, half), [P, 2, CHUNKS[n][1]], tag) for half, tag in enumerate((4, 7))]
+            for mo in range(PACK):
+                out_pass(banks[mo // 2][:, mo % 2, :], mo, n, "z2", mo % 2 == 0, False)
+            return banks
+
+        def close_last(n, banks):
             c0, width = CHUNKS[n]
-            cells = slice(c0, c0 + width)
-            west_sum = sb("y_west%d" % n, [P, PACK, width], F32, tag="z2_t2")
-            grouped = sb("z_grp%d" % n, [P, width, PACK], BF16)
+            for half, copy in enumerate((nc.scalar.copy, nc.vector.tensor_copy)):
+                for mo in (2 * half, 2 * half + 1):
+                    out_pass(banks[half][:, mo % 2, :], mo, n, "z", False, mo % 2 == 1)
+                result = sb("result%d_%d" % (n, half), [P, 2, width], F32)
+                copy(result[:], banks[half][:])
+                nc.sync.dma_start(out=out_rows[:, 2 * half : 2 * half + 2, c0 : c0 + width], in_=result[:])
 
-            def west_step(t):
-                nc.vector.tensor_tensor(
-                    west_sum[:, t, :], y[t][:].indirect(west_sb[:, entries(cells)]), y_local[t][:, cells], ALU.subtract
-                )
-
-            def east_step(t, tag=None):
-                y_sum = sb("y_sum%d_%d" % (n, t), [P, width], F32, tag=tag)
-                nc.vector.tensor_tensor(y_sum[:], y[t][:].indirect(east_sb[:, entries(cells)]), west_sum[:, t, :], ALU.add)
-                nc.scalar.activation(
-                    grouped[:, :, t], y_sum[:], ACT.Identity, bias=g1_eighth[:, t : t + 1], scale=g1_quarter[:, t : t + 1]
-                )
-
-            west_step(0)
-            west_step(1)
-            quantise_z(n - 1)
-            east_step(0, tag="z_grp%d" % (n - 1))
-            west_step(2)
-            late["z2", 1] = quantise("z2_1", z2_grp, 2 * P)
-            east_step(1, tag="z2_words1")
-            west_step(3)
-            east_step(2)
-            east_step(3)
-            z_grp.append(grouped[:].rearrange("p c t -> p (c t)"))
-
-        west_y(0)
-        east_y(0, [sb("y_sum0_%d" % t, [P, 2 * P], F32, tag=tag)[:] for t, tag in enumerate(("q1", "q2", "q3", None))])
-        w4_grp = round_rows("w4_grp", w4_raw, nc.vector.tensor_copy)
-        w3_grp = round_rows("w3_grp", w3_raw, nc.vector.tensor_copy)
-        late["w4"] = quantise("w4", w4_grp, N, tag="q0")
-        late["w3"] = quantise("w3", w3_grp, N, tag="made0")
-        west_y(1, tag="y_west0")
+        sum_z2(slice(0, S), (0, 1))
+        for t in range(PACK):
+            west_step(t)
+        for half in halves:
+            sum_z2(half, (2, 3))
+        planes0 = z_planes[0] = sb("z_planes0", [P, PACK, CHUNKS[0][1]], BF16)
+        planes1 = z_planes[1] = sb("z_planes1", [P, PACK, CHUNKS[1][1]], BF16)
+        east_step(0, 0, planes0[:, 0, :])
         z2_grp0 = finish_z2(0)
-        y_sum1 = sb("y_sum1", [P, PACK, P], F32, tag="z2_t0")
-        east_y(1, [y_sum1[:, t, :] for t in range(PACK)])
+        east_step(0, 1, planes0[:, 1, :], "e_west3_0")
+        east_step(0, 2, planes0[:, 2, :], "z2_t0")
+        east_step(0, 3, planes0[:, 3, :], "z2_t1")
+        weave_z(0, nc.scalar.copy)
         z2_grp1 = finish_z2(1)
-        quantise_z(0)
-        first_banks = open_product(0, "z", 0)
         late["z2", 0] = quantise("z2_0", z2_grp0, 2 * P)
-        close_product(0, "z2", first_banks, (nc.scalar.copy, nc.scalar.copy))
-        last_chunk(2, z2_grp1)
-        last_banks = open_product(2, "z2", 4)
-        middle_product(1, "y_sum2_3")
+        east_step(1, 0, planes1[:, 0, :], "e_west3_256")
+        quantise_z(0)
+        close_product(0, "z", open_product(0, "z2", 0), (nc.scalar.copy, nc.scalar.copy))
+        east_step(1, 1, planes1[:, 1, :], "g2_eighth")
+        east_step(1, 2, planes1[:, 2, :], "z2_t2")
+        east_step(1, 3, planes1[:, 3, :], "z2_t3")
+        late["z2", 1] = quantise("z2_1", z2_grp1, 2 * P)
+        middle_bank = open_middle(1)
+        last_banks = open_last(2)
+        last = sb("z_grp2", [P, CHUNKS[2][1], PACK], BF16)
+        east_step(2, 0, last[:, :, 0], "z_grp0")
+        east_step(2, 1, last[:, :, 1], "g2_eighth")
+        weave_z(1, nc.vector.tensor_copy)
+        east_step(2, 2, last[:, :, 2], "z2_words1")
+        quantise_z(1)
+        east_step(2, 3, last[:, :, 3], "z_planes1")
+        z_grp[2] = last[:].rearrange("p c t -> p (c t)")
+        close_middle(1, middle_bank)
         quantise_z(2)
-        close_product(2, "z", last_banks, (nc.scalar.copy, nc.vector.tensor_copy))
+        close_last(2, last_banks)

@@ -91,7 +91,6 @@ def tile_picked_grayscott_none_p_kernel(
         g2_eighth = sb("g2_eighth", [P, H], F32)
         nc.scalar.copy(g2_eighth[:].rearrange("c (p t) -> c p t", t=PACK), spread[:].rearrange("c t p -> c p t"))
         g1_quarter = scaled("g1_quarter", g1_sb, 0.25)
-        g1_eighth = scaled("g1_eighth", g1_sb, 0.125)
 
         x_scale = sb("x_scale", [P, S], U8)
         nc.vector.tensor_copy(x_scale[:], x_scale_tab[:].indirect(offs_sb[:]))
@@ -124,13 +123,11 @@ def tile_picked_grayscott_none_p_kernel(
             )
             return bank
 
-        def round_rows(name, raw, copy):
-            grouped = sb(name, [P, N, PACK], BF16)
+        def round_rows(grouped, raw, cols, copy):
             copy(
-                grouped[:].rearrange("p (c i) j -> p c j i", i=4),
-                raw[:].rearrange("p j (c i) -> p c j i", i=4),
+                grouped[:, cols, :].rearrange("p (c i) j -> p c j i", i=4),
+                raw[:, :, cols].rearrange("p j (c i) -> p c j i", i=4),
             )
-            return grouped[:].rearrange("p n j -> p (n j)")
 
         def entries(cells):
             return slice(cells.start // 16, cells.stop // 16)
@@ -151,7 +148,7 @@ def tile_picked_grayscott_none_p_kernel(
         q_tiles = [sb("q%d" % t, [P, S], F32) for t in range(PACK)]
         q = [tile[:] for tile in q_tiles]
         y_local = [sb("y_local%d" % t, [P, S], F32) for t in range(PACK)]
-        made = [sb("made%d" % t, [P, S], F32) for t in range(PACK)]
+        made = {t: sb("made%d" % t, [P, S], F32) for t in range(1, PACK)}
 
         for tag, half in zip((4, 3), halves):
             bank = first_product(0, tag, *w1_q[0], cells=half)
@@ -168,18 +165,17 @@ def tile_picked_grayscott_none_p_kernel(
             )
         w2_q = [quantise("w2_%d" % u, w2_grp[:, 2 * u : 2 * u + 2].rearrange("p t m j -> p (t m j)"), 2 * P) for u in range(2)]
         late = {}
-        late_raw = {0: ("w4", w4_raw), 2: ("w3", w3_raw)}
+        w3_grp = sb("w3_grp", [P, N, PACK], BF16)
+        w4_grp = sb("w4_grp", [P, N, PACK], BF16)
         e_bank = [first_product(t, t, *w2_q[t // 2]) for t in range(PACK)]
         for t in range(PACK):
             nc.scalar.activation(e_tanh[t], e_bank[t][:], ACT.Tanh, scale=0.5)
             nc.scalar.activation(q[t], e_tanh[t], ACT.Square, bias=1.0)
-            if t in late_raw:
-                name, raw = late_raw[t]
-                grp = round_rows(name + "_grp", raw, nc.vector.tensor_copy)
+            if t == 0:
+                round_rows(w4_grp, w4_raw, halves[0], nc.vector.tensor_copy)
             nc.vector.scalar_tensor_tensor(y_local[t][:], q[t], 1.5, y[t], ALU.subtract, ALU.mult)
-            nc.vector.scalar_tensor_tensor(made[t][:], q[t], 2.0, y[t], ALU.mult, ALU.mult)
-            if t in late_raw:
-                late[name] = quantise(name, grp, N)
+            if t:
+                nc.vector.scalar_tensor_tensor(made[t][:], q[t], 2.0, y[t], ALU.mult, ALU.mult)
 
         z2_sum = [bank_tile("z2_sum%d" % cb, [P, PACK, P], 4 + cb) for cb in range(4)]
 
@@ -192,7 +188,8 @@ def tile_picked_grayscott_none_p_kernel(
                 e_west = sb("e_west%d_%d" % (t, cells.start), [P, width], F32)
                 nc.scalar.activation(e_east[:], e_window[t][:].indirect(east_sb[:, entries(cells)]), ACT.Sigmoid)
                 nc.scalar.activation(e_west[:], e_window[t][:].indirect(west_sb[:, entries(cells)]), ACT.Sigmoid)
-                terms = (e_tanh[t][:, cells], e_tanh[t][:, cells], made[t][:, cells], e_east, e_west)
+                reaction = [made[t][:, cells]] if t else 3 * [y[t][:, cells]] + 2 * [y_local[t][:, cells]]
+                terms = 2 * [e_tanh[t][:, cells]] + reaction + [e_east, e_west]
                 for n, term in enumerate(terms):
                     for b, cb in enumerate(range(cells.start // P, cells.stop // P)):
                         nc.tensor.matmul(
@@ -224,17 +221,8 @@ def tile_picked_grayscott_none_p_kernel(
             nc.scalar.copy(z2_words[:].rearrange("p (r c) u -> p r c u", r=2), back[:].rearrange("p r u c -> p r c u"))
             return z2_words[:].rearrange("p c u -> p (c u)").bitcast(BF16)
 
-        def weave(name, planes, width, copy):
-            grouped = sb(name, [P, width, PACK], BF16)
-            copy(
-                grouped[:].rearrange("p (c i) t -> p c t i", i=4),
-                planes[:].rearrange("p t (c i) -> p c t i", i=4),
-            )
-            return grouped[:].rearrange("p c t -> p (c t)")
-
         out_rows = out.rearrange("(mo p) c -> p mo c", p=P)
         z_grp = {}
-        z_planes = {}
         y_west = {}
         z_q = {}
 
@@ -248,19 +236,27 @@ def tile_picked_grayscott_none_p_kernel(
                     y_west[t][:, half], y_window[t][:].indirect(west_sb[:, entries(half)]), y_local[t][:, half], ALU.subtract
                 )
 
-        def east_step(n, t, dest, tag=None):
+        y_sum = {}
+
+        def east_steps(n, planes, tag=None):
             cells = chunk_cells(n)
-            y_sum = sb("y_sum%d_%d" % (n, t), [P, CHUNKS[n][1]], F32, tag=tag)
-            nc.vector.tensor_tensor(y_sum[:], y_window[t][:].indirect(east_sb[:, entries(cells)]), y_west[t][:, cells], ALU.add)
-            nc.scalar.activation(dest, y_sum[:], ACT.Identity, bias=g1_eighth[:, t : t + 1], scale=g1_quarter[:, t : t + 1])
+            if n not in y_sum:
+                y_sum[n] = sb("y_sum%d" % n, [P, PACK, CHUNKS[n][1]], F32, tag=tag)
+            for t in planes:
+                nc.vector.tensor_tensor(y_sum[n][:, t, :], y_window[t][:].indirect(east_sb[:, entries(cells)]), y_west[t][:, cells], ALU.add)
 
-        def gather_y(n):
-            z_planes[n] = sb("z_planes%d" % n, [P, PACK, CHUNKS[n][1]], BF16)
-            for t in range(PACK):
-                east_step(n, t, z_planes[n][:, t, :])
-
-        def weave_z(n, copy):
-            z_grp[n] = weave("z_grp%d" % n, z_planes[n], CHUNKS[n][1], copy)
+        def weave_z(n):
+            width = CHUNKS[n][1]
+            grouped = sb("z_grp%d" % n, [P, width, PACK], BF16)
+            nc.vector.scalar_tensor_tensor(
+                grouped[:],
+                y_sum[n][:].rearrange("p t c -> p c t"),
+                0.5,
+                g1_quarter[:].unsqueeze(1).to_broadcast([P, width, PACK]),
+                ALU.add,
+                ALU.mult,
+            )
+            z_grp[n] = grouped[:].rearrange("p c t -> p (c t)")
 
         def quantise_z(n):
             z_q[n] = quantise("z_chunk%d" % n, z_grp[n], CHUNKS[n][1])
@@ -282,21 +278,6 @@ def tile_picked_grayscott_none_p_kernel(
                 stop=stop,
             )
 
-        def open_product(n, term, bank0):
-            banks = [bank_tile("acc%d_%d" % (n, mo), [P, CHUNKS[n][1]], bank0 + mo) for mo in range(PACK)]
-            for mo in range(PACK):
-                out_pass(banks[mo][:], mo, n, term, True, False)
-            return banks
-
-        def close_product(n, term, banks, copies):
-            c0, width = CHUNKS[n]
-            result = sb("result%d" % n, [P, PACK, width], F32)
-            for mo in range(PACK):
-                out_pass(banks[mo][:], mo, n, term, False, True)
-                copies[mo % 2](result[:, mo, :], banks[mo][:])
-                if mo % 2:
-                    nc.sync.dma_start(out=out_rows[:, mo - 1 : mo + 1, c0 : c0 + width], in_=result[:, mo - 1 : mo + 1, :])
-
         def open_middle(n):
             bank = bank_tile("acc%d" % n, [P, PACK, CHUNKS[n][1]], 5)
             for mo in range(PACK):
@@ -311,17 +292,17 @@ def tile_picked_grayscott_none_p_kernel(
             nc.scalar.copy(result[:], bank[:])
             nc.sync.dma_start(out=out_rows[:, :, c0 : c0 + width], in_=result[:])
 
-        def open_last(n):
-            banks = [bank_tile("acc%d_%d" % (n, half), [P, 2, CHUNKS[n][1]], tag) for half, tag in enumerate((4, 7))]
+        def open_pairs(n, term, tags):
+            banks = [bank_tile("acc%d_%d" % (n, half), [P, 2, CHUNKS[n][1]], tag) for half, tag in enumerate(tags)]
             for mo in range(PACK):
-                out_pass(banks[mo // 2][:, mo % 2, :], mo, n, "z2", mo % 2 == 0, False)
+                out_pass(banks[mo // 2][:, mo % 2, :], mo, n, term, mo % 2 == 0, False)
             return banks
 
-        def close_last(n, banks):
+        def close_pairs(n, term, banks, copies):
             c0, width = CHUNKS[n]
-            for half, copy in enumerate((nc.scalar.copy, nc.vector.tensor_copy)):
+            for half, copy in enumerate(copies):
                 for mo in (2 * half, 2 * half + 1):
-                    out_pass(banks[half][:, mo % 2, :], mo, n, "z", False, mo % 2 == 1)
+                    out_pass(banks[half][:, mo % 2, :], mo, n, term, False, mo % 2 == 1)
                 result = sb("result%d_%d" % (n, half), [P, 2, width], F32)
                 copy(result[:], banks[half][:])
                 nc.sync.dma_start(out=out_rows[:, 2 * half : 2 * half + 2, c0 : c0 + width], in_=result[:])
@@ -331,33 +312,26 @@ def tile_picked_grayscott_none_p_kernel(
             west_step(t)
         for half in halves:
             sum_z2(half, (2, 3))
-        planes0 = z_planes[0] = sb("z_planes0", [P, PACK, CHUNKS[0][1]], BF16)
-        planes1 = z_planes[1] = sb("z_planes1", [P, PACK, CHUNKS[1][1]], BF16)
-        east_step(0, 0, planes0[:, 0, :])
+        east_steps(0, range(PACK))
         z2_grp0 = finish_z2(0)
-        east_step(0, 1, planes0[:, 1, :], "e_west3_0")
-        east_step(0, 2, planes0[:, 2, :], "z2_t0")
-        east_step(0, 3, planes0[:, 3, :], "z2_t1")
-        weave_z(0, nc.scalar.copy)
+        weave_z(0)
         z2_grp1 = finish_z2(1)
-        late["z2", 0] = quantise("z2_0", z2_grp0, 2 * P)
-        east_step(1, 0, planes1[:, 0, :], "e_west3_256")
+        for half in halves:
+            round_rows(w3_grp, w3_raw, half, nc.scalar.copy)
+        round_rows(w4_grp, w4_raw, halves[1], nc.scalar.copy)
         quantise_z(0)
-        close_product(0, "z", open_product(0, "z2", 0), (nc.scalar.copy, nc.scalar.copy))
-        east_step(1, 1, planes1[:, 1, :], "g2_eighth")
-        east_step(1, 2, planes1[:, 2, :], "z2_t2")
-        east_step(1, 3, planes1[:, 3, :], "z2_t3")
+        east_steps(1, range(PACK), "e_west3_256")
+        late["w3"] = quantise("w3", w3_grp[:].rearrange("p n j -> p (n j)"), N, tag="z2_t1")
+        late["w4"] = quantise("w4", w4_grp[:].rearrange("p n j -> p (n j)"), N, tag="z2_t2")
+        late["z2", 0] = quantise("z2_0", z2_grp0, 2 * P)
+        close_pairs(0, "z2", open_pairs(0, "z", (0, 1)), (nc.scalar.copy, nc.scalar.copy))
+        weave_z(1)
         late["z2", 1] = quantise("z2_1", z2_grp1, 2 * P)
         middle_bank = open_middle(1)
-        last_banks = open_last(2)
-        last = sb("z_grp2", [P, CHUNKS[2][1], PACK], BF16)
-        east_step(2, 0, last[:, :, 0], "z_grp0")
-        east_step(2, 1, last[:, :, 1], "g2_eighth")
-        weave_z(1, nc.vector.tensor_copy)
-        east_step(2, 2, last[:, :, 2], "z2_words1")
+        last_banks = open_pairs(2, "z2", (2, 3))
+        east_steps(2, range(PACK), "z2_t3")
         quantise_z(1)
-        east_step(2, 3, last[:, :, 3], "z_planes1")
-        z_grp[2] = last[:].rearrange("p c t -> p (c t)")
         close_middle(1, middle_bank)
+        weave_z(2)
         quantise_z(2)
-        close_last(2, last_banks)
+        close_pairs(2, "z", last_banks, (nc.scalar.copy, nc.vector.tensor_copy))

@@ -54,6 +54,12 @@ def tile_picked_grayscott_none_p_kernel(
             nc.sync.dma_start(out=raw[:], in_=w.rearrange("(p j) c -> p j c", j=PACK))
             return raw
 
+        def load_weight_halves(name, w):
+            raw = [sb("%s%d" % (name, h), [P, PACK, 256], F32) for h in range(2)]
+            for h in range(2):
+                nc.sync.dma_start(out=raw[h][:], in_=w.rearrange("(p j) c -> p j c", j=PACK)[:, :, 256 * h : 256 * (h + 1)])
+            return raw
+
         def load_gain(name, g):
             col = sb(name, [P, PACK], F32)
             nc.sync.dma_start(out=col[:], in_=g.rearrange("(p t) o -> p (t o)", t=PACK))
@@ -65,12 +71,10 @@ def tile_picked_grayscott_none_p_kernel(
         g1_sb = load_gain("g1_sb", g1)
         x_word_tab = sb("x_word_tab", [P, T], I32)
         nc.sync.dma_start(out=x_word_tab[:], in_=x_words[0].rearrange("p n t -> p (n t)").bitcast(I32))
-        w2_raw = [sb("w2_raw%d" % h, [P, PACK, H // 2], F32) for h in range(2)]
-        for h in range(2):
-            nc.sync.dma_start(out=w2_raw[h][:], in_=w2.rearrange("(p j) c -> p j c", j=PACK)[:, :, h * H // 2 : (h + 1) * H // 2])
+        w2_raw = load_weight_halves("w2_raw", w2)
+        w4_raw = load_weight_halves("w4_raw", w4)
         nc.sync.dma_start(west_sb[:], west)
         nc.sync.dma_start(east_sb[:], east)
-        w4_raw = load_weight("w4_raw", w4)
         w3_raw = load_weight("w3_raw", w3)
 
         ident = sb("ident", [P, P], F32)
@@ -123,11 +127,8 @@ def tile_picked_grayscott_none_p_kernel(
             )
             return bank
 
-        def round_rows(grouped, raw, cols, copy):
-            copy(
-                grouped[:, cols, :].rearrange("p (c i) j -> p c j i", i=4),
-                raw[:, :, cols].rearrange("p j (c i) -> p c j i", i=4),
-            )
+        def round_rows(grouped, raw, copy):
+            copy(grouped.rearrange("p (c i) j -> p c j i", i=4), raw.rearrange("p j (c i) -> p c j i", i=4))
 
         def entries(cells):
             return slice(cells.start // 16, cells.stop // 16)
@@ -168,18 +169,31 @@ def tile_picked_grayscott_none_p_kernel(
         w3_grp = sb("w3_grp", [P, N, PACK], BF16)
         w4_grp = sb("w4_grp", [P, N, PACK], BF16)
         e_bank = [first_product(t, t, *w2_q[t // 2]) for t in range(PACK)]
+        z2_sum = [bank_tile("z2_sum%d" % cb, [P, PACK, P], 4 + cb) for cb in range(4)]
+
+        def add_to_z2(t, cells, term, start=False, stop=False):
+            for b, cb in enumerate(range(cells.start // P, cells.stop // P)):
+                nc.tensor.matmul(
+                    z2_sum[cb][:, t, :], lhsT=term[:, b * P : (b + 1) * P], rhs=ident[:], is_transpose=True, start=start, stop=stop
+                )
+
         for t in range(PACK):
             nc.scalar.activation(e_tanh[t], e_bank[t][:], ACT.Tanh, scale=0.5)
             nc.scalar.activation(q[t], e_tanh[t], ACT.Square, bias=1.0)
             if t == 0:
-                round_rows(w4_grp, w4_raw, halves[0], nc.vector.tensor_copy)
+                for h, half in enumerate(halves):
+                    round_rows(w4_grp[:, half, :], w4_raw[h][:], nc.vector.tensor_copy)
             nc.vector.scalar_tensor_tensor(y_local[t][:], q[t], 1.5, y[t], ALU.subtract, ALU.mult)
-            if t:
+            if t == 0:
+                late["w4"] = quantise("w4", w4_grp[:].rearrange("p n j -> p (n j)"), N)
+            else:
                 nc.vector.scalar_tensor_tensor(made[t][:], q[t], 2.0, y[t], ALU.mult, ALU.mult)
+            reaction = [made[t][:]] if t else 3 * [y[t]] + 2 * [y_local[t][:]]
+            for n, term in enumerate(2 * [e_tanh[t]] + reaction):
+                add_to_z2(t, slice(0, S), term, start=t == 0 and n == 0)
 
-        z2_sum = [bank_tile("z2_sum%d" % cb, [P, PACK, P], 4 + cb) for cb in range(4)]
 
-        def sum_z2(cells, planes):
+        def gather_e(cells, planes):
             for t in planes:
                 if cells.start == 0:
                     nc.scalar.copy(e_pre[t], e_bank[t][:])
@@ -188,18 +202,8 @@ def tile_picked_grayscott_none_p_kernel(
                 e_west = sb("e_west%d_%d" % (t, cells.start), [P, width], F32)
                 nc.scalar.activation(e_east[:], e_window[t][:].indirect(east_sb[:, entries(cells)]), ACT.Sigmoid)
                 nc.scalar.activation(e_west[:], e_window[t][:].indirect(west_sb[:, entries(cells)]), ACT.Sigmoid)
-                reaction = [made[t][:, cells]] if t else 3 * [y[t][:, cells]] + 2 * [y_local[t][:, cells]]
-                terms = 2 * [e_tanh[t][:, cells]] + reaction + [e_east, e_west]
-                for n, term in enumerate(terms):
-                    for b, cb in enumerate(range(cells.start // P, cells.stop // P)):
-                        nc.tensor.matmul(
-                            z2_sum[cb][:, t, :],
-                            lhsT=term[:, b * P : (b + 1) * P],
-                            rhs=ident[:],
-                            is_transpose=True,
-                            start=n == 0,
-                            stop=n == len(terms) - 1,
-                        )
+                add_to_z2(t, cells, e_east)
+                add_to_z2(t, cells, e_west, stop=t == PACK - 1)
 
         def finish_z2(pair):
             z2_words = sb("z2_words%d" % pair, [P, 2 * P, 2], F32)
@@ -307,22 +311,20 @@ def tile_picked_grayscott_none_p_kernel(
                 copy(result[:], banks[half][:])
                 nc.sync.dma_start(out=out_rows[:, 2 * half : 2 * half + 2, c0 : c0 + width], in_=result[:])
 
-        sum_z2(slice(0, S), (0, 1))
+        gather_e(slice(0, S), (0, 1))
         for t in range(PACK):
             west_step(t)
         for half in halves:
-            sum_z2(half, (2, 3))
+            gather_e(half, (2, 3))
         east_steps(0, range(PACK))
         z2_grp0 = finish_z2(0)
         weave_z(0)
         z2_grp1 = finish_z2(1)
         for half in halves:
-            round_rows(w3_grp, w3_raw, half, nc.scalar.copy)
-        round_rows(w4_grp, w4_raw, halves[1], nc.scalar.copy)
+            round_rows(w3_grp[:, half, :], w3_raw[:, :, half], nc.scalar.copy)
         quantise_z(0)
         east_steps(1, range(PACK), "e_west3_256")
         late["w3"] = quantise("w3", w3_grp[:].rearrange("p n j -> p (n j)"), N, tag="z2_t1")
-        late["w4"] = quantise("w4", w4_grp[:].rearrange("p n j -> p (n j)"), N, tag="z2_t2")
         late["z2", 0] = quantise("z2_0", z2_grp0, 2 * P)
         close_pairs(0, "z2", open_pairs(0, "z", (0, 1)), (nc.scalar.copy, nc.scalar.copy))
         weave_z(1)

@@ -95,6 +95,7 @@ def tile_picked_grayscott_none_p_kernel(
         g2_eighth = sb("g2_eighth", [P, H], F32)
         nc.scalar.copy(g2_eighth[:].rearrange("c (p t) -> c p t", t=PACK), spread[:].rearrange("c t p -> c p t"))
         g1_quarter = scaled("g1_quarter", g1_sb, 0.25)
+        g1_eighth = scaled("g1_eighth", g1_sb, 0.125)
 
         x_scale = sb("x_scale", [P, S], U8)
         nc.vector.tensor_copy(x_scale[:], x_scale_tab[:].indirect(offs_sb[:]))
@@ -181,11 +182,12 @@ def tile_picked_grayscott_none_p_kernel(
             nc.scalar.activation(e_tanh[t], e_bank[t][:], ACT.Tanh, scale=0.5)
             nc.scalar.activation(q[t], e_tanh[t], ACT.Square, bias=1.0)
             if t == 0:
-                for h, half in enumerate(halves):
-                    round_rows(w4_grp[:, half, :], w4_raw[h][:], nc.vector.tensor_copy)
+                round_rows(w4_grp[:, halves[0], :], w4_raw[0][:], nc.vector.tensor_copy)
+                w4_q = [quantise("w4_0", w4_grp[:, halves[0], :].rearrange("p n j -> p (n j)"), N // 2)]
+                round_rows(w4_grp[:, halves[1], :], w4_raw[1][:], nc.vector.tensor_copy)
             nc.vector.scalar_tensor_tensor(y_local[t][:], q[t], 1.5, y[t], ALU.subtract, ALU.mult)
             if t == 0:
-                late["w4"] = quantise("w4", w4_grp[:].rearrange("p n j -> p (n j)"), N)
+                w4_q.append(quantise("w4_1", w4_grp[:, halves[1], :].rearrange("p n j -> p (n j)"), N // 2))
             else:
                 nc.vector.scalar_tensor_tensor(made[t][:], q[t], 2.0, y[t], ALU.mult, ALU.mult)
             reaction = [made[t][:]] if t else 3 * [y[t]] + 2 * [y_local[t][:]]
@@ -262,16 +264,28 @@ def tile_picked_grayscott_none_p_kernel(
             )
             z_grp[n] = grouped[:].rearrange("p c t -> p (c t)")
 
-        def quantise_z(n):
-            z_q[n] = quantise("z_chunk%d" % n, z_grp[n], CHUNKS[n][1])
+        def weave_z_on_scalar(n):
+            width = CHUNKS[n][1]
+            planes = sb("z_planes%d" % n, [P, PACK, width], BF16)
+            for t in range(PACK):
+                nc.scalar.activation(
+                    planes[:, t, :], y_sum[n][:, t, :], ACT.Identity, bias=g1_eighth[:, t : t + 1], scale=g1_quarter[:, t : t + 1]
+                )
+            grouped = sb("z_grp%d" % n, [P, width, PACK], BF16)
+            nc.scalar.copy(grouped[:].rearrange("p (c i) t -> p c t i", i=4), planes[:].rearrange("p t (c i) -> p c t i", i=4))
+            z_grp[n] = grouped[:].rearrange("p c t -> p (c t)")
+
+        def quantise_z(n, tag=None):
+            z_q[n] = quantise("z_chunk%d" % n, z_grp[n], CHUNKS[n][1], tag=tag)
 
         def out_pass(acc, mo, n, term, start, stop):
             c0, width = CHUNKS[n]
             if term == "z":
                 w_q, act_q, cells = late["w3"], z_q[n], slice(0, width)
             else:
-                w_q, act_q, cells = late["w4"], late["z2", c0 // 256], slice(c0 % 256, c0 % 256 + width)
-            cols = slice(mo * P, (mo + 1) * P)
+                w_q, act_q, cells = w4_q[mo // 2], late["z2", c0 // 256], slice(c0 % 256, c0 % 256 + width)
+            first = mo * P if term == "z" else mo % 2 * P
+            cols = slice(first, first + P)
             nc.tensor.matmul_mx(
                 out=acc,
                 lhsT=w_q[0][:, cols].bitcast(FP8X4),
@@ -302,38 +316,40 @@ def tile_picked_grayscott_none_p_kernel(
                 out_pass(banks[mo // 2][:, mo % 2, :], mo, n, term, mo % 2 == 0, False)
             return banks
 
-        def close_pairs(n, term, banks, copies):
+        def close_pairs(n, term, banks, copies, queues):
             c0, width = CHUNKS[n]
             for half, copy in enumerate(copies):
                 for mo in (2 * half, 2 * half + 1):
                     out_pass(banks[half][:, mo % 2, :], mo, n, term, False, mo % 2 == 1)
                 result = sb("result%d_%d" % (n, half), [P, 2, width], F32)
                 copy(result[:], banks[half][:])
-                nc.sync.dma_start(out=out_rows[:, 2 * half : 2 * half + 2, c0 : c0 + width], in_=result[:])
+                queues[half].dma_start(out=out_rows[:, 2 * half : 2 * half + 2, c0 : c0 + width], in_=result[:])
 
         gather_e(slice(0, S), (0, 1))
-        for t in range(PACK):
+        round_rows(w3_grp[:], w3_raw[:], nc.vector.tensor_copy)
+        west_step(0)
+        late["w3"] = quantise("w3", w3_grp[:].rearrange("p n j -> p (n j)"), N)
+        for t in range(1, PACK):
             west_step(t)
         for half in halves:
             gather_e(half, (2, 3))
         east_steps(0, range(PACK))
+        weave_z_on_scalar(0)
         z2_grp0 = finish_z2(0)
-        weave_z(0)
+        east_steps(1, range(PACK), "e_west3_0")
         z2_grp1 = finish_z2(1)
-        for half in halves:
-            round_rows(w3_grp[:, half, :], w3_raw[:, :, half], nc.scalar.copy)
-        quantise_z(0)
-        east_steps(1, range(PACK), "e_west3_256")
-        late["w3"] = quantise("w3", w3_grp[:].rearrange("p n j -> p (n j)"), N, tag="z2_t1")
-        late["z2", 0] = quantise("z2_0", z2_grp0, 2 * P)
-        close_pairs(0, "z2", open_pairs(0, "z", (0, 1)), (nc.scalar.copy, nc.scalar.copy))
         weave_z(1)
+        late["z2", 0] = quantise("z2_0", z2_grp0, 2 * P, tag="e_west3_256")
+        first_banks = open_pairs(0, "z2", (0, 1))
+        quantise_z(1)
+        quantise_z(0, "z2_t2")
+        close_pairs(0, "z", first_banks, (nc.scalar.copy, nc.scalar.copy), (nc.sync, nc.sync))
+        east_steps(2, (0, 1), "z2_t3")
         late["z2", 1] = quantise("z2_1", z2_grp1, 2 * P)
         middle_bank = open_middle(1)
-        last_banks = open_pairs(2, "z2", (2, 3))
-        east_steps(2, range(PACK), "z2_t3")
-        quantise_z(1)
         close_middle(1, middle_bank)
+        last_banks = open_pairs(2, "z2", (2, 3))
+        east_steps(2, (2, 3))
         weave_z(2)
         quantise_z(2)
-        close_pairs(2, "z", last_banks, (nc.scalar.copy, nc.vector.tensor_copy))
+        close_pairs(2, "z", last_banks, (nc.scalar.copy, nc.vector.tensor_copy), (nc.scalar, nc.sync))

@@ -18,8 +18,23 @@ ALU = mybir.AluOpType
 
 P = 128
 PACK = 4
+LINE = 4
 LIST_COLS = S // 16
-CHUNKS = ((0, 256), (256, 128), (384, 128))
+HALF = S // 2
+HALVES = (slice(0, HALF), slice(HALF, S))
+CHUNKS = (slice(0, HALF), slice(HALF, HALF + P), slice(HALF + P, S))
+
+
+def width_of(cells):
+    return cells.stop - cells.start
+
+
+def entries(cells):
+    return slice(cells.start // 16, cells.stop // 16)
+
+
+def slot(t):
+    return 2 * (t % 2) + t // 2
 
 
 def tile_picked_grayscott_none_p_kernel(
@@ -31,11 +46,11 @@ def tile_picked_grayscott_none_p_kernel(
         keep = ctx.enter_context(tc.tile_pool(name="keep", bufs=1))
         psum = ctx.enter_context(tc.psum_pool(name="psum", bufs=1))
 
-        seen = {}
+        def sb(name, shape, dtype, reuse=None):
+            return keep.tile(shape, dtype, name=name, tag=reuse or name, align_bytes=64)
 
-        def sb(name, shape, dtype, tag=None):
-            seen[name] = keep.tile(shape, dtype, name=name, tag=tag or name, align_bytes=64)
-            return seen[name]
+        def bank_tile(name, shape, bank):
+            return psum.tile(shape, F32, name=name, tag="bank%d" % bank)
 
         offs_sb = lists.tile([P, LIST_COLS], U16, name="offs_sb")
         west_sb = lists.tile([P, LIST_COLS], U16, name="west_sb")
@@ -49,15 +64,9 @@ def tile_picked_grayscott_none_p_kernel(
                 in_=x_scales[0, 4 * quad : 4 * quad + 4, :].bitcast(I32),
             )
 
-        def load_weight(name, w):
-            raw = sb(name, [P, PACK, 512], F32)
-            nc.sync.dma_start(out=raw[:], in_=w.rearrange("(p j) c -> p j c", j=PACK))
-            return raw
-
-        def load_weight_halves(name, w):
-            raw = [sb("%s%d" % (name, h), [P, PACK, 256], F32) for h in range(2)]
-            for h in range(2):
-                nc.sync.dma_start(out=raw[h][:], in_=w.rearrange("(p j) c -> p j c", j=PACK)[:, :, 256 * h : 256 * (h + 1)])
+        def load_weight(name, w, cols):
+            raw = sb(name, [P, PACK, width_of(cols)], F32)
+            nc.sync.dma_start(out=raw[:], in_=w.rearrange("(p j) c -> p j c", j=PACK)[:, :, cols])
             return raw
 
         def load_gain(name, g):
@@ -66,290 +75,252 @@ def tile_picked_grayscott_none_p_kernel(
             return col
 
         nc.sync.dma_start(offs_sb[:], offs)
-        w1_raw = load_weight("w1_raw", w1)
+        w1_raw = load_weight("w1_raw", w1, slice(0, H))
         g2_sb = load_gain("g2_sb", g2)
         g1_sb = load_gain("g1_sb", g1)
         x_word_tab = sb("x_word_tab", [P, T], I32)
         nc.sync.dma_start(out=x_word_tab[:], in_=x_words[0].rearrange("p n t -> p (n t)").bitcast(I32))
-        w2_raw = load_weight_halves("w2_raw", w2)
-        w4_raw = load_weight_halves("w4_raw", w4)
+        w2_raw = [load_weight("w2_raw%d" % h, w2, cols) for h, cols in enumerate(HALVES)]
+        w4_raw = [load_weight("w4_raw%d" % h, w4, cols) for h, cols in enumerate(HALVES)]
         nc.sync.dma_start(west_sb[:], west)
         nc.sync.dma_start(east_sb[:], east)
-        w3_raw = load_weight("w3_raw", w3)
+        w3_raw = load_weight("w3_raw", w3, slice(0, N))
 
         ident = sb("ident", [P, P], F32)
         make_identity(nc, ident[:])
-
-        def bank_tile(name, shape, tag):
-            return psum.tile(shape, F32, name=name, tag="bank%d" % tag)
 
         def scaled(name, g, factor):
             res = sb(name, [P, PACK], F32)
             nc.gpsimd.tensor_scalar(res[:], g[:], factor, 0.0, ALU.mult, ALU.add)
             return res
 
-        g2_col = scaled("g2_col", g2_sb, 0.125)
+        g2_eighth = scaled("g2_eighth", g2_sb, 0.125)
         spread = bank_tile("spread", [P, PACK, P], 2)
         for t in range(PACK):
-            nc.tensor.transpose(spread[:, t, :], g2_col[:, t : t + 1].to_broadcast([P, P]), ident[:])
-        g2_eighth = sb("g2_eighth", [P, H], F32)
-        nc.scalar.copy(g2_eighth[:].rearrange("c (p t) -> c p t", t=PACK), spread[:].rearrange("c t p -> c p t"))
+            nc.tensor.transpose(spread[:, slot(t), :], g2_eighth[:, t : t + 1].to_broadcast([P, P]), ident[:])
+        g2_row = sb("g2_row", [P, H], F32)
+        nc.scalar.copy(g2_row[:].rearrange("c (w i) -> c w i", i=2), spread[:].rearrange("c (i u) p -> c (u p) i", i=2))
         g1_quarter = scaled("g1_quarter", g1_sb, 0.25)
         g1_eighth = scaled("g1_eighth", g1_sb, 0.125)
 
         x_scale = sb("x_scale", [P, S], U8)
         nc.vector.tensor_copy(x_scale[:], x_scale_tab[:].indirect(offs_sb[:]))
 
-        def quantise(name, grouped, width, tag=None):
-            code = sb(name + "_code", [P, width], U32, tag=tag)
-            scale = sb(name + "_scale", [P, width], U8)
-            nc.vector.quantize_mx(out=code[:].bitcast(FP8X4), scales=scale[:], in_=grouped)
+        def quantise(name, woven, reuse=None):
+            columns = woven.shape[1] // PACK
+            code = sb(name + "_code", [P, columns], U32, reuse=reuse)
+            scale = sb(name + "_scale", [P, columns], U8)
+            nc.vector.quantize_mx(out=code[:].bitcast(FP8X4), scales=scale[:], in_=woven)
             return code, scale
 
+        def mx_pass(acc, weights, cols, values, cells, start, stop):
+            nc.tensor.matmul_mx(
+                out=acc,
+                lhsT=weights[0][:, cols].bitcast(FP8X4),
+                lhsT_scale=weights[1][:, cols],
+                rhs=values[0][:, cells].bitcast(FP8X4),
+                rhs_scale=values[1][:, cells],
+                start=start,
+                stop=stop,
+            )
+
         def round_plane_pair(name, raw, u, copy):
-            grouped = sb(name, [P, 2, P, PACK], BF16)
+            woven = sb(name, [P, 2, P, PACK], BF16)
             copy(
-                grouped[:].rearrange("p t m j -> p m t j"),
+                woven[:].rearrange("p t m j -> p m t j"),
                 raw[:].rearrange("p j (m t) -> p m t j", t=PACK)[:, :, 2 * u : 2 * u + 2, :],
             )
-            return grouped[:].rearrange("p t m j -> p (t m j)")
+            return woven[:].rearrange("p t m j -> p (t m j)")
 
-        def first_product(t, tag, code, scale, cells=slice(0, S)):
-            bank = bank_tile("pre", [P, cells.stop - cells.start], tag)
-            cols = slice((t % 2) * P, (t % 2 + 1) * P)
-            nc.tensor.matmul_mx(
-                out=bank[:],
-                lhsT=code[:, cols].bitcast(FP8X4),
-                lhsT_scale=scale[:, cols],
-                rhs=x_code[:, cells].bitcast(FP8X4),
-                rhs_scale=x_scale[:, cells],
-                start=True,
-                stop=True,
-            )
-            return bank
+        def first_product(t, bank, pairs, cells=slice(0, S)):
+            acc = bank_tile("pre", [P, width_of(cells)], bank)
+            mx_pass(acc[:], pairs[t // 2], slice(t % 2 * P, (t % 2 + 1) * P), (x_code, x_scale), cells, True, True)
+            return acc
 
-        def round_rows(grouped, raw, copy):
-            copy(grouped.rearrange("p (c i) j -> p c j i", i=4), raw.rearrange("p j (c i) -> p c j i", i=4))
+        def weave(dest, src, copy):
+            copy(dest.rearrange("p (c i) j -> p c j i", i=LINE), src.rearrange("p j (c i) -> p c j i", i=LINE))
 
-        def entries(cells):
-            return slice(cells.start // 16, cells.stop // 16)
-
-        halves = (slice(0, S // 2), slice(S // 2, S))
-
-        w1_grp = [round_plane_pair("w1_grp0", w1_raw, 0, nc.vector.tensor_copy), round_plane_pair("w1_grp1", w1_raw, 1, nc.scalar.copy)]
-        w1_q = [quantise("w1_%d" % u, w1_grp[u], 2 * P) for u in range(2)]
+        w1_woven = [
+            round_plane_pair("w1_woven%d" % u, w1_raw, u, copy) for u, copy in enumerate((nc.vector.tensor_copy, nc.scalar.copy))
+        ]
+        w1_q = [quantise("w1_%d" % u, w1_woven[u]) for u in range(2)]
         x_code = sb("x_code", [P, S], U32)
-        for half in halves:
+        for half in HALVES:
             nc.vector.tensor_copy(x_code[:, half], x_word_tab[:].bitcast(U32).indirect(offs_sb[:, entries(half)]))
 
         e_window = [sb("e_window%d" % t, [P, 2 * S], F32) for t in range(PACK)]
         e_pre = [window[:, :S] for window in e_window]
-        e_tanh = [window[:, S:] for window in e_window]
-        y_window = [sb("y_window%d" % t, [P, S], F32) for t in range(PACK)]
-        y = [window[:] for window in y_window]
-        q_tiles = [sb("q%d" % t, [P, S], F32) for t in range(PACK)]
-        q = [tile[:] for tile in q_tiles]
+        tanh_e = [window[:, S:] for window in e_window]
+        y = [sb("y%d" % t, [P, S], F32) for t in range(PACK)]
+        q = [sb("q%d" % t, [P, S], F32) for t in range(PACK)]
         y_local = [sb("y_local%d" % t, [P, S], F32) for t in range(PACK)]
         made = {t: sb("made%d" % t, [P, S], F32) for t in range(1, PACK)}
 
-        for tag, half in zip((4, 3), halves):
-            bank = first_product(0, tag, *w1_q[0], cells=half)
-            nc.scalar.activation(y[0][:, half], bank[:], ACT.Sigmoid)
+        for bank, half in zip((4, 3), HALVES):
+            nc.scalar.activation(y[0][:, half], first_product(0, bank, w1_q, cells=half)[:], ACT.Sigmoid)
         for t in range(1, PACK):
-            bank = first_product(t, 4 + t, *w1_q[t // 2])
-            nc.scalar.activation(y[t], bank[:], ACT.Sigmoid)
+            nc.scalar.activation(y[t][:], first_product(t, 4 + t, w1_q)[:], ACT.Sigmoid)
 
-        w2_grp = sb("w2_grp", [P, PACK, P, PACK], BF16)
+        w2_woven = sb("w2_woven", [P, PACK, P, PACK], BF16)
         for h in range(2):
             nc.vector.tensor_copy(
-                w2_grp[:].rearrange("p t m j -> p m t j")[:, h * P // 2 : (h + 1) * P // 2],
+                w2_woven[:].rearrange("p t m j -> p m t j")[:, h * P // 2 : (h + 1) * P // 2],
                 w2_raw[h][:].rearrange("p j (m t) -> p m t j", t=PACK),
             )
-        w2_q = [quantise("w2_%d" % u, w2_grp[:, 2 * u : 2 * u + 2].rearrange("p t m j -> p (t m j)"), 2 * P) for u in range(2)]
-        late = {}
-        w3_grp = sb("w3_grp", [P, N, PACK], BF16)
-        w4_grp = sb("w4_grp", [P, N, PACK], BF16)
-        e_bank = [first_product(t, t, *w2_q[t // 2]) for t in range(PACK)]
-        z2_sum = [bank_tile("z2_sum%d" % cb, [P, PACK, P], 4 + cb) for cb in range(4)]
+        w2_q = [quantise("w2_%d" % u, w2_woven[:, 2 * u : 2 * u + 2].rearrange("p t m j -> p (t m j)")) for u in range(2)]
+        w3_woven = sb("w3_woven", [P, N, PACK], BF16)
+        w4_woven = sb("w4_woven", [P, N, PACK], BF16)
+        e_acc = [first_product(t, t, w2_q) for t in range(PACK)]
+
+        z2_sum = [bank_tile("z2_sum%d" % b, [P, PACK, P], 4 + b) for b in range(S // P)]
 
         def add_to_z2(t, cells, term, start=False, stop=False):
-            for b, cb in enumerate(range(cells.start // P, cells.stop // P)):
+            for n, b in enumerate(range(cells.start // P, cells.stop // P)):
                 nc.tensor.matmul(
-                    z2_sum[cb][:, t, :], lhsT=term[:, b * P : (b + 1) * P], rhs=ident[:], is_transpose=True, start=start, stop=stop
+                    z2_sum[b][:, slot(t), :], lhsT=term[:, n * P : (n + 1) * P], rhs=ident[:], is_transpose=True, start=start, stop=stop
                 )
 
-        for t in range(PACK):
-            nc.scalar.activation(e_tanh[t], e_bank[t][:], ACT.Tanh, scale=0.5)
-            nc.scalar.activation(q[t], e_tanh[t], ACT.Square, bias=1.0)
-            if t == 0:
-                round_rows(w4_grp[:, halves[0], :], w4_raw[0][:], nc.vector.tensor_copy)
-                w4_q = [quantise("w4_0", w4_grp[:, halves[0], :].rearrange("p n j -> p (n j)"), N // 2)]
-                round_rows(w4_grp[:, halves[1], :], w4_raw[1][:], nc.vector.tensor_copy)
-            nc.vector.scalar_tensor_tensor(y_local[t][:], q[t], 1.5, y[t], ALU.subtract, ALU.mult)
-            if t == 0:
-                w4_q.append(quantise("w4_1", w4_grp[:, halves[1], :].rearrange("p n j -> p (n j)"), N // 2))
-            else:
-                nc.vector.scalar_tensor_tensor(made[t][:], q[t], 2.0, y[t], ALU.mult, ALU.mult)
-            reaction = [made[t][:]] if t else 3 * [y[t]] + 2 * [y_local[t][:]]
-            for n, term in enumerate(2 * [e_tanh[t]] + reaction):
-                add_to_z2(t, slice(0, S), term, start=t == 0 and n == 0)
+        def quantise_w4(h):
+            return quantise("w4_%d" % h, w4_woven[:, HALVES[h], :].rearrange("p n j -> p (n j)"))
 
+        for t in range(PACK):
+            nc.scalar.activation(tanh_e[t], e_acc[t][:], ACT.Tanh, scale=0.5)
+            nc.scalar.activation(q[t][:], tanh_e[t], ACT.Square, bias=1.0)
+            if t == 0:
+                weave(w4_woven[:, HALVES[0], :], w4_raw[0][:], nc.vector.tensor_copy)
+                w4_q = [quantise_w4(0)]
+                weave(w4_woven[:, HALVES[1], :], w4_raw[1][:], nc.vector.tensor_copy)
+            nc.vector.scalar_tensor_tensor(y_local[t][:], q[t][:], 1.5, y[t][:], ALU.subtract, ALU.mult)
+            if t == 0:
+                w4_q.append(quantise_w4(1))
+                reaction = 3 * [y[t]] + 2 * [y_local[t]]
+            else:
+                nc.vector.scalar_tensor_tensor(made[t][:], q[t][:], 2.0, y[t][:], ALU.mult, ALU.mult)
+                reaction = [made[t]]
+            for n, term in enumerate(2 * [tanh_e[t]] + reaction):
+                add_to_z2(t, slice(0, S), term, start=t == 0 and n == 0)
 
         def gather_e(cells, planes):
             for t in planes:
                 if cells.start == 0:
-                    nc.scalar.copy(e_pre[t], e_bank[t][:])
-                width = cells.stop - cells.start
-                e_east = sb("e_east%d_%d" % (t, cells.start), [P, width], F32)
-                e_west = sb("e_west%d_%d" % (t, cells.start), [P, width], F32)
+                    nc.scalar.copy(e_pre[t], e_acc[t][:])
+                e_east = sb("e_east%d_%d" % (t, cells.start), [P, width_of(cells)], F32)
+                e_west = sb("e_west%d_%d" % (t, cells.start), [P, width_of(cells)], F32)
                 nc.scalar.activation(e_east[:], e_window[t][:].indirect(east_sb[:, entries(cells)]), ACT.Sigmoid)
                 nc.scalar.activation(e_west[:], e_window[t][:].indirect(west_sb[:, entries(cells)]), ACT.Sigmoid)
                 add_to_z2(t, cells, e_east)
                 add_to_z2(t, cells, e_west, stop=t == PACK - 1)
 
-        def finish_z2(pair):
-            z2_words = sb("z2_words%d" % pair, [P, 2 * P, 2], F32)
-            back = bank_tile("back%d" % pair, [P, 2, 2, P], 4 + 2 * pair)
+        def gather_y_west(t):
+            y_west = sb("y_west%d" % t, [P, S], F32)
+            for half in HALVES:
+                nc.vector.tensor_tensor(y_west[:, half], y[t][:].indirect(west_sb[:, entries(half)]), y_local[t][:, half], ALU.subtract)
+            return y_west
+
+        def sum_tile(n, reuse=None):
+            return sb("y_sum%d" % n, [P, PACK, width_of(CHUNKS[n])], F32, reuse=reuse)
+
+        def gather_y_east(n, y_sum, planes):
+            cells = CHUNKS[n]
+            for t in planes:
+                nc.vector.tensor_tensor(y_sum[:, t, :], y[t][:].indirect(east_sb[:, entries(cells)]), y_west[t][:, cells], ALU.add)
+
+        def finish_z2(h):
+            z2_words = sb("z2_words%d" % h, [P, HALF, 2], F32)
+            back = bank_tile("back%d" % h, [P, 2, 2, P], 4 + 2 * h)
             for r in range(2):
-                cb = 2 * pair + r
-                z2_t = sb("z2_t%d" % cb, [P, H], BF16)
+                b = 2 * h + r
+                z2_turned = sb("z2_turned%d" % b, [P, H], BF16)
                 nc.vector.scalar_tensor_tensor(
-                    z2_t[:].rearrange("c (p t) -> c p t", t=PACK),
-                    z2_sum[cb][:].rearrange("c t p -> c p t"),
+                    z2_turned[:].rearrange("c (w i) -> c w i", i=2),
+                    z2_sum[b][:].rearrange("c (i u) p -> c (u p) i", i=2),
                     2.0,
-                    g2_eighth[:].rearrange("c (p t) -> c p t", t=PACK),
+                    g2_row[:].rearrange("c (w i) -> c w i", i=2),
                     ALU.add,
                     ALU.mult,
                 )
-                words = z2_t[:].bitcast(F32)
+                words = z2_turned[:].bitcast(F32)
                 for u in range(2):
-                    nc.tensor.transpose(back[:, r, u, :], words[:, u : 2 * P : 2], ident[:])
+                    nc.tensor.transpose(back[:, r, u, :], words[:, u * P : (u + 1) * P], ident[:])
             nc.scalar.copy(z2_words[:].rearrange("p (r c) u -> p r c u", r=2), back[:].rearrange("p r u c -> p r c u"))
             return z2_words[:].rearrange("p c u -> p (c u)").bitcast(BF16)
 
-        out_rows = out.rearrange("(mo p) c -> p mo c", p=P)
-        z_grp = {}
-        y_west = {}
-        z_q = {}
-
-        def chunk_cells(n):
-            return slice(CHUNKS[n][0], CHUNKS[n][0] + CHUNKS[n][1])
-
-        def west_step(t):
-            y_west[t] = sb("y_west%d" % t, [P, S], F32)
-            for half in halves:
-                nc.vector.tensor_tensor(
-                    y_west[t][:, half], y_window[t][:].indirect(west_sb[:, entries(half)]), y_local[t][:, half], ALU.subtract
+        def scale_z(n, y_sum):
+            planes = sb("z_planes%d" % n, [P, PACK, width_of(CHUNKS[n])], BF16)
+            for t in range(PACK):
+                nc.scalar.activation(
+                    planes[:, t, :], y_sum[:, t, :], ACT.Identity, bias=g1_eighth[:, t : t + 1], scale=g1_quarter[:, t : t + 1]
                 )
+            return planes
 
-        y_sum = {}
+        def weave_z(n, planes, reuse=None):
+            woven = sb("z_woven%d" % n, [P, width_of(CHUNKS[n]), PACK], BF16, reuse=reuse)
+            weave(woven[:], planes[:], nc.vector.tensor_copy)
+            return woven[:].rearrange("p c t -> p (c t)")
 
-        def east_steps(n, planes, tag=None):
-            cells = chunk_cells(n)
-            if n not in y_sum:
-                y_sum[n] = sb("y_sum%d" % n, [P, PACK, CHUNKS[n][1]], F32, tag=tag)
-            for t in planes:
-                nc.vector.tensor_tensor(y_sum[n][:, t, :], y_window[t][:].indirect(east_sb[:, entries(cells)]), y_west[t][:, cells], ALU.add)
-
-        def weave_z(n):
-            width = CHUNKS[n][1]
-            grouped = sb("z_grp%d" % n, [P, width, PACK], BF16)
+        def scale_and_weave_z(n, y_sum):
+            width = width_of(CHUNKS[n])
+            woven = sb("z_woven%d" % n, [P, width, PACK], BF16)
             nc.vector.scalar_tensor_tensor(
-                grouped[:],
-                y_sum[n][:].rearrange("p t c -> p c t"),
+                woven[:],
+                y_sum[:].rearrange("p t c -> p c t"),
                 0.5,
                 g1_quarter[:].unsqueeze(1).to_broadcast([P, width, PACK]),
                 ALU.add,
                 ALU.mult,
             )
-            z_grp[n] = grouped[:].rearrange("p c t -> p (c t)")
+            return woven[:].rearrange("p c t -> p (c t)")
 
-        def weave_z_on_scalar(n):
-            width = CHUNKS[n][1]
-            planes = sb("z_planes%d" % n, [P, PACK, width], BF16)
-            for t in range(PACK):
-                nc.scalar.activation(
-                    planes[:, t, :], y_sum[n][:, t, :], ACT.Identity, bias=g1_eighth[:, t : t + 1], scale=g1_quarter[:, t : t + 1]
-                )
-            grouped = sb("z_grp%d" % n, [P, width, PACK], BF16)
-            nc.scalar.copy(grouped[:].rearrange("p (c i) t -> p c t i", i=4), planes[:].rearrange("p t (c i) -> p c t i", i=4))
-            z_grp[n] = grouped[:].rearrange("p c t -> p (c t)")
+        out_rows = out.rearrange("(m p) c -> p m c", p=P)
 
-        def quantise_z(n, tag=None):
-            z_q[n] = quantise("z_chunk%d" % n, z_grp[n], CHUNKS[n][1], tag=tag)
+        def open_groups(n, z2_q, banks):
+            cells = CHUNKS[n]
+            blocks = N // P // len(banks)
+            accs = [bank_tile("acc%d_%d" % (n, a), [P, blocks, width_of(cells)], bank) for a, bank in enumerate(banks)]
+            in_half = slice(cells.start % HALF, cells.start % HALF + width_of(cells))
+            for m in range(N // P):
+                acc = accs[m // blocks][:, m % blocks, :]
+                mx_pass(acc, w4_q[m // 2], slice(m % 2 * P, (m % 2 + 1) * P), z2_q, in_half, m % blocks == 0, False)
+            return accs
 
-        def out_pass(acc, mo, n, term, start, stop):
-            c0, width = CHUNKS[n]
-            if term == "z":
-                w_q, act_q, cells = late["w3"], z_q[n], slice(0, width)
-            else:
-                w_q, act_q, cells = w4_q[mo // 2], late["z2", c0 // 256], slice(c0 % 256, c0 % 256 + width)
-            first = mo * P if term == "z" else mo % 2 * P
-            cols = slice(first, first + P)
-            nc.tensor.matmul_mx(
-                out=acc,
-                lhsT=w_q[0][:, cols].bitcast(FP8X4),
-                lhsT_scale=w_q[1][:, cols],
-                rhs=act_q[0][:, cells].bitcast(FP8X4),
-                rhs_scale=act_q[1][:, cells],
-                start=start,
-                stop=stop,
-            )
-
-        def open_middle(n):
-            bank = bank_tile("acc%d" % n, [P, PACK, CHUNKS[n][1]], 5)
-            for mo in range(PACK):
-                out_pass(bank[:, mo, :], mo, n, "z2", mo == 0, False)
-            return bank
-
-        def close_middle(n, bank):
-            c0, width = CHUNKS[n]
-            for mo in range(PACK):
-                out_pass(bank[:, mo, :], mo, n, "z", False, mo == PACK - 1)
-            result = sb("result%d" % n, [P, PACK, width], F32)
-            nc.scalar.copy(result[:], bank[:])
-            nc.sync.dma_start(out=out_rows[:, :, c0 : c0 + width], in_=result[:])
-
-        def open_pairs(n, term, tags):
-            banks = [bank_tile("acc%d_%d" % (n, half), [P, 2, CHUNKS[n][1]], tag) for half, tag in enumerate(tags)]
-            for mo in range(PACK):
-                out_pass(banks[mo // 2][:, mo % 2, :], mo, n, term, mo % 2 == 0, False)
-            return banks
-
-        def close_pairs(n, term, banks, copies, queues):
-            c0, width = CHUNKS[n]
-            for half, copy in enumerate(copies):
-                for mo in (2 * half, 2 * half + 1):
-                    out_pass(banks[half][:, mo % 2, :], mo, n, term, False, mo % 2 == 1)
-                result = sb("result%d_%d" % (n, half), [P, 2, width], F32)
-                copy(result[:], banks[half][:])
-                queues[half].dma_start(out=out_rows[:, 2 * half : 2 * half + 2, c0 : c0 + width], in_=result[:])
+        def close_groups(n, z_q, accs, copies, queues):
+            cells = CHUNKS[n]
+            blocks = N // P // len(accs)
+            for a, acc in enumerate(accs):
+                for r in range(blocks):
+                    m = a * blocks + r
+                    mx_pass(acc[:, r, :], w3_q, slice(m * P, (m + 1) * P), z_q, slice(0, width_of(cells)), False, r == blocks - 1)
+                result = sb("result%d_%d" % (n, a), [P, blocks, width_of(cells)], F32)
+                copies[a](result[:], acc[:])
+                queues[a].dma_start(out=out_rows[:, a * blocks : (a + 1) * blocks, cells], in_=result[:])
 
         gather_e(slice(0, S), (0, 1))
-        round_rows(w3_grp[:], w3_raw[:], nc.vector.tensor_copy)
-        west_step(0)
-        late["w3"] = quantise("w3", w3_grp[:].rearrange("p n j -> p (n j)"), N)
-        for t in range(1, PACK):
-            west_step(t)
-        for half in halves:
+        weave(w3_woven[:], w3_raw[:], nc.vector.tensor_copy)
+        y_west = [gather_y_west(0)]
+        w3_q = quantise("w3", w3_woven[:].rearrange("p n j -> p (n j)"))
+        y_west.extend(gather_y_west(t) for t in range(1, PACK))
+        for half in HALVES:
             gather_e(half, (2, 3))
-        east_steps(0, range(PACK))
-        weave_z_on_scalar(0)
-        z2_grp0 = finish_z2(0)
-        east_steps(1, range(PACK), "e_west3_0")
-        z2_grp1 = finish_z2(1)
-        weave_z(1)
-        late["z2", 0] = quantise("z2_0", z2_grp0, 2 * P, tag="e_west3_256")
-        first_banks = open_pairs(0, "z2", (0, 1))
-        quantise_z(1)
-        quantise_z(0, "z2_t2")
-        close_pairs(0, "z", first_banks, (nc.scalar.copy, nc.scalar.copy), (nc.sync, nc.sync))
-        east_steps(2, (0, 1), "z2_t3")
-        late["z2", 1] = quantise("z2_1", z2_grp1, 2 * P)
-        middle_bank = open_middle(1)
-        close_middle(1, middle_bank)
-        last_banks = open_pairs(2, "z2", (2, 3))
-        east_steps(2, (2, 3))
-        weave_z(2)
-        quantise_z(2)
-        close_pairs(2, "z", last_banks, (nc.scalar.copy, nc.vector.tensor_copy), (nc.scalar, nc.sync))
+
+        y_sum0 = sum_tile(0)
+        gather_y_east(0, y_sum0, range(PACK))
+        z_planes0 = scale_z(0, y_sum0)
+        z2_woven0 = finish_z2(0)
+        y_sum1 = sum_tile(1, reuse="e_west3_0")
+        gather_y_east(1, y_sum1, range(PACK))
+        z_planes1 = scale_z(1, y_sum1)
+        z2_woven1 = finish_z2(1)
+        z_woven0 = weave_z(0, z_planes0, reuse="e_east3_%d" % HALF)
+        z2_q0 = quantise("z2_0", z2_woven0, reuse="e_west3_%d" % HALF)
+        accs0 = open_groups(0, z2_q0, (0, 1))
+        z_woven1 = weave_z(1, z_planes1)
+        close_groups(0, quantise("z_chunk0", z_woven0), accs0, (nc.scalar.copy, nc.scalar.copy), (nc.sync, nc.sync))
+        z_q1 = quantise("z_chunk1", z_woven1)
+        y_sum2 = sum_tile(2, reuse="z2_turned3")
+        gather_y_east(2, y_sum2, (0, 1))
+        z2_q1 = quantise("z2_1", z2_woven1)
+        close_groups(1, z_q1, open_groups(1, z2_q1, (5,)), (nc.scalar.copy,), (nc.sync,))
+        accs2 = open_groups(2, z2_q1, (2, 3))
+        gather_y_east(2, y_sum2, (2, 3))
+        z_q2 = quantise("z_chunk2", scale_and_weave_z(2, y_sum2))
+        close_groups(2, z_q2, accs2, (nc.scalar.copy, nc.vector.tensor_copy), (nc.scalar, nc.sync))

@@ -74,9 +74,9 @@ def tile_picked_grayscott_none_p_kernel(
             nc.sync.dma_start(out=col[:], in_=g.rearrange("(p t) o -> p (t o)", t=PACK))
             return col
 
-        nc.sync.dma_start(offs_sb[:], offs)
-        w1_raw = load_weight("w1_raw", w1, slice(0, H))
         g2_sb = load_gain("g2_sb", g2)
+        w1_raw = load_weight("w1_raw", w1, slice(0, H))
+        nc.sync.dma_start(offs_sb[:], offs)
         g1_sb = load_gain("g1_sb", g1)
         x_word_tab = sb("x_word_tab", [P, T], I32)
         nc.sync.dma_start(out=x_word_tab[:], in_=x_words[0].rearrange("p n t -> p (n t)").bitcast(I32))
@@ -103,8 +103,6 @@ def tile_picked_grayscott_none_p_kernel(
         g1_quarter = scaled("g1_quarter", g1_sb, 0.25)
         g1_eighth = scaled("g1_eighth", g1_sb, 0.125)
 
-        x_scale = sb("x_scale", [P, S], U8)
-        nc.vector.tensor_copy(x_scale[:], x_scale_tab[:].indirect(offs_sb[:]))
 
         def quantise(name, woven, reuse=None):
             columns = woven.shape[1] // PACK
@@ -144,6 +142,8 @@ def tile_picked_grayscott_none_p_kernel(
             round_plane_pair("w1_woven%d" % u, w1_raw, u, copy) for u, copy in enumerate((nc.vector.tensor_copy, nc.scalar.copy))
         ]
         w1_q = [quantise("w1_%d" % u, w1_woven[u]) for u in range(2)]
+        x_scale = sb("x_scale", [P, S], U8)
+        nc.vector.tensor_copy(x_scale[:], x_scale_tab[:].indirect(offs_sb[:]))
         x_code = sb("x_code", [P, S], U32)
         for half in HALVES:
             nc.vector.tensor_copy(x_code[:, half], x_word_tab[:].bitcast(U32).indirect(offs_sb[:, entries(half)]))

@@ -75,12 +75,12 @@ def tile_picked_grayscott_none_p_kernel(
             return col
 
         g2_sb = load_gain("g2_sb", g2)
-        w1_raw = load_weight("w1_raw", w1, slice(0, H))
+        w2_raw = load_weight("w2_raw", w2, slice(0, H))
         nc.sync.dma_start(offs_sb[:], offs)
         g1_sb = load_gain("g1_sb", g1)
         x_word_tab = sb("x_word_tab", [P, T], I32)
         nc.sync.dma_start(out=x_word_tab[:], in_=x_words[0].rearrange("p n t -> p (n t)").bitcast(I32))
-        w2_raw = [load_weight("w2_raw%d" % h, w2, cols) for h, cols in enumerate(HALVES)]
+        w1_raw = [load_weight("w1_raw%d" % h, w1, cols) for h, cols in enumerate(HALVES)]
         w4_raw = [load_weight("w4_raw%d" % h, w4, cols) for h, cols in enumerate(HALVES)]
         nc.sync.dma_start(west_sb[:], west)
         nc.sync.dma_start(east_sb[:], east)
@@ -88,6 +88,8 @@ def tile_picked_grayscott_none_p_kernel(
 
         ident = sb("ident", [P, P], F32)
         make_identity(nc, ident[:])
+        minus_two = sb("minus_two", [P, 1], F32)
+        nc.gpsimd.memset(minus_two[:], -2.0)
 
         def scaled(name, g, factor):
             res = sb(name, [P, PACK], F32)
@@ -95,7 +97,7 @@ def tile_picked_grayscott_none_p_kernel(
             return res
 
         g2_eighth = scaled("g2_eighth", g2_sb, 0.125)
-        spread = bank_tile("spread", [P, PACK, P], 2)
+        spread = bank_tile("spread", [P, PACK, P], 3)
         for t in range(PACK):
             nc.tensor.transpose(spread[:, slot(t), :], g2_eighth[:, t : t + 1].to_broadcast([P, P]), ident[:])
         g2_row = sb("g2_row", [P, H], F32)
@@ -138,10 +140,10 @@ def tile_picked_grayscott_none_p_kernel(
         def weave(dest, src, copy):
             copy(dest.rearrange("p (c i) j -> p c j i", i=LINE), src.rearrange("p j (c i) -> p c j i", i=LINE))
 
-        w1_woven = [
-            round_plane_pair("w1_woven%d" % u, w1_raw, u, copy) for u, copy in enumerate((nc.vector.tensor_copy, nc.scalar.copy))
+        w2_woven = [
+            round_plane_pair("w2_woven%d" % u, w2_raw, u, copy) for u, copy in enumerate((nc.vector.tensor_copy, nc.scalar.copy))
         ]
-        w1_q = [quantise("w1_%d" % u, w1_woven[u]) for u in range(2)]
+        w2_q = [quantise("w2_%d" % u, w2_woven[u]) for u in range(2)]
         x_scale = sb("x_scale", [P, S], U8)
         nc.vector.tensor_copy(x_scale[:], x_scale_tab[:].indirect(offs_sb[:]))
         x_code = sb("x_code", [P, S], U32)
@@ -154,23 +156,7 @@ def tile_picked_grayscott_none_p_kernel(
         y = [sb("y%d" % t, [P, S], F32) for t in range(PACK)]
         q = [sb("q%d" % t, [P, S], F32) for t in range(PACK)]
         y_local = [sb("y_local%d" % t, [P, S], F32) for t in range(PACK)]
-        made = {t: sb("made%d" % t, [P, S], F32) for t in range(1, PACK)}
-
-        for bank, half in zip((4, 3), HALVES):
-            nc.scalar.activation(y[0][:, half], first_product(0, bank, w1_q, cells=half)[:], ACT.Sigmoid)
-        for t in range(1, PACK):
-            nc.scalar.activation(y[t][:], first_product(t, 4 + t, w1_q)[:], ACT.Sigmoid)
-
-        w2_woven = sb("w2_woven", [P, PACK, P, PACK], BF16)
-        for h in range(2):
-            nc.vector.tensor_copy(
-                w2_woven[:].rearrange("p t m j -> p m t j")[:, h * P // 2 : (h + 1) * P // 2],
-                w2_raw[h][:].rearrange("p j (m t) -> p m t j", t=PACK),
-            )
-        w2_q = [quantise("w2_%d" % u, w2_woven[:, 2 * u : 2 * u + 2].rearrange("p t m j -> p (t m j)")) for u in range(2)]
-        w3_woven = sb("w3_woven", [P, N, PACK], BF16)
-        w4_woven = sb("w4_woven", [P, N, PACK], BF16)
-        e_acc = [first_product(t, t, w2_q) for t in range(PACK)]
+        made = {t: sb("made%d" % t, [P, S], F32) for t in range(2, PACK)}
 
         z2_sum = [bank_tile("z2_sum%d" % b, [P, PACK, P], 4 + b) for b in range(S // P)]
 
@@ -180,30 +166,64 @@ def tile_picked_grayscott_none_p_kernel(
                     z2_sum[b][:, slot(t), :], lhsT=term[:, n * P : (n + 1) * P], rhs=ident[:], is_transpose=True, start=start, stop=stop
                 )
 
+        def local_e(t, bank):
+            acc = first_product(t, bank, w2_q)
+            nc.scalar.activation(tanh_e[t], acc[:], ACT.Tanh, scale=0.5)
+            nc.scalar.copy(e_pre[t], acc[:])
+            nc.scalar.activation(q[t][:], tanh_e[t], ACT.Square, bias=1.0)
+
+        def local_y(t, bank):
+            nc.scalar.activation(y[t][:], first_product(t, bank, w1_q)[:], ACT.Sigmoid)
+
+        def react(t):
+            nc.vector.scalar_tensor_tensor(y_local[t][:], q[t][:], 1.5, y[t][:], ALU.subtract, ALU.mult)
+            if t in made:
+                nc.vector.scalar_tensor_tensor(made[t][:], q[t][:], 2.0, y[t][:], ALU.mult, ALU.mult)
+                reaction = [made[t]]
+            else:
+                reaction = 3 * [y[t]] + 2 * [y_local[t]]
+            for term in 2 * tanh_e[t + 1 : t + 2]:
+                add_to_z2(t + 1, slice(0, S), term)
+            for term in reaction:
+                add_to_z2(t, slice(0, S), term)
+
         def quantise_w4(h):
             return quantise("w4_%d" % h, w4_woven[:, HALVES[h], :].rearrange("p n j -> p (n j)"))
 
-        for t in range(PACK):
-            nc.scalar.activation(tanh_e[t], e_acc[t][:], ACT.Tanh, scale=0.5)
-            nc.scalar.activation(q[t][:], tanh_e[t], ACT.Square, bias=1.0)
-            if t == 0:
-                weave(w4_woven[:, HALVES[0], :], w4_raw[0][:], nc.vector.tensor_copy)
-                w4_q = [quantise_w4(0)]
-                weave(w4_woven[:, HALVES[1], :], w4_raw[1][:], nc.vector.tensor_copy)
-            nc.vector.scalar_tensor_tensor(y_local[t][:], q[t][:], 1.5, y[t][:], ALU.subtract, ALU.mult)
-            if t == 0:
-                w4_q.append(quantise_w4(1))
-                reaction = 3 * [y[t]] + 2 * [y_local[t]]
-            else:
-                nc.vector.scalar_tensor_tensor(made[t][:], q[t][:], 2.0, y[t][:], ALU.mult, ALU.mult)
-                reaction = [made[t]]
-            for n, term in enumerate(2 * [tanh_e[t]] + reaction):
-                add_to_z2(t, slice(0, S), term, start=t == 0 and n == 0)
+        for bank, half in enumerate(HALVES):
+            acc = first_product(0, bank, w2_q, cells=half)
+            nc.scalar.activation(tanh_e[0][:, half], acc[:], ACT.Sigmoid)
+            nc.scalar.copy(e_pre[0][:, half], acc[:])
+        nc.scalar.activation(q[0][:], tanh_e[0], ACT.Square, scale=2.0)
+
+        w1_woven = sb("w1_woven", [P, PACK, P, PACK], BF16)
+        for h in range(2):
+            nc.vector.tensor_copy(
+                w1_woven[:].rearrange("p t m j -> p m t j")[:, h * P // 2 : (h + 1) * P // 2],
+                w1_raw[h][:].rearrange("p j (m t) -> p m t j", t=PACK),
+            )
+        w1_q = [quantise("w1_%d" % u, w1_woven[:, 2 * u : 2 * u + 2].rearrange("p t m j -> p (t m j)")) for u in range(2)]
+        w3_woven = sb("w3_woven", [P, N, PACK], BF16)
+        w4_woven = sb("w4_woven", [P, N, PACK], BF16)
+
+        local_y(0, 0)
+        local_e(1, 2)
+        local_y(1, 1)
+        local_e(2, 0)
+        local_y(2, 2)
+        local_e(3, 1)
+        local_y(3, 3)
+        add_to_z2(0, slice(0, S), minus_two[:].to_broadcast([P, S]), start=True)
+        for n in range(4):
+            add_to_z2(0, slice(0, S), tanh_e[0])
+        weave(w4_woven[:, HALVES[0], :], w4_raw[0][:], nc.vector.tensor_copy)
+        w4_q = [quantise_w4(0)]
+        weave(w4_woven[:, HALVES[1], :], w4_raw[1][:], nc.vector.tensor_copy)
+        react(0)
+        w4_q.append(quantise_w4(1))
 
         def gather_e(cells, planes):
             for t in planes:
-                if cells.start == 0:
-                    nc.scalar.copy(e_pre[t], e_acc[t][:])
                 e_east = sb("e_east%d_%d" % (t, cells.start), [P, width_of(cells)], F32)
                 e_west = sb("e_west%d_%d" % (t, cells.start), [P, width_of(cells)], F32)
                 nc.scalar.activation(e_east[:], e_window[t][:].indirect(east_sb[:, entries(cells)]), ACT.Sigmoid)
@@ -294,11 +314,13 @@ def tile_picked_grayscott_none_p_kernel(
                 copies[a](result[:], acc[:])
                 queues[a].dma_start(out=out_rows[:, a * blocks : (a + 1) * blocks, cells], in_=result[:])
 
+        y_west = [gather_y_west(0)]
+        for t in range(1, PACK):
+            react(t)
+            y_west.append(gather_y_west(t))
         gather_e(slice(0, S), (0, 1))
         weave(w3_woven[:], w3_raw[:], nc.vector.tensor_copy)
-        y_west = [gather_y_west(0)]
         w3_q = quantise("w3", w3_woven[:].rearrange("p n j -> p (n j)"))
-        y_west.extend(gather_y_west(t) for t in range(1, PACK))
         for half in HALVES:
             gather_e(half, (2, 3))
 

@@ -181,7 +181,7 @@ def tile_picked_grayscott_none_p_kernel(
                 nc.vector.scalar_tensor_tensor(made[t][:], q[t][:], 2.0, y[t][:], ALU.mult, ALU.mult)
                 reaction = [made[t]]
             else:
-                reaction = 3 * [y[t]] + 2 * [y_local[t]]
+                reaction = (3 if t else 0) * [y[t]] + 2 * [y_local[t]]
             for term in 2 * tanh_e[t + 1 : t + 2]:
                 add_to_z2(t + 1, slice(0, S), term)
             for term in reaction:
@@ -213,7 +213,9 @@ def tile_picked_grayscott_none_p_kernel(
         local_y(2, 2)
         local_e(3, 1)
         local_y(3, 3)
-        add_to_z2(0, slice(0, S), minus_two[:].to_broadcast([P, S]), start=True)
+        for n in range(3):
+            add_to_z2(0, slice(0, S), y[0], start=n == 0)
+        add_to_z2(0, slice(0, S), minus_two[:].to_broadcast([P, S]))
         for n in range(4):
             add_to_z2(0, slice(0, S), tanh_e[0])
         weave(w4_woven[:, HALVES[0], :], w4_raw[0][:], nc.vector.tensor_copy)

@@ -74,9 +74,9 @@ def tile_picked_grayscott_none_p_kernel(
             nc.sync.dma_start(out=col[:], in_=g.rearrange("(p t) o -> p (t o)", t=PACK))
             return col
 
-        g2_sb = load_gain("g2_sb", g2)
-        w2_raw = load_weight("w2_raw", w2, slice(0, H))
         nc.sync.dma_start(offs_sb[:], offs)
+        w2_raw = load_weight("w2_raw", w2, slice(0, H))
+        g2_sb = load_gain("g2_sb", g2)
         g1_sb = load_gain("g1_sb", g1)
         x_word_tab = sb("x_word_tab", [P, T], I32)
         nc.sync.dma_start(out=x_word_tab[:], in_=x_words[0].rearrange("p n t -> p (n t)").bitcast(I32))
@@ -88,8 +88,8 @@ def tile_picked_grayscott_none_p_kernel(
 
         ident = sb("ident", [P, P], F32)
         make_identity(nc, ident[:])
-        minus_two = sb("minus_two", [P, 1], F32)
-        nc.gpsimd.memset(minus_two[:], -2.0)
+        warm_up = sb("warm_up", [P, 1], F32)
+        nc.scalar.activation(warm_up[:], g2_sb[:, 0:1], ACT.Sigmoid)
 
         def scaled(name, g, factor):
             res = sb(name, [P, PACK], F32)
@@ -192,9 +192,9 @@ def tile_picked_grayscott_none_p_kernel(
 
         for bank, half in enumerate(HALVES):
             acc = first_product(0, bank, w2_q, cells=half)
-            nc.scalar.activation(tanh_e[0][:, half], acc[:], ACT.Sigmoid)
+            nc.scalar.activation(tanh_e[0][:, half], acc[:], ACT.Tanh, scale=0.5)
             nc.scalar.copy(e_pre[0][:, half], acc[:])
-        nc.scalar.activation(q[0][:], tanh_e[0], ACT.Square, scale=2.0)
+        nc.scalar.activation(q[0][:], tanh_e[0], ACT.Square, bias=1.0)
 
         w1_woven = sb("w1_woven", [P, PACK, P, PACK], BF16)
         for h in range(2):
@@ -215,8 +215,7 @@ def tile_picked_grayscott_none_p_kernel(
         local_y(3, 3)
         for n in range(3):
             add_to_z2(0, slice(0, S), y[0], start=n == 0)
-        add_to_z2(0, slice(0, S), minus_two[:].to_broadcast([P, S]))
-        for n in range(4):
+        for n in range(2):
             add_to_z2(0, slice(0, S), tanh_e[0])
         weave(w4_woven[:, HALVES[0], :], w4_raw[0][:], nc.vector.tensor_copy)
         w4_q = [quantise_w4(0)]
@@ -344,7 +343,7 @@ def tile_picked_grayscott_none_p_kernel(
         gather_y_east(2, y_sum2, (0, 1))
         z2_q1 = quantise("z2_1", z2_woven1)
         close_groups(1, z_q1, open_groups(1, z2_q1, (5,)), (nc.scalar.copy,), (nc.sync,))
-        accs2 = open_groups(2, z2_q1, (2, 3))
+        accs2 = open_groups(2, z2_q1, (2, 3, 4, 7))
         gather_y_east(2, y_sum2, (2, 3))
         z_q2 = quantise("z_chunk2", scale_and_weave_z(2, y_sum2))
-        close_groups(2, z_q2, accs2, (nc.scalar.copy, nc.vector.tensor_copy), (nc.scalar, nc.sync))
+        close_groups(2, z_q2, accs2, 2 * (nc.scalar.copy, nc.vector.tensor_copy), 2 * (nc.scalar, nc.sync))

@@ -77,33 +77,33 @@ def tile_picked_grayscott_none_p_kernel(
         nc.sync.dma_start(offs_sb[:], offs)
         w2_raw = load_weight("w2_raw", w2, slice(0, H))
         g2_sb = load_gain("g2_sb", g2)
-        g1_sb = load_gain("g1_sb", g1)
+        nc.sync.dma_start(west_sb[:], west)
         x_word_tab = sb("x_word_tab", [P, T], I32)
         nc.sync.dma_start(out=x_word_tab[:], in_=x_words[0].rearrange("p n t -> p (n t)").bitcast(I32))
         w1_raw = [load_weight("w1_raw%d" % h, w1, cols) for h, cols in enumerate(HALVES)]
         w4_raw = [load_weight("w4_raw%d" % h, w4, cols) for h, cols in enumerate(HALVES)]
-        nc.sync.dma_start(west_sb[:], west)
         nc.sync.dma_start(east_sb[:], east)
         w3_raw = load_weight("w3_raw", w3, slice(0, N))
+        g1_sb = load_gain("g1_sb", g1)
 
         ident = sb("ident", [P, P], F32)
         make_identity(nc, ident[:])
         warm_up = sb("warm_up", [P, 1], F32)
         nc.scalar.activation(warm_up[:], g2_sb[:, 0:1], ACT.Sigmoid)
 
-        def scaled(name, g, factor):
+        def scaled(name, g, factor, engine):
             res = sb(name, [P, PACK], F32)
-            nc.gpsimd.tensor_scalar(res[:], g[:], factor, 0.0, ALU.mult, ALU.add)
+            engine.tensor_scalar(res[:], g[:], factor, 0.0, ALU.mult, ALU.add)
             return res
 
-        g2_eighth = scaled("g2_eighth", g2_sb, 0.125)
+        g2_eighth = scaled("g2_eighth", g2_sb, 0.125, nc.gpsimd)
         spread = bank_tile("spread", [P, PACK, P], 3)
         for t in range(PACK):
             nc.tensor.transpose(spread[:, slot(t), :], g2_eighth[:, t : t + 1].to_broadcast([P, P]), ident[:])
         g2_row = sb("g2_row", [P, H], F32)
         nc.scalar.copy(g2_row[:].rearrange("c (w i) -> c w i", i=2), spread[:].rearrange("c (i u) p -> c (u p) i", i=2))
-        g1_quarter = scaled("g1_quarter", g1_sb, 0.25)
-        g1_eighth = scaled("g1_eighth", g1_sb, 0.125)
+        g1_quarter = scaled("g1_quarter", g1_sb, 0.25, nc.vector)
+        g1_eighth = scaled("g1_eighth", g1_sb, 0.125, nc.vector)
 
 
         def quantise(name, woven, reuse=None):
@@ -294,23 +294,26 @@ def tile_picked_grayscott_none_p_kernel(
 
         out_rows = out.rearrange("(m p) c -> p m c", p=P)
 
-        def open_groups(n, z2_q, banks):
-            cells = CHUNKS[n]
+        def z_operands(z_q, n):
+            return lambda m: (w3_q, slice(m * P, (m + 1) * P), z_q, slice(0, width_of(CHUNKS[n])))
+
+        def z2_operands(z2_q, n):
+            first = CHUNKS[n].start % HALF
+            return lambda m: (w4_q[m // 2], slice(m % 2 * P, (m % 2 + 1) * P), z2_q, slice(first, first + width_of(CHUNKS[n])))
+
+        def open_groups(n, operands, banks):
             blocks = N // P // len(banks)
-            accs = [bank_tile("acc%d_%d" % (n, a), [P, blocks, width_of(cells)], bank) for a, bank in enumerate(banks)]
-            in_half = slice(cells.start % HALF, cells.start % HALF + width_of(cells))
+            accs = [bank_tile("acc%d_%d" % (n, a), [P, blocks, width_of(CHUNKS[n])], bank) for a, bank in enumerate(banks)]
             for m in range(N // P):
-                acc = accs[m // blocks][:, m % blocks, :]
-                mx_pass(acc, w4_q[m // 2], slice(m % 2 * P, (m % 2 + 1) * P), z2_q, in_half, m % blocks == 0, False)
+                mx_pass(accs[m // blocks][:, m % blocks, :], *operands(m), m % blocks == 0, False)
             return accs
 
-        def close_groups(n, z_q, accs, copies, queues):
+        def close_groups(n, operands, accs, copies, queues):
             cells = CHUNKS[n]
             blocks = N // P // len(accs)
             for a, acc in enumerate(accs):
                 for r in range(blocks):
-                    m = a * blocks + r
-                    mx_pass(acc[:, r, :], w3_q, slice(m * P, (m + 1) * P), z_q, slice(0, width_of(cells)), False, r == blocks - 1)
+                    mx_pass(acc[:, r, :], *operands(a * blocks + r), False, r == blocks - 1)
                 result = sb("result%d_%d" % (n, a), [P, blocks, width_of(cells)], F32)
                 copies[a](result[:], acc[:])
                 queues[a].dma_start(out=out_rows[:, a * blocks : (a + 1) * blocks, cells], in_=result[:])
@@ -335,15 +338,15 @@ def tile_picked_grayscott_none_p_kernel(
         z2_woven1 = finish_z2(1)
         z_woven0 = weave_z(0, z_planes0, reuse="e_east3_%d" % HALF)
         z2_q0 = quantise("z2_0", z2_woven0, reuse="e_west3_%d" % HALF)
-        accs0 = open_groups(0, z2_q0, (0, 1))
+        accs0 = open_groups(0, z2_operands(z2_q0, 0), (0, 1))
         z_woven1 = weave_z(1, z_planes1)
-        close_groups(0, quantise("z_chunk0", z_woven0), accs0, (nc.scalar.copy, nc.scalar.copy), (nc.sync, nc.sync))
-        z_q1 = quantise("z_chunk1", z_woven1)
+        close_groups(0, z_operands(quantise("z_chunk0", z_woven0), 0), accs0, (nc.scalar.copy, nc.scalar.copy), (nc.sync, nc.sync))
+        accs1 = open_groups(1, z_operands(quantise("z_chunk1", z_woven1), 1), (5,))
         y_sum2 = sum_tile(2, reuse="z2_turned3")
         gather_y_east(2, y_sum2, (0, 1))
         z2_q1 = quantise("z2_1", z2_woven1)
-        close_groups(1, z_q1, open_groups(1, z2_q1, (5,)), (nc.scalar.copy,), (nc.sync,))
-        accs2 = open_groups(2, z2_q1, (2, 3, 4, 7))
+        close_groups(1, z2_operands(z2_q1, 1), accs1, (nc.scalar.copy,), (nc.sync,))
+        accs2 = open_groups(2, z2_operands(z2_q1, 2), (2, 3, 4, 7))
         gather_y_east(2, y_sum2, (2, 3))
         z_q2 = quantise("z_chunk2", scale_and_weave_z(2, y_sum2))
-        close_groups(2, z_q2, accs2, 2 * (nc.scalar.copy, nc.vector.tensor_copy), 2 * (nc.scalar, nc.sync))
+        close_groups(2, z_operands(z_q2, 2), accs2, 2 * (nc.scalar.copy, nc.vector.tensor_copy), 2 * (nc.scalar, nc.sync))

@@ -88,8 +88,8 @@ def tile_picked_grayscott_none_p_kernel(
 
         ident = sb("ident", [P, P], F32)
         make_identity(nc, ident[:])
-        warm_up = sb("warm_up", [P, 1], F32)
-        nc.scalar.activation(warm_up[:], g2_sb[:, 0:1], ACT.Sigmoid)
+        minus_two = sb("minus_two", [P, 1], F32)
+        nc.gpsimd.memset(minus_two[:], -2.0)
 
         def scaled(name, g, factor, engine):
             res = sb(name, [P, PACK], F32)
@@ -192,9 +192,9 @@ def tile_picked_grayscott_none_p_kernel(
 
         for bank, half in enumerate(HALVES):
             acc = first_product(0, bank, w2_q, cells=half)
-            nc.scalar.activation(tanh_e[0][:, half], acc[:], ACT.Tanh, scale=0.5)
+            nc.scalar.activation(tanh_e[0][:, half], acc[:], ACT.Sigmoid)
             nc.scalar.copy(e_pre[0][:, half], acc[:])
-        nc.scalar.activation(q[0][:], tanh_e[0], ACT.Square, bias=1.0)
+        nc.scalar.activation(q[0][:], tanh_e[0], ACT.Square, scale=2.0)
 
         w1_woven = sb("w1_woven", [P, PACK, P, PACK], BF16)
         for h in range(2):
@@ -215,7 +215,8 @@ def tile_picked_grayscott_none_p_kernel(
         local_y(3, 3)
         for n in range(3):
             add_to_z2(0, slice(0, S), y[0], start=n == 0)
-        for n in range(2):
+        add_to_z2(0, slice(0, S), minus_two[:].to_broadcast([P, S]))
+        for n in range(4):
             add_to_z2(0, slice(0, S), tanh_e[0])
         weave(w4_woven[:, HALVES[0], :], w4_raw[0][:], nc.vector.tensor_copy)
         w4_q = [quantise_w4(0)]

@@ -56,10 +56,14 @@ def tile_picked_grayscott_none_p_kernel(
         west_sb = lists.tile([P, LIST_COLS], U16, name="west_sb")
         east_sb = lists.tile([P, LIST_COLS], U16, name="east_sb")
 
+        g2_rows = sb("g2_rows", [P, P], F32)
+        nc.gpsimd.memset(g2_rows[:], 0.0)
+        nc.scalar.dma_start(out=g2_rows[0:PACK, :], in_=g2.rearrange("(r c) o -> r (c o)", r=PACK))
+
         x_scale_tab = sb("x_scale_tab", [P, T], U8)
-        nc.vector.memset(x_scale_tab[:].bitcast(I32), 0)
-        for quad in range(4):
-            nc.scalar.dma_start(
+        nc.gpsimd.memset(x_scale_tab[:].bitcast(I32), 0)
+        for quad, queue in enumerate((nc.sync, nc.sync, nc.scalar, nc.scalar)):
+            queue.dma_start(
                 out=x_scale_tab[32 * quad : 32 * quad + 4, :].bitcast(I32),
                 in_=x_scales[0, 4 * quad : 4 * quad + 4, :].bitcast(I32),
             )
@@ -74,14 +78,13 @@ def tile_picked_grayscott_none_p_kernel(
             nc.sync.dma_start(out=col[:], in_=g.rearrange("(p t) o -> p (t o)", t=PACK))
             return col
 
-        nc.sync.dma_start(offs_sb[:], offs)
         w2_raw = load_weight("w2_raw", w2, slice(0, H))
-        g2_sb = load_gain("g2_sb", g2)
-        nc.sync.dma_start(west_sb[:], west)
+        nc.sync.dma_start(offs_sb[:], offs)
         x_word_tab = sb("x_word_tab", [P, T], I32)
         nc.sync.dma_start(out=x_word_tab[:], in_=x_words[0].rearrange("p n t -> p (n t)").bitcast(I32))
         w1_raw = [load_weight("w1_raw%d" % h, w1, cols) for h, cols in enumerate(HALVES)]
         w4_raw = [load_weight("w4_raw%d" % h, w4, cols) for h, cols in enumerate(HALVES)]
+        nc.sync.dma_start(west_sb[:], west)
         nc.sync.dma_start(east_sb[:], east)
         w3_raw = load_weight("w3_raw", w3, slice(0, N))
         g1_sb = load_gain("g1_sb", g1)
@@ -91,19 +94,24 @@ def tile_picked_grayscott_none_p_kernel(
         minus_two = sb("minus_two", [P, 1], F32)
         nc.gpsimd.memset(minus_two[:], -2.0)
 
-        def scaled(name, g, factor, engine):
-            res = sb(name, [P, PACK], F32)
+        def scaled(name, g, factor, engine, reuse=None):
+            res = sb(name, [P, PACK], F32, reuse=reuse)
             engine.tensor_scalar(res[:], g[:], factor, 0.0, ALU.mult, ALU.add)
             return res
 
-        g2_eighth = scaled("g2_eighth", g2_sb, 0.125, nc.gpsimd)
-        spread = bank_tile("spread", [P, PACK, P], 3)
-        for t in range(PACK):
-            nc.tensor.transpose(spread[:, slot(t), :], g2_eighth[:, t : t + 1].to_broadcast([P, P]), ident[:])
+        g2_turned = bank_tile("g2_turned", [P, P], 0)
+        nc.tensor.transpose(g2_turned[:], g2_rows[:], ident[:])
+        g2_eighth = sb("g2_eighth", [P, PACK], F32)
+        nc.scalar.activation(g2_eighth[:], g2_turned[:, 0:PACK], ACT.Copy, scale=0.125)
         g2_row = sb("g2_row", [P, H], F32)
-        nc.scalar.copy(g2_row[:].rearrange("c (w i) -> c w i", i=2), spread[:].rearrange("c (i u) p -> c (u p) i", i=2))
-        g1_quarter = scaled("g1_quarter", g1_sb, 0.25, nc.vector)
-        g1_eighth = scaled("g1_eighth", g1_sb, 0.125, nc.vector)
+        for half, bank in enumerate((1, 2)):
+            spread = bank_tile("spread", [P, 2, P], bank)
+            for r in range(2):
+                nc.tensor.transpose(spread[:, r, :], g2_eighth[:, 2 * half + r : 2 * half + r + 1].to_broadcast([P, P]), ident[:])
+            nc.scalar.copy(
+                g2_row[:].rearrange("c (u p i) -> c u p i", u=2, i=2)[:, :, half * P // 2 : (half + 1) * P // 2, :],
+                spread[:].rearrange("c r (p u i) -> c u (r p) i", u=2, i=2),
+            )
 
 
         def quantise(name, woven, reuse=None):
@@ -206,8 +214,8 @@ def tile_picked_grayscott_none_p_kernel(
         w3_woven = sb("w3_woven", [P, N, PACK], BF16)
         w4_woven = sb("w4_woven", [P, N, PACK], BF16)
 
-        local_y(0, 0)
         local_e(1, 2)
+        local_y(0, 0)
         local_y(1, 1)
         local_e(2, 0)
         local_y(2, 2)
@@ -323,6 +331,8 @@ def tile_picked_grayscott_none_p_kernel(
         for t in range(1, PACK):
             react(t)
             y_west.append(gather_y_west(t))
+        g1_quarter = scaled("g1_quarter", g1_sb, 0.25, nc.vector, reuse="q1")
+        g1_eighth = scaled("g1_eighth", g1_sb, 0.125, nc.vector, reuse="q2")
         gather_e(slice(0, S), (0, 1))
         weave(w3_woven[:], w3_raw[:], nc.vector.tensor_copy)
         w3_q = quantise("w3", w3_woven[:].rearrange("p n j -> p (n j)"))

@@ -23,6 +23,7 @@ LIST_COLS = S // 16
 HALF = S // 2
 HALVES = (slice(0, HALF), slice(HALF, S))
 CHUNKS = (slice(0, HALF), slice(HALF, HALF + P), slice(HALF + P, S))
+BLOCKS = [slice(m * P, (m + 1) * P) for m in range(N // P)]
 
 
 def width_of(cells):
@@ -73,11 +74,6 @@ def tile_picked_grayscott_none_p_kernel(
             nc.sync.dma_start(out=raw[:], in_=w.rearrange("(p j) c -> p j c", j=PACK)[:, :, cols])
             return raw
 
-        def load_gain(name, g):
-            col = sb(name, [P, PACK], F32)
-            nc.sync.dma_start(out=col[:], in_=g.rearrange("(p t) o -> p (t o)", t=PACK))
-            return col
-
         w2_raw = load_weight("w2_raw", w2, slice(0, H))
         nc.sync.dma_start(offs_sb[:], offs)
         x_word_tab = sb("x_word_tab", [P, T], I32)
@@ -87,32 +83,25 @@ def tile_picked_grayscott_none_p_kernel(
         nc.sync.dma_start(west_sb[:], west)
         nc.sync.dma_start(east_sb[:], east)
         w3_raw = load_weight("w3_raw", w3, slice(0, N))
-        g1_sb = load_gain("g1_sb", g1)
+        g1_sb = sb("g1_sb", [P, PACK], F32)
+        nc.sync.dma_start(out=g1_sb[:], in_=g1.rearrange("(p t) o -> p (t o)", t=PACK))
 
         ident = sb("ident", [P, P], F32)
         make_identity(nc, ident[:])
-        minus_two = sb("minus_two", [P, 1], F32)
-        nc.gpsimd.memset(minus_two[:], -2.0)
-
-        def scaled(name, g, factor, engine, reuse=None):
-            res = sb(name, [P, PACK], F32, reuse=reuse)
-            engine.tensor_scalar(res[:], g[:], factor, 0.0, ALU.mult, ALU.add)
-            return res
 
         g2_turned = bank_tile("g2_turned", [P, P], 0)
         nc.tensor.transpose(g2_turned[:], g2_rows[:], ident[:])
-        g2_eighth = sb("g2_eighth", [P, PACK], F32)
-        nc.scalar.activation(g2_eighth[:], g2_turned[:, 0:PACK], ACT.Copy, scale=0.125)
+        g2_quarter = sb("g2_quarter", [P, PACK], F32)
+        nc.scalar.activation(g2_quarter[:], g2_turned[:, 0:PACK], ACT.Copy, scale=0.25)
         g2_row = sb("g2_row", [P, H], F32)
         for half, bank in enumerate((1, 2)):
             spread = bank_tile("spread", [P, 2, P], bank)
             for r in range(2):
-                nc.tensor.transpose(spread[:, r, :], g2_eighth[:, 2 * half + r : 2 * half + r + 1].to_broadcast([P, P]), ident[:])
+                nc.tensor.transpose(spread[:, r, :], g2_quarter[:, 2 * half + r : 2 * half + r + 1].to_broadcast([P, P]), ident[:])
             nc.scalar.copy(
                 g2_row[:].rearrange("c (u p i) -> c u p i", u=2, i=2)[:, :, half * P // 2 : (half + 1) * P // 2, :],
                 spread[:].rearrange("c r (p u i) -> c u (r p) i", u=2, i=2),
             )
-
 
         def quantise(name, woven, reuse=None):
             columns = woven.shape[1] // PACK
@@ -142,7 +131,7 @@ def tile_picked_grayscott_none_p_kernel(
 
         def first_product(t, bank, pairs, cells=slice(0, S)):
             acc = bank_tile("pre", [P, width_of(cells)], bank)
-            mx_pass(acc[:], pairs[t // 2], slice(t % 2 * P, (t % 2 + 1) * P), (x_code, x_scale), cells, True, True)
+            mx_pass(acc[:], pairs[t // 2], BLOCKS[t % 2], (x_code, x_scale), cells, True, True)
             return acc
 
         def weave(dest, src, copy):
@@ -159,50 +148,37 @@ def tile_picked_grayscott_none_p_kernel(
             nc.vector.tensor_copy(x_code[:, half], x_word_tab[:].bitcast(U32).indirect(offs_sb[:, entries(half)]))
 
         e_window = [sb("e_window%d" % t, [P, 2 * S], F32) for t in range(PACK)]
-        e_pre = [window[:, :S] for window in e_window]
-        tanh_e = [window[:, S:] for window in e_window]
-        y = [sb("y%d" % t, [P, S], F32) for t in range(PACK)]
-        q = [sb("q%d" % t, [P, S], F32) for t in range(PACK)]
+        e_like = [window[:, :S] for window in e_window]
+        q = [window[:, S:] for window in e_window]
+        y_window = [sb("y_window%d" % t, [P, 2 * S], F32) for t in range(PACK)]
+        y = [window[:, :S] for window in y_window]
+        y_fed = [window[:, S:] for window in y_window]
         y_local = [sb("y_local%d" % t, [P, S], F32) for t in range(PACK)]
-        made = {t: sb("made%d" % t, [P, S], F32) for t in range(2, PACK)}
 
         z2_sum = [bank_tile("z2_sum%d" % b, [P, PACK, P], 4 + b) for b in range(S // P)]
 
-        def add_to_z2(t, cells, term, start=False, stop=False):
+        def add_to_z2(t, term, cells=slice(0, S), start=False, stop=False):
             for n, b in enumerate(range(cells.start // P, cells.stop // P)):
-                nc.tensor.matmul(
-                    z2_sum[b][:, slot(t), :], lhsT=term[:, n * P : (n + 1) * P], rhs=ident[:], is_transpose=True, start=start, stop=stop
-                )
+                nc.tensor.matmul(z2_sum[b][:, slot(t), :], lhsT=term[:, BLOCKS[n]], rhs=ident[:], is_transpose=True, start=start, stop=stop)
 
         def local_e(t, bank):
-            acc = first_product(t, bank, w2_q)
-            nc.scalar.activation(tanh_e[t], acc[:], ACT.Tanh, scale=0.5)
-            nc.scalar.copy(e_pre[t], acc[:])
-            nc.scalar.activation(q[t][:], tanh_e[t], ACT.Square, bias=1.0)
+            nc.scalar.activation(e_like[t], first_product(t, bank, w2_q)[:], ACT.Tanh, scale=0.5)
+
+        def square(t):
+            nc.scalar.activation(q[t], e_like[t], ACT.Square, bias=1.0)
 
         def local_y(t, bank):
-            nc.scalar.activation(y[t][:], first_product(t, bank, w1_q)[:], ACT.Sigmoid)
+            nc.scalar.activation(y[t], first_product(t, bank, w1_q)[:], ACT.Sigmoid)
 
         def react(t):
-            nc.vector.scalar_tensor_tensor(y_local[t][:], q[t][:], 1.5, y[t][:], ALU.subtract, ALU.mult)
-            if t in made:
-                nc.vector.scalar_tensor_tensor(made[t][:], q[t][:], 2.0, y[t][:], ALU.mult, ALU.mult)
-                reaction = [made[t]]
-            else:
-                reaction = (3 if t else 0) * [y[t]] + 2 * [y_local[t]]
-            for term in 2 * tanh_e[t + 1 : t + 2]:
-                add_to_z2(t + 1, slice(0, S), term)
-            for term in reaction:
-                add_to_z2(t, slice(0, S), term)
-
-        def quantise_w4(h):
-            return quantise("w4_%d" % h, w4_woven[:, HALVES[h], :].rearrange("p n j -> p (n j)"))
+            nc.vector.scalar_tensor_tensor(y_local[t][:], q[t], 1.5, y[t], ALU.subtract, ALU.mult)
+            nc.vector.tensor_scalar(y_fed[t], y[t], 1.5, 0.0, ALU.mult, ALU.add)
+            add_to_z2(t, y_local[t])
+            add_to_z2(t, y_fed[t])
 
         for bank, half in enumerate(HALVES):
-            acc = first_product(0, bank, w2_q, cells=half)
-            nc.scalar.activation(tanh_e[0][:, half], acc[:], ACT.Sigmoid)
-            nc.scalar.copy(e_pre[0][:, half], acc[:])
-        nc.scalar.activation(q[0][:], tanh_e[0], ACT.Square, scale=2.0)
+            nc.scalar.activation(e_like[0][:, half], first_product(0, bank, w2_q, cells=half)[:], ACT.Sigmoid)
+        nc.scalar.activation(q[0], e_like[0], ACT.Square, scale=2.0)
 
         w1_woven = sb("w1_woven", [P, PACK, P, PACK], BF16)
         for h in range(2):
@@ -211,104 +187,108 @@ def tile_picked_grayscott_none_p_kernel(
                 w1_raw[h][:].rearrange("p j (m t) -> p m t j", t=PACK),
             )
         w1_q = [quantise("w1_%d" % u, w1_woven[:, 2 * u : 2 * u + 2].rearrange("p t m j -> p (t m j)")) for u in range(2)]
-        w3_woven = sb("w3_woven", [P, N, PACK], BF16)
-        w4_woven = sb("w4_woven", [P, N, PACK], BF16)
 
         local_e(1, 2)
-        local_y(0, 0)
-        local_y(1, 1)
+        square(1)
         local_e(2, 0)
-        local_y(2, 2)
-        local_e(3, 1)
-        local_y(3, 3)
-        for n in range(3):
-            add_to_z2(0, slice(0, S), y[0], start=n == 0)
-        add_to_z2(0, slice(0, S), minus_two[:].to_broadcast([P, S]))
-        for n in range(4):
-            add_to_z2(0, slice(0, S), tanh_e[0])
-        weave(w4_woven[:, HALVES[0], :], w4_raw[0][:], nc.vector.tensor_copy)
-        w4_q = [quantise_w4(0)]
-        weave(w4_woven[:, HALVES[1], :], w4_raw[1][:], nc.vector.tensor_copy)
-        react(0)
-        w4_q.append(quantise_w4(1))
+        local_y(0, 1)
+        square(2)
+        local_y(1, 2)
+        local_e(3, 0)
+        local_y(2, 3)
+        square(3)
+        local_y(3, 1)
 
-        def gather_e(cells, planes):
-            for t in planes:
-                e_east = sb("e_east%d_%d" % (t, cells.start), [P, width_of(cells)], F32)
-                e_west = sb("e_west%d_%d" % (t, cells.start), [P, width_of(cells)], F32)
-                nc.scalar.activation(e_east[:], e_window[t][:].indirect(east_sb[:, entries(cells)]), ACT.Sigmoid)
-                nc.scalar.activation(e_west[:], e_window[t][:].indirect(west_sb[:, entries(cells)]), ACT.Sigmoid)
-                add_to_z2(t, cells, e_east)
-                add_to_z2(t, cells, e_west, stop=t == PACK - 1)
+        w4_woven = sb("w4_woven", [P, N, PACK], BF16)
+        for h in range(2):
+            weave(w4_woven[:, HALVES[h], :], w4_raw[h][:], nc.vector.tensor_copy)
+        w4_q = [quantise("w4_%d" % h, w4_woven[:, HALVES[h], :].rearrange("p n j -> p (n j)")) for h in range(2)]
+
+        def gather_e(t, cells=slice(0, S)):
+            scale, shift = (0.5, 0.0) if t == 0 else (0.25, 1.5)
+            e_west = sb("e_west%d_%d" % (t, cells.start), [P, width_of(cells)], F32)
+            e_east = sb("e_east%d_%d" % (t, cells.start), [P, width_of(cells)], F32)
+            nc.scalar.activation(e_west[:], e_window[t][:].indirect(west_sb[:, entries(cells)]), ACT.Copy, scale=scale, bias=shift)
+            nc.scalar.activation(e_east[:], e_window[t][:].indirect(east_sb[:, entries(cells)]), ACT.Copy, scale=scale)
+            add_to_z2(t, e_west, cells)
+            add_to_z2(t, e_east, cells, stop=t == PACK - 1)
+
+        y_west = [sb("y_west%d" % t, [P, S], F32) for t in range(PACK)]
+        y_sum = [sb("y_sum%d" % t, [P, S], F32) for t in range(PACK)]
 
         def gather_y_west(t):
-            y_west = sb("y_west%d" % t, [P, S], F32)
-            for half in HALVES:
-                nc.vector.tensor_tensor(y_west[:, half], y[t][:].indirect(west_sb[:, entries(half)]), y_local[t][:, half], ALU.subtract)
-            return y_west
+            nc.vector.tensor_tensor(y_west[t][:], y_window[t][:].indirect(west_sb[:]), y_local[t][:], ALU.subtract)
 
-        def sum_tile(n, reuse=None):
-            return sb("y_sum%d" % n, [P, PACK, width_of(CHUNKS[n])], F32, reuse=reuse)
+        def gather_y_east(t):
+            nc.vector.tensor_tensor(y_sum[t][:], y_window[t][:].indirect(east_sb[:]), y_west[t][:], ALU.add)
 
-        def gather_y_east(n, y_sum, planes):
-            cells = CHUNKS[n]
-            for t in planes:
-                nc.vector.tensor_tensor(y_sum[:, t, :], y[t][:].indirect(east_sb[:, entries(cells)]), y_west[t][:, cells], ALU.add)
+        add_to_z2(0, e_like[0], start=True)
+        add_to_z2(0, e_like[0])
+        add_to_z2(1, e_like[1])
+        add_to_z2(2, e_like[2])
+        react(0)
+        add_to_z2(3, e_like[3])
+        react(1)
+        gather_y_west(0)
+        react(2)
+        gather_e(0)
+        gather_y_west(1)
+        react(3)
+        gather_y_east(0)
+        gather_y_west(2)
+        gather_y_east(1)
+        gather_y_west(3)
+        gather_y_east(2)
+        gather_y_east(3)
+        gather_e(1)
+        for half in HALVES:
+            for t in (2, 3):
+                gather_e(t, half)
 
-        def finish_z2(h):
-            z2_words = sb("z2_words%d" % h, [P, HALF, 2], F32)
-            back = bank_tile("back%d" % h, [P, 2, 2, P], 4 + 2 * h)
-            for r in range(2):
-                b = 2 * h + r
-                z2_turned = sb("z2_turned%d" % b, [P, H], BF16)
-                nc.vector.scalar_tensor_tensor(
-                    z2_turned[:].rearrange("c (w i) -> c w i", i=2),
-                    z2_sum[b][:].rearrange("c (i u) p -> c (u p) i", i=2),
-                    2.0,
-                    g2_row[:].rearrange("c (w i) -> c w i", i=2),
-                    ALU.add,
-                    ALU.mult,
-                )
-                words = z2_turned[:].bitcast(F32)
-                for u in range(2):
-                    nc.tensor.transpose(back[:, r, u, :], words[:, u * P : (u + 1) * P], ident[:])
-            nc.scalar.copy(z2_words[:].rearrange("p (r c) u -> p r c u", r=2), back[:].rearrange("p r u c -> p r c u"))
-            return z2_words[:].rearrange("p c u -> p (c u)").bitcast(BF16)
+        g1_quarter = sb("g1_quarter", [P, PACK], F32, reuse="y_west0")
+        nc.scalar.activation(g1_quarter[:], g1_sb[:], ACT.Copy, scale=0.25)
+        g1_eighth = sb("g1_eighth", [P, PACK], F32, reuse="y_west1")
+        nc.scalar.activation(g1_eighth[:], g1_sb[:], ACT.Copy, scale=0.125)
 
-        def scale_z(n, y_sum):
-            planes = sb("z_planes%d" % n, [P, PACK, width_of(CHUNKS[n])], BF16)
+        def scale_z(h, reuse=None):
+            planes = sb("z_planes%d" % h, [P, PACK, HALF], BF16, reuse=reuse)
             for t in range(PACK):
                 nc.scalar.activation(
-                    planes[:, t, :], y_sum[:, t, :], ACT.Identity, bias=g1_eighth[:, t : t + 1], scale=g1_quarter[:, t : t + 1]
+                    planes[:, t, :], y_sum[t][:, HALVES[h]], ACT.Identity, bias=g1_eighth[:, t : t + 1], scale=g1_quarter[:, t : t + 1]
                 )
             return planes
 
-        def weave_z(n, planes, reuse=None):
-            woven = sb("z_woven%d" % n, [P, width_of(CHUNKS[n]), PACK], BF16, reuse=reuse)
+        def weave_z(h, planes, reuse):
+            woven = sb("z_woven%d" % h, [P, HALF, PACK], BF16, reuse=reuse)
             weave(woven[:], planes[:], nc.vector.tensor_copy)
             return woven[:].rearrange("p c t -> p (c t)")
 
-        def scale_and_weave_z(n, y_sum):
-            width = width_of(CHUNKS[n])
-            woven = sb("z_woven%d" % n, [P, width, PACK], BF16)
-            nc.vector.scalar_tensor_tensor(
-                woven[:],
-                y_sum[:].rearrange("p t c -> p c t"),
-                0.5,
-                g1_quarter[:].unsqueeze(1).to_broadcast([P, width, PACK]),
-                ALU.add,
+
+        def finish_z2(b, back):
+            z2_turned = sb("z2_turned%d" % b, [P, H], BF16)
+            nc.vector.tensor_tensor(
+                z2_turned[:].rearrange("c (w i) -> c w i", i=2),
+                z2_sum[b][:].rearrange("c (i u) p -> c (u p) i", i=2),
+                g2_row[:].rearrange("c (w i) -> c w i", i=2),
                 ALU.mult,
             )
-            return woven[:].rearrange("p c t -> p (c t)")
+            words = z2_turned[:].bitcast(F32)
+            for u in range(2):
+                nc.tensor.transpose(back[:, u, :], words[:, u * P : (u + 1) * P], ident[:])
+
+        def copy_back(n, back):
+            blocks = back.shape[1]
+            z2_words = sb("z2_words%d" % n, [P, blocks * P, 2], F32)
+            nc.scalar.copy(z2_words[:].rearrange("p (r c) u -> p r c u", r=blocks), back[:].rearrange("p r u c -> p r c u"))
+            return z2_words[:].rearrange("p c u -> p (c u)").bitcast(BF16)
 
         out_rows = out.rearrange("(m p) c -> p m c", p=P)
 
-        def z_operands(z_q, n):
-            return lambda m: (w3_q, slice(m * P, (m + 1) * P), z_q, slice(0, width_of(CHUNKS[n])))
+        def z_side(z_q, cells):
+            return lambda m: (w3_q, BLOCKS[m], z_q, cells)
 
-        def z2_operands(z2_q, n):
-            first = CHUNKS[n].start % HALF
-            return lambda m: (w4_q[m // 2], slice(m % 2 * P, (m % 2 + 1) * P), z2_q, slice(first, first + width_of(CHUNKS[n])))
+        def z2_side(z2_q, cells):
+            return lambda m: (w4_q[m // 2], BLOCKS[m % 2], z2_q, cells)
 
         def open_groups(n, operands, banks):
             blocks = N // P // len(banks)
@@ -318,46 +298,34 @@ def tile_picked_grayscott_none_p_kernel(
             return accs
 
         def close_groups(n, operands, accs, copies, queues):
-            cells = CHUNKS[n]
             blocks = N // P // len(accs)
             for a, acc in enumerate(accs):
                 for r in range(blocks):
                     mx_pass(acc[:, r, :], *operands(a * blocks + r), False, r == blocks - 1)
-                result = sb("result%d_%d" % (n, a), [P, blocks, width_of(cells)], F32)
+                result = sb("result%d_%d" % (n, a), [P, blocks, width_of(CHUNKS[n])], F32)
                 copies[a](result[:], acc[:])
-                queues[a].dma_start(out=out_rows[:, a * blocks : (a + 1) * blocks, cells], in_=result[:])
+                queues[a].dma_start(out=out_rows[:, a * blocks : (a + 1) * blocks, CHUNKS[n]], in_=result[:])
 
-        y_west = [gather_y_west(0)]
-        for t in range(1, PACK):
-            react(t)
-            y_west.append(gather_y_west(t))
-        g1_quarter = scaled("g1_quarter", g1_sb, 0.25, nc.vector, reuse="q1")
-        g1_eighth = scaled("g1_eighth", g1_sb, 0.125, nc.vector, reuse="q2")
-        gather_e(slice(0, S), (0, 1))
+        backs = [bank_tile("back%d" % n, [P, blocks, 2, P], bank) for n, (blocks, bank) in enumerate(((2, 4), (1, 6), (1, 7)))]
+        z_planes0 = scale_z(0)
+        finish_z2(0, backs[0][:, 0])
+        finish_z2(1, backs[0][:, 1])
+        z2_woven0 = copy_back(0, backs[0])
+        z_planes1 = scale_z(1, reuse="z2_turned1")
+        w3_woven = sb("w3_woven", [P, N, PACK], BF16, reuse="z2_turned0")
         weave(w3_woven[:], w3_raw[:], nc.vector.tensor_copy)
+        z_woven0 = weave_z(0, z_planes0, "w3_raw")
+        accs0 = open_groups(0, z2_side(quantise("z2_0", z2_woven0), slice(0, HALF)), (0, 1))
         w3_q = quantise("w3", w3_woven[:].rearrange("p n j -> p (n j)"))
-        for half in HALVES:
-            gather_e(half, (2, 3))
-
-        y_sum0 = sum_tile(0)
-        gather_y_east(0, y_sum0, range(PACK))
-        z_planes0 = scale_z(0, y_sum0)
-        z2_woven0 = finish_z2(0)
-        y_sum1 = sum_tile(1, reuse="e_west3_0")
-        gather_y_east(1, y_sum1, range(PACK))
-        z_planes1 = scale_z(1, y_sum1)
-        z2_woven1 = finish_z2(1)
-        z_woven0 = weave_z(0, z_planes0, reuse="e_east3_%d" % HALF)
-        z2_q0 = quantise("z2_0", z2_woven0, reuse="e_west3_%d" % HALF)
-        accs0 = open_groups(0, z2_operands(z2_q0, 0), (0, 1))
-        z_woven1 = weave_z(1, z_planes1)
-        close_groups(0, z_operands(quantise("z_chunk0", z_woven0), 0), accs0, (nc.scalar.copy, nc.scalar.copy), (nc.sync, nc.sync))
-        accs1 = open_groups(1, z_operands(quantise("z_chunk1", z_woven1), 1), (5,))
-        y_sum2 = sum_tile(2, reuse="z2_turned3")
-        gather_y_east(2, y_sum2, (0, 1))
-        z2_q1 = quantise("z2_1", z2_woven1)
-        close_groups(1, z2_operands(z2_q1, 1), accs1, (nc.scalar.copy,), (nc.sync,))
-        accs2 = open_groups(2, z2_operands(z2_q1, 2), (2, 3, 4, 7))
-        gather_y_east(2, y_sum2, (2, 3))
-        z_q2 = quantise("z_chunk2", scale_and_weave_z(2, y_sum2))
-        close_groups(2, z_operands(z_q2, 2), accs2, 2 * (nc.scalar.copy, nc.vector.tensor_copy), 2 * (nc.scalar, nc.sync))
+        z_q0 = quantise("z_0", z_woven0)
+        finish_z2(2, backs[1][:, 0])
+        z2_woven1 = copy_back(1, backs[1])
+        finish_z2(3, backs[2][:, 0])
+        z2_woven2 = copy_back(2, backs[2])
+        close_groups(0, z_side(z_q0, slice(0, HALF)), accs0, (nc.scalar.copy, nc.scalar.copy), (nc.sync, nc.sync))
+        z_woven1 = weave_z(1, z_planes1, "g2_row")
+        accs1 = open_groups(1, z2_side(quantise("z2_1", z2_woven1), slice(0, P)), (2,))
+        z_q1 = quantise("z_1", z_woven1)
+        close_groups(1, z_side(z_q1, slice(0, P)), accs1, (nc.vector.tensor_copy,), (nc.sync,))
+        accs2 = open_groups(2, z_side(z_q1, slice(P, HALF)), (3, 4, 5, 6))
+        close_groups(2, z2_side(quantise("z2_2", z2_woven2), slice(0, P)), accs2, 2 * (nc.scalar.copy, nc.vector.tensor_copy), 2 * (nc.scalar, nc.sync))

@@ -140,12 +140,13 @@ def tile_picked_grayscott_none_p_kernel(
         w2_woven = [
             round_plane_pair("w2_woven%d" % u, w2_raw, u, copy) for u, copy in enumerate((nc.vector.tensor_copy, nc.scalar.copy))
         ]
-        w2_q = [quantise("w2_%d" % u, w2_woven[u]) for u in range(2)]
         x_scale = sb("x_scale", [P, S], U8)
         nc.vector.tensor_copy(x_scale[:], x_scale_tab[:].indirect(offs_sb[:]))
+        w2_q = [quantise("w2_0", w2_woven[0], reuse="x_scale_tab")]
         x_code = sb("x_code", [P, S], U32)
         for half in HALVES:
             nc.vector.tensor_copy(x_code[:, half], x_word_tab[:].bitcast(U32).indirect(offs_sb[:, entries(half)]))
+        w2_q.append(quantise("w2_1", w2_woven[1], reuse="x_word_tab"))
 
         e_window = [sb("e_window%d" % t, [P, 2 * S], F32) for t in range(PACK)]
         e_like = [window[:, :S] for window in e_window]
@@ -297,12 +298,12 @@ def tile_picked_grayscott_none_p_kernel(
                 mx_pass(accs[m // blocks][:, m % blocks, :], *operands(m), m % blocks == 0, False)
             return accs
 
-        def close_groups(n, operands, accs, copies, queues):
+        def close_groups(n, operands, accs, copies, queues, reuse=4 * (None,)):
             blocks = N // P // len(accs)
             for a, acc in enumerate(accs):
                 for r in range(blocks):
                     mx_pass(acc[:, r, :], *operands(a * blocks + r), False, r == blocks - 1)
-                result = sb("result%d_%d" % (n, a), [P, blocks, width_of(CHUNKS[n])], F32)
+                result = sb("result%d_%d" % (n, a), [P, blocks, width_of(CHUNKS[n])], F32, reuse=reuse[a])
                 copies[a](result[:], acc[:])
                 queues[a].dma_start(out=out_rows[:, a * blocks : (a + 1) * blocks, CHUNKS[n]], in_=result[:])
 
@@ -322,10 +323,10 @@ def tile_picked_grayscott_none_p_kernel(
         z2_woven1 = copy_back(1, backs[1])
         finish_z2(3, backs[2][:, 0])
         z2_woven2 = copy_back(2, backs[2])
-        close_groups(0, z_side(z_q0, slice(0, HALF)), accs0, (nc.scalar.copy, nc.scalar.copy), (nc.sync, nc.sync))
+        close_groups(0, z_side(z_q0, slice(0, HALF)), accs0, (nc.scalar.copy, nc.scalar.copy), (nc.sync, nc.sync), ("z2_turned2", "z2_turned3"))
         z_woven1 = weave_z(1, z_planes1, "g2_row")
         accs1 = open_groups(1, z2_side(quantise("z2_1", z2_woven1), slice(0, P)), (2,))
         z_q1 = quantise("z_1", z_woven1)
-        close_groups(1, z_side(z_q1, slice(0, P)), accs1, (nc.vector.tensor_copy,), (nc.sync,))
+        close_groups(1, z_side(z_q1, slice(0, P)), accs1, (nc.scalar.copy,), (nc.sync,))
         accs2 = open_groups(2, z_side(z_q1, slice(P, HALF)), (3, 4, 5, 6))
         close_groups(2, z2_side(quantise("z2_2", z2_woven2), slice(0, P)), accs2, 2 * (nc.scalar.copy, nc.vector.tensor_copy), 2 * (nc.scalar, nc.sync))

@@ -312,6 +312,9 @@ def tile_picked_grayscott_none_p_kernel(
         finish_z2(0, backs[0][:, 0])
         finish_z2(1, backs[0][:, 1])
         z2_woven0 = copy_back(0, backs[0])
+        warm = bank_tile("warm", [P, HALF], 4)
+        for n in range(3):
+            mx_pass(warm[:], w4_q[0], BLOCKS[0], w4_q[1], slice(0, HALF), n == 0, n == 2)
         z_planes1 = scale_z(1, reuse="z2_turned1")
         w3_woven = sb("w3_woven", [P, N, PACK], BF16, reuse="z2_turned0")
         weave(w3_woven[:], w3_raw[:], nc.vector.tensor_copy)

@@ -247,16 +247,19 @@ def tile_picked_grayscott_none_p_kernel(
                 gather_e(t, half)
 
         g1_quarter = sb("g1_quarter", [P, PACK], F32, reuse="y_west0")
-        nc.scalar.activation(g1_quarter[:], g1_sb[:], ACT.Copy, scale=0.25)
+        nc.vector.tensor_scalar(g1_quarter[:], g1_sb[:], 0.25, 0.0, ALU.mult, ALU.add)
         g1_eighth = sb("g1_eighth", [P, PACK], F32, reuse="y_west1")
-        nc.scalar.activation(g1_eighth[:], g1_sb[:], ACT.Copy, scale=0.125)
+        nc.vector.tensor_scalar(g1_eighth[:], g1_sb[:], 0.125, 0.0, ALU.mult, ALU.add)
 
         def scale_z(h, reuse=None):
             planes = sb("z_planes%d" % h, [P, PACK, HALF], BF16, reuse=reuse)
             for t in range(PACK):
-                nc.scalar.activation(
-                    planes[:, t, :], y_sum[t][:, HALVES[h]], ACT.Identity, bias=g1_eighth[:, t : t + 1], scale=g1_quarter[:, t : t + 1]
-                )
+                if h == 0 and t < 2:
+                    nc.gpsimd.tensor_scalar(planes[:, t, :], y_sum[t][:, HALVES[h]], 0.5, g1_quarter[:, t : t + 1], ALU.add, ALU.mult)
+                else:
+                    nc.scalar.activation(
+                        planes[:, t, :], y_sum[t][:, HALVES[h]], ACT.Identity, bias=g1_eighth[:, t : t + 1], scale=g1_quarter[:, t : t + 1]
+                    )
             return planes
 
         def weave_z(h, planes, reuse):
@@ -308,7 +311,7 @@ def tile_picked_grayscott_none_p_kernel(
                 queues[a].dma_start(out=out_rows[:, a * blocks : (a + 1) * blocks, CHUNKS[n]], in_=result[:])
 
         backs = [bank_tile("back%d" % n, [P, blocks, 2, P], bank) for n, (blocks, bank) in enumerate(((2, 4), (1, 6), (1, 7)))]
-        z_planes0 = scale_z(0)
+        z_planes0 = scale_z(0, reuse="y_west3")
         finish_z2(0, backs[0][:, 0])
         finish_z2(1, backs[0][:, 1])
         z2_woven0 = copy_back(0, backs[0])

@@ -82,7 +82,7 @@ def tile_picked_grayscott_none_p_kernel(
         w4_raw = [load_weight("w4_raw%d" % h, w4, cols) for h, cols in enumerate(HALVES)]
         nc.sync.dma_start(west_sb[:], west)
         nc.sync.dma_start(east_sb[:], east)
-        w3_raw = load_weight("w3_raw", w3, slice(0, N))
+        w3_raw = [load_weight("w3_raw%d" % h, w3, cols) for h, cols in enumerate(HALVES)]
         g1_sb = sb("g1_sb", [P, PACK], F32)
         nc.sync.dma_start(out=g1_sb[:], in_=g1.rearrange("(p t) o -> p (t o)", t=PACK))
 
@@ -289,7 +289,7 @@ def tile_picked_grayscott_none_p_kernel(
         out_rows = out.rearrange("(m p) c -> p m c", p=P)
 
         def z_side(z_q, cells):
-            return lambda m: (w3_q, BLOCKS[m], z_q, cells)
+            return lambda m: (w3_q[m // 2], BLOCKS[m % 2], z_q, cells)
 
         def z2_side(z2_q, cells):
             return lambda m: (w4_q[m // 2], BLOCKS[m % 2], z2_q, cells)
@@ -311,20 +311,23 @@ def tile_picked_grayscott_none_p_kernel(
                 queues[a].dma_start(out=out_rows[:, a * blocks : (a + 1) * blocks, CHUNKS[n]], in_=result[:])
 
         backs = [bank_tile("back%d" % n, [P, blocks, 2, P], bank) for n, (blocks, bank) in enumerate(((2, 4), (1, 6), (1, 7)))]
+        w3_late = sb("w3_late", [P, HALF, PACK], BF16, reuse="e_window2")
+        weave(w3_late[:], w3_raw[1][:], nc.scalar.copy)
         z_planes0 = scale_z(0, reuse="y_west3")
         finish_z2(0, backs[0][:, 0])
         finish_z2(1, backs[0][:, 1])
         z2_woven0 = copy_back(0, backs[0])
-        warm = bank_tile("warm", [P, HALF], 4)
+        warm = bank_tile("warm", [P, HALF], 5)
         for n in range(3):
             mx_pass(warm[:], w4_q[0], BLOCKS[0], w4_q[1], slice(0, HALF), n == 0, n == 2)
         z_planes1 = scale_z(1, reuse="z2_turned1")
-        w3_woven = sb("w3_woven", [P, N, PACK], BF16, reuse="z2_turned0")
-        weave(w3_woven[:], w3_raw[:], nc.vector.tensor_copy)
-        z_woven0 = weave_z(0, z_planes0, "w3_raw")
+        w3_woven = sb("w3_woven", [P, HALF, PACK], BF16, reuse="z2_turned0")
+        weave(w3_woven[:], w3_raw[0][:], nc.vector.tensor_copy)
+        z_woven0 = weave_z(0, z_planes0, "w3_raw0")
         accs0 = open_groups(0, z2_side(quantise("z2_0", z2_woven0), slice(0, HALF)), (0, 1))
-        w3_q = quantise("w3", w3_woven[:].rearrange("p n j -> p (n j)"))
+        w3_q = [quantise("w3_0", w3_woven[:].rearrange("p n j -> p (n j)"))]
         z_q0 = quantise("z_0", z_woven0)
+        w3_q.append(quantise("w3_1", w3_late[:].rearrange("p n j -> p (n j)"), reuse="y_west3"))
         finish_z2(2, backs[1][:, 0])
         z2_woven1 = copy_back(1, backs[1])
         finish_z2(3, backs[2][:, 0])

@@ -317,9 +317,6 @@ def tile_picked_grayscott_none_p_kernel(
         finish_z2(0, backs[0][:, 0])
         finish_z2(1, backs[0][:, 1])
         z2_woven0 = copy_back(0, backs[0])
-        warm = bank_tile("warm", [P, HALF], 5)
-        for n in range(3):
-            mx_pass(warm[:], w4_q[0], BLOCKS[0], w4_q[1], slice(0, HALF), n == 0, n == 2)
         z_planes1 = scale_z(1, reuse="z2_turned1")
         w3_woven = sb("w3_woven", [P, HALF, PACK], BF16, reuse="z2_turned0")
         weave(w3_woven[:], w3_raw[0][:], nc.vector.tensor_copy)

from contextlib import ExitStack

import concourse.mybir as mybir
from concourse.masks import make_identity

K, T, S, N, H = 512, 2048, 512, 512, 512
FLOPS = 2 * (2 * K * H * S + 2 * H * N * S)

F32 = mybir.dt.float32
BF16 = mybir.dt.bfloat16
I32 = mybir.dt.int32
U32 = mybir.dt.uint32
U16 = mybir.dt.uint16
U8 = mybir.dt.uint8
FP8X4 = mybir.dt.float8_e4m3fn_x4
ACT = mybir.ActivationFunctionType
ALU = mybir.AluOpType

P = 128
PACK = 4
LINE = 4
LIST_COLS = S // 16
HALF = S // 2
HALVES = (slice(0, HALF), slice(HALF, S))
CHUNKS = (slice(0, HALF), slice(HALF, HALF + P), slice(HALF + P, S))
BLOCKS = [slice(m * P, (m + 1) * P) for m in range(N // P)]


def width_of(cells):
    return cells.stop - cells.start


def entries(cells):
    return slice(cells.start // 16, cells.stop // 16)


def slot(t):
    return 2 * (t % 2) + t // 2


def tile_picked_grayscott_none_p_kernel(
    tc, x_words, x_scales, w1, w2, g1, g2, w3, w4, offs, west, east, out
):
    nc = tc.nc
    with ExitStack() as ctx:
        lists = ctx.enter_context(tc.tile_pool(name="lists", bufs=1))
        keep = ctx.enter_context(tc.tile_pool(name="keep", bufs=1))
        psum = ctx.enter_context(tc.psum_pool(name="psum", bufs=1))

        def sb(name, shape, dtype, reuse=None):
            return keep.tile(shape, dtype, name=name, tag=reuse or name, align_bytes=64)

        def bank_tile(name, shape, bank):
            return psum.tile(shape, F32, name=name, tag="bank%d" % bank)

        offs_sb = lists.tile([P, LIST_COLS], U16, name="offs_sb")
        west_sb = lists.tile([P, LIST_COLS], U16, name="west_sb")
        east_sb = lists.tile([P, LIST_COLS], U16, name="east_sb")

        g2_rows = sb("g2_rows", [P, P], F32)
        nc.gpsimd.memset(g2_rows[:], 0.0)
        nc.scalar.dma_start(out=g2_rows[0:PACK, :], in_=g2.rearrange("(r c) o -> r (c o)", r=PACK))

        x_scale_tab = sb("x_scale_tab", [P, T], U8)
        nc.gpsimd.memset(x_scale_tab[:].bitcast(I32), 0)
        for quad, queue in enumerate((nc.sync, nc.sync, nc.scalar, nc.scalar)):
            queue.dma_start(
                out=x_scale_tab[32 * quad : 32 * quad + 4, :].bitcast(I32),
                in_=x_scales[0, 4 * quad : 4 * quad + 4, :].bitcast(I32),
            )

        def load_weight(name, w, cols):
            raw = sb(name, [P, PACK, width_of(cols)], F32)
            nc.sync.dma_start(out=raw[:], in_=w.rearrange("(p j) c -> p j c", j=PACK)[:, :, cols])
            return raw

        w2_raw = load_weight("w2_raw", w2, slice(0, H))
        nc.sync.dma_start(offs_sb[:], offs)
        x_word_tab = sb("x_word_tab", [P, T], I32)
        nc.sync.dma_start(out=x_word_tab[:], in_=x_words[0].rearrange("p n t -> p (n t)").bitcast(I32))
        w1_raw = [load_weight("w1_raw%d" % h, w1, cols) for h, cols in enumerate(HALVES)]
        w4_raw = [load_weight("w4_raw%d" % h, w4, cols) for h, cols in enumerate(HALVES)]
        nc.sync.dma_start(west_sb[:], west)
        nc.sync.dma_start(east_sb[:], east)
        w3_raw = [load_weight("w3_raw%d" % h, w3, cols) for h, cols in enumerate(HALVES)]
        g1_sb = sb("g1_sb", [P, PACK], F32)
        nc.sync.dma_start(out=g1_sb[:], in_=g1.rearrange("(p t) o -> p (t o)", t=PACK))

        ident = sb("ident", [P, P], F32)
        make_identity(nc, ident[:])

        g2_turned = bank_tile("g2_turned", [P, P], 0)
        nc.tensor.transpose(g2_turned[:], g2_rows[:], ident[:])
        g2_quarter = sb("g2_quarter", [P, PACK], F32)
        nc.scalar.activation(g2_quarter[:], g2_turned[:, 0:PACK], ACT.Copy, scale=0.25)
        g2_row = sb("g2_row", [P, H], F32)
        for half, bank in enumerate((1, 2)):
            spread = bank_tile("spread", [P, 2, P], bank)
            for r in range(2):
                nc.tensor.transpose(spread[:, r, :], g2_quarter[:, 2 * half + r : 2 * half + r + 1].to_broadcast([P, P]), ident[:])
            nc.scalar.copy(
                g2_row[:].rearrange("c (u p i) -> c u p i", u=2, i=2)[:, :, half * P // 2 : (half + 1) * P // 2, :],
                spread[:].rearrange("c r (p u i) -> c u (r p) i", u=2, i=2),
            )

        def quantise(name, woven, reuse=None):
            columns = woven.shape[1] // PACK
            code = sb(name + "_code", [P, columns], U32, reuse=reuse)
            scale = sb(name + "_scale", [P, columns], U8)
            nc.vector.quantize_mx(out=code[:].bitcast(FP8X4), scales=scale[:], in_=woven)
            return code, scale

        def mx_pass(acc, weights, cols, values, cells, start, stop):
            nc.tensor.matmul_mx(
                out=acc,
                lhsT=weights[0][:, cols].bitcast(FP8X4),
                lhsT_scale=weights[1][:, cols],
                rhs=values[0][:, cells].bitcast(FP8X4),
                rhs_scale=values[1][:, cells],
                start=start,
                stop=stop,
            )

        def round_plane_pair(name, raw, u, copy):
            woven = sb(name, [P, 2, P, PACK], BF16)
            copy(
                woven[:].rearrange("p t m j -> p m t j"),
                raw[:].rearrange("p j (m t) -> p m t j", t=PACK)[:, :, 2 * u : 2 * u + 2, :],
            )
            return woven[:].rearrange("p t m j -> p (t m j)")

        def first_product(t, bank, pairs, cells=slice(0, S)):
            acc = bank_tile("pre", [P, width_of(cells)], bank)
            mx_pass(acc[:], pairs[t // 2], BLOCKS[t % 2], (x_code, x_scale), cells, True, True)
            return acc

        def weave(dest, src, copy):
            copy(dest.rearrange("p (c i) j -> p c j i", i=LINE), src.rearrange("p j (c i) -> p c j i", i=LINE))

        w2_woven = [
            round_plane_pair("w2_woven%d" % u, w2_raw, u, copy) for u, copy in enumerate((nc.vector.tensor_copy, nc.scalar.copy))
        ]
        x_scale = sb("x_scale", [P, S], U8)
        nc.vector.tensor_copy(x_scale[:], x_scale_tab[:].indirect(offs_sb[:]))
        w2_q = [quantise("w2_0", w2_woven[0], reuse="x_scale_tab")]
        x_code = sb("x_code", [P, S], U32)
        for half in HALVES:
            nc.vector.tensor_copy(x_code[:, half], x_word_tab[:].bitcast(U32).indirect(offs_sb[:, entries(half)]))
        w2_q.append(quantise("w2_1", w2_woven[1], reuse="x_word_tab"))

        e_window = [sb("e_window%d" % t, [P, 2 * S], F32) for t in range(PACK)]
        e_like = [window[:, :S] for window in e_window]
        q = [window[:, S:] for window in e_window]
        y_window = [sb("y_window%d" % t, [P, 2 * S], F32) for t in range(PACK)]
        y = [window[:, :S] for window in y_window]
        y_fed = [window[:, S:] for window in y_window]
        y_local = [sb("y_local%d" % t, [P, S], F32) for t in range(PACK)]

        z2_sum = [bank_tile("z2_sum%d" % b, [P, PACK, P], 4 + b) for b in range(S // P)]

        def add_to_z2(t, term, cells=slice(0, S), start=False, stop=False):
            for n, b in enumerate(range(cells.start // P, cells.stop // P)):
                nc.tensor.matmul(z2_sum[b][:, slot(t), :], lhsT=term[:, BLOCKS[n]], rhs=ident[:], is_transpose=True, start=start, stop=stop)

        def local_e(t, bank):
            nc.scalar.activation(e_like[t], first_product(t, bank, w2_q)[:], ACT.Tanh, scale=0.5)

        def square(t):
            nc.scalar.activation(q[t], e_like[t], ACT.Square, bias=1.0)

        def local_y(t, bank):
            nc.scalar.activation(y[t], first_product(t, bank, w1_q)[:], ACT.Sigmoid)

        def react(t):
            nc.vector.scalar_tensor_tensor(y_local[t][:], q[t], 1.5, y[t], ALU.subtract, ALU.mult)
            nc.vector.tensor_scalar(y_fed[t], y[t], 1.5, 0.0, ALU.mult, ALU.add)
            add_to_z2(t, y_local[t])
            add_to_z2(t, y_fed[t])

        for bank, half in enumerate(HALVES):
            nc.scalar.activation(e_like[0][:, half], first_product(0, bank, w2_q, cells=half)[:], ACT.Sigmoid)
        nc.scalar.activation(q[0], e_like[0], ACT.Square, scale=2.0)

        w1_woven = sb("w1_woven", [P, PACK, P, PACK], BF16)
        for h in range(2):
            nc.vector.tensor_copy(
                w1_woven[:].rearrange("p t m j -> p m t j")[:, h * P // 2 : (h + 1) * P // 2],
                w1_raw[h][:].rearrange("p j (m t) -> p m t j", t=PACK),
            )
        w1_q = [quantise("w1_%d" % u, w1_woven[:, 2 * u : 2 * u + 2].rearrange("p t m j -> p (t m j)")) for u in range(2)]

        local_e(1, 2)
        square(1)
        local_e(2, 0)
        local_y(0, 1)
        square(2)
        local_y(1, 2)
        local_e(3, 0)
        local_y(2, 3)
        square(3)
        local_y(3, 1)

        w4_woven = sb("w4_woven", [P, N, PACK], BF16)
        for h in range(2):
            weave(w4_woven[:, HALVES[h], :], w4_raw[h][:], nc.vector.tensor_copy)
        w4_q = [quantise("w4_%d" % h, w4_woven[:, HALVES[h], :].rearrange("p n j -> p (n j)")) for h in range(2)]

        def gather_e(t, cells=slice(0, S)):
            scale, shift = (0.5, 0.0) if t == 0 else (0.25, 1.5)
            e_west = sb("e_west%d_%d" % (t, cells.start), [P, width_of(cells)], F32)
            e_east = sb("e_east%d_%d" % (t, cells.start), [P, width_of(cells)], F32)
            nc.scalar.activation(e_west[:], e_window[t][:].indirect(west_sb[:, entries(cells)]), ACT.Copy, scale=scale, bias=shift)
            nc.scalar.activation(e_east[:], e_window[t][:].indirect(east_sb[:, entries(cells)]), ACT.Copy, scale=scale)
            add_to_z2(t, e_west, cells)
            add_to_z2(t, e_east, cells, stop=t == PACK - 1)

        y_west = [sb("y_west%d" % t, [P, S], F32) for t in range(PACK)]
        y_sum = [sb("y_sum%d" % t, [P, S], F32) for t in range(PACK)]

        def gather_y_west(t):
            nc.vector.tensor_tensor(y_west[t][:], y_window[t][:].indirect(west_sb[:]), y_local[t][:], ALU.subtract)

        def gather_y_east(t):
            nc.vector.tensor_tensor(y_sum[t][:], y_window[t][:].indirect(east_sb[:]), y_west[t][:], ALU.add)

        add_to_z2(0, e_like[0], start=True)
        add_to_z2(0, e_like[0])
        add_to_z2(1, e_like[1])
        add_to_z2(2, e_like[2])
        react(0)
        add_to_z2(3, e_like[3])
        react(1)
        gather_y_west(0)
        react(2)
        gather_e(0)
        gather_y_west(1)
        react(3)
        gather_y_east(0)
        gather_y_west(2)
        gather_y_east(1)
        gather_y_west(3)
        gather_y_east(2)
        gather_y_east(3)
        gather_e(1)
        for half in HALVES:
            for t in (2, 3):
                gather_e(t, half)

        g1_quarter = sb("g1_quarter", [P, PACK], F32, reuse="y_west0")
        nc.vector.tensor_scalar(g1_quarter[:], g1_sb[:], 0.25, 0.0, ALU.mult, ALU.add)
        g1_eighth = sb("g1_eighth", [P, PACK], F32, reuse="y_west1")
        nc.vector.tensor_scalar(g1_eighth[:], g1_sb[:], 0.125, 0.0, ALU.mult, ALU.add)

        def scale_z(h, reuse=None):
            planes = sb("z_planes%d" % h, [P, PACK, HALF], BF16, reuse=reuse)
            for t in range(PACK):
                if h == 0 and t < 2:
                    nc.gpsimd.tensor_scalar(planes[:, t, :], y_sum[t][:, HALVES[h]], 0.5, g1_quarter[:, t : t + 1], ALU.add, ALU.mult)
                else:
                    nc.scalar.activation(
                        planes[:, t, :], y_sum[t][:, HALVES[h]], ACT.Identity, bias=g1_eighth[:, t : t + 1], scale=g1_quarter[:, t : t + 1]
                    )
            return planes

        def weave_z(h, planes, reuse):
            woven = sb("z_woven%d" % h, [P, HALF, PACK], BF16, reuse=reuse)
            weave(woven[:], planes[:], nc.vector.tensor_copy)
            return woven[:].rearrange("p c t -> p (c t)")


        def finish_z2(b, back):
            z2_turned = sb("z2_turned%d" % b, [P, H], BF16)
            nc.vector.tensor_tensor(
                z2_turned[:].rearrange("c (w i) -> c w i", i=2),
                z2_sum[b][:].rearrange("c (i u) p -> c (u p) i", i=2),
                g2_row[:].rearrange("c (w i) -> c w i", i=2),
                ALU.mult,
            )
            words = z2_turned[:].bitcast(F32)
            for u in range(2):
                nc.tensor.transpose(back[:, u, :], words[:, u * P : (u + 1) * P], ident[:])

        def copy_back(n, back):
            blocks = back.shape[1]
            z2_words = sb("z2_words%d" % n, [P, blocks * P, 2], F32)
            nc.scalar.copy(z2_words[:].rearrange("p (r c) u -> p r c u", r=blocks), back[:].rearrange("p r u c -> p r c u"))
            return z2_words[:].rearrange("p c u -> p (c u)").bitcast(BF16)

        out_rows = out.rearrange("(m p) c -> p m c", p=P)

        def z_side(z_q, cells):
            return lambda m: (w3_q[m // 2], BLOCKS[m % 2], z_q, cells)

        def z2_side(z2_q, cells):
            return lambda m: (w4_q[m // 2], BLOCKS[m % 2], z2_q, cells)

        def open_groups(n, operands, banks):
            blocks = N // P // len(banks)
            accs = [bank_tile("acc%d_%d" % (n, a), [P, blocks, width_of(CHUNKS[n])], bank) for a, bank in enumerate(banks)]
            for m in range(N // P):
                mx_pass(accs[m // blocks][:, m % blocks, :], *operands(m), m % blocks == 0, False)
            return accs

        def close_groups(n, operands, accs, copies, queues, reuse=4 * (None,)):
            blocks = N // P // len(accs)
            for a, acc in enumerate(accs):
                for r in range(blocks):
                    mx_pass(acc[:, r, :], *operands(a * blocks + r), False, r == blocks - 1)
                result = sb("result%d_%d" % (n, a), [P, blocks, width_of(CHUNKS[n])], F32, reuse=reuse[a])
                copies[a](result[:], acc[:])
                queues[a].dma_start(out=out_rows[:, a * blocks : (a + 1) * blocks, CHUNKS[n]], in_=result[:])

        backs = [bank_tile("back%d" % n, [P, blocks, 2, P], bank) for n, (blocks, bank) in enumerate(((2, 4), (1, 6), (1, 7)))]
        w3_late = sb("w3_late", [P, HALF, PACK], BF16, reuse="e_window2")
        weave(w3_late[:], w3_raw[1][:], nc.scalar.copy)
        z_planes0 = scale_z(0, reuse="y_west3")
        finish_z2(0, backs[0][:, 0])
        finish_z2(1, backs[0][:, 1])
        z2_woven0 = copy_back(0, backs[0])
        z_planes1 = scale_z(1, reuse="z2_turned1")
        w3_woven = sb("w3_woven", [P, HALF, PACK], BF16, reuse="z2_turned0")
        weave(w3_woven[:], w3_raw[0][:], nc.vector.tensor_copy)
        z_woven0 = weave_z(0, z_planes0, "w3_raw0")
        accs0 = open_groups(0, z2_side(quantise("z2_0", z2_woven0), slice(0, HALF)), (0, 1))
        w3_q = [quantise("w3_0", w3_woven[:].rearrange("p n j -> p (n j)"))]
        z_q0 = quantise("z_0", z_woven0)
        w3_q.append(quantise("w3_1", w3_late[:].rearrange("p n j -> p (n j)"), reuse="y_west3"))
        finish_z2(2, backs[1][:, 0])
        z2_woven1 = copy_back(1, backs[1])
        finish_z2(3, backs[2][:, 0])
        z2_woven2 = copy_back(2, backs[2])
        close_groups(0, z_side(z_q0, slice(0, HALF)), accs0, (nc.scalar.copy, nc.scalar.copy), (nc.sync, nc.sync), ("z2_turned2", "z2_turned3"))
        z_woven1 = weave_z(1, z_planes1, "g2_row")
        accs1 = open_groups(1, z2_side(quantise("z2_1", z2_woven1), slice(0, P)), (2,))
        z_q1 = quantise("z_1", z_woven1)
        close_groups(1, z_side(z_q1, slice(0, P)), accs1, (nc.scalar.copy,), (nc.sync,))
        accs2 = open_groups(2, z_side(z_q1, slice(P, HALF)), (3, 4, 5, 6))
        close_groups(2, z2_side(quantise("z2_2", z2_woven2), slice(0, P)), accs2, 2 * (nc.scalar.copy, nc.vector.tensor_copy), 2 * (nc.scalar, nc.sync))
